import numpy as np
import ml_dtypes


def mxq(x, axis, fmt="e4m3"):
    dtype, down = {"e4m3": (ml_dtypes.float8_e4m3fn, 7), "e5m2": (ml_dtypes.float8_e5m2, 14)}[fmt]
    v = np.moveaxis(np.asarray(x, np.float32).astype(ml_dtypes.bfloat16).astype(np.float64), axis, -1)
    blocks = v.reshape(v.shape[:-1] + (-1, 32))
    amax = np.abs(blocks).max(-1, keepdims=True)
    byte = np.maximum(np.where(amax > 0, np.frexp(amax)[1] - 1 + 127, 0) - down, 1)
    scale = np.exp2(byte - 127.0)
    codes = (blocks / scale).astype(np.float32).astype(dtype).astype(np.float64)
    return np.moveaxis((codes * scale).reshape(v.shape), -1, axis)


WIDE = False


def mx_kscale(k):
    if not WIDE:
        return np.ones(k)
    levels = np.array([10, -10, 5, -5, 0])
    if k % 512:
        return np.exp2(np.random.permutation(np.resize(levels, k // 32))).repeat(32)
    a = np.empty((k // 512, 16))
    for p in range(k // 512):
        a[p, :8] = np.random.permutation(np.resize(levels, 8))
        for g in range(8):
            far = levels[np.abs(levels - a[p, g]) >= 10]
            a[p, g + 8] = far[np.random.randint(len(far))]
    return np.exp2(a.ravel()).repeat(32)


def f64(x):
    return np.asarray(x).astype(np.float64)


def striped(idx):
    return np.tile(idx.reshape(-1, 16).T, (8, 1)).astype(np.uint16)


def unstriped(offs):
    return offs[:16].T.reshape(-1).astype(np.int64)


E2M1 = np.array([0.0, 0.5, 1.0, 1.5, 2.0, 3.0, 4.0, 6.0, -0.0, -0.5, -1.0, -1.5, -2.0, -3.0, -4.0, -6.0])


def pack_weight(w, fmt):
    k, n = w.shape
    w = f64(np.asarray(w, np.float32).astype(ml_dtypes.bfloat16)).reshape(k // 32, 32, n)
    amax = np.abs(w).max(1)
    if fmt == "e4m3":
        byte = np.frexp(amax)[1] - 1 + 127 - 7
    else:
        mant, ex = np.frexp(amax / 6.0)
        byte = np.where(mant > 0.5, ex, ex - 1) + 127
    byte = np.clip(np.where(amax > 0, byte, 1), 1, 254)
    scaled = (w * np.exp2(127.0 - byte)[:, None, :]).reshape(k, n).astype(np.float32)
    by_word = np.ascontiguousarray(scaled.reshape(k // 512, 128, 4, n).transpose(0, 1, 3, 2))
    if fmt == "e4m3":
        words = by_word.astype(ml_dtypes.float8_e4m3fn).view(np.uint8)
    else:
        c = by_word.astype(ml_dtypes.float4_e2m1fn).view(np.uint8) & 0xF
        words = (c[..., 0::2] | (c[..., 1::2] << 4)).reshape(k // 512, 128, 2 * n)
    return np.ascontiguousarray(words), np.ascontiguousarray(byte.astype(np.uint8).reshape(k // 512, 16, n))


def unpack_weight(words, scales, fmt):
    g, _, n = scales.shape
    words = np.ascontiguousarray(words).reshape(g, 128, n, -1)
    if fmt == "e4m3":
        vals = words.view(ml_dtypes.float8_e4m3fn).astype(np.float64)
    else:
        nib = np.empty((g, 128, n, 4), np.uint8)
        nib[..., 0::2] = words & 0xF
        nib[..., 1::2] = words >> 4
        vals = E2M1[nib]
    vals = vals * np.repeat(np.exp2(scales.astype(np.float64) - 127.0), 8, axis=1)[..., None]
    return vals.transpose(0, 1, 3, 2).reshape(g * 512, n)


def gelu(v):
    return 0.5 * v * (1.0 + np.tanh(np.sqrt(2.0 / np.pi) * (v + 0.044715 * v**3)))


K, H, T, S, T2, S2 = 1024, 1024, 4096, 1024, 1024, 512

def setup_inputs():
    n = np.random.standard_normal
    s = mx_kscale(K)[:, None]
    u = mx_kscale(H)[:, None]
    tab_words, tab_scales = pack_weight(n((K, T)) * s, "e4m3")
    tab2_words, tab2_scales = pack_weight(n((H, T2)) / (u * np.sqrt(H)), "e4m3")
    w4_words, w4_scales = pack_weight(n((K, H)) / (s * np.sqrt(K)), "e2m1")
    w1 = (n((K, H)) * u.T / (s * np.sqrt(K))).astype(np.float32)
    discount = np.random.uniform(0.5, 1.0, S).astype(np.float32)
    reward = (0.5 * n(S)).astype(np.float32)
    offs = striped(np.random.permutation(T)[:S])
    offs2 = striped(np.random.permutation(T2)[:S2])
    return {"tab_words": tab_words, "tab_scales": tab_scales, "offs": offs,
            "tab2_words": tab2_words, "tab2_scales": tab2_scales, "offs2": offs2,
            "w1": w1, "w4_words": w4_words, "w4_scales": w4_scales,
            "discount": discount, "reward": reward}

def reference(tab_words, tab_scales, offs, tab2_words, tab2_scales, offs2,
              w1, w4_words, w4_scales, discount, reward):
    v = unpack_weight(tab_words, tab_scales, "e4m3")[:, unstriped(offs)]
    v2 = unpack_weight(tab2_words, tab2_scales, "e4m3")[:, unstriped(offs2)]
    w4 = unpack_weight(w4_words, w4_scales, "e2m1")
    a = mxq(f64(w1), 0, "e4m3").T @ v
    b = w4.T @ v
    h = a * np.maximum(b, np.exp(np.minimum(b, 0.0)) - 1.0)
    q = v2.T @ mxq(h, 0, "e4m3")
    return f64(reward)[None, :] + f64(discount)[None, :] * q

@@ -1,0 +1,435 @@
+from contextlib import ExitStack
+
+import concourse.mybir as mybir
+from concourse.masks import make_identity
+
+K, H, T, S, T2, S2 = 1024, 1024, 4096, 1024, 1024, 512
+FLOPS = 2 * K * H * S * 2 + 2 * H * S2 * S
+
+F32 = mybir.dt.float32
+BF16 = mybir.dt.bfloat16
+I32 = mybir.dt.int32
+U32 = mybir.dt.uint32
+U16 = mybir.dt.uint16
+U8 = mybir.dt.uint8
+FP8X4 = mybir.dt.float8_e4m3fn_x4
+FP4X4 = mybir.dt.float4_e2m1fn_x4
+ALU = mybir.AluOpType
+ACT = mybir.ActivationFunctionType
+
+P = 128
+PACK = 4
+BANK = 512
+PASSES = 2
+CAST = [["VV","VS"],["SS","SS"]]
+P1V = [[0,0,1],[0,0,3]]
+
+
+def tile_list_replay_action_targets_kernel(
+    tc, tab_words, tab_scales, offs, tab2_words, tab2_scales, offs2, w1, w4_words, w4_scales, discount, reward, out
+):
+    nc = tc.nc
+    with ExitStack() as ctx:
+        keep = ctx.enter_context(tc.tile_pool(name="keep", bufs=1))
+        work = ctx.enter_context(tc.tile_pool(name="work", bufs=4))
+        psum = ctx.enter_context(tc.psum_pool(name="psum", bufs=1))
+
+        def held(shape, dtype, name, tag=None):
+            return keep.tile(shape, dtype, name=name, tag=tag or name, align_bytes=64)
+
+        idx = keep.tile([P, S // 16], U16, name="idx")
+        idx2 = keep.tile([P, S2 // 16], U16, name="idx2")
+        tab_s = held([P, T // 4], I32, "tab_s", "stage")
+        w4_raw = held([P, PASSES, H // 2], I32, "w4_raw")
+        w4_raw_s = held([P, PASSES, H // 4], I32, "w4_raw_s")
+        def queued(shape, dtype, name):
+            return keep.tile(shape, dtype, name=name, tag="queued", bufs=3, align_bytes=64)
+
+        v_s1 = queued([P, S // 4], I32, "v_s1")
+        tab_w = [queued([P, T], I32, f"tab_w{a}") for a in range(PASSES)]
+        coef = held([P, 16], F32, "coef")
+        ident = held([P, P], F32, "ident")
+        warm = held([P, 1], F32, "warm")
+
+        nc.vector.memset(tab_s[:], 0)
+        nc.vector.memset(w4_raw_s[:], 0)
+        nc.vector.memset(v_s1[:], 0)
+        make_identity(nc, ident[:])
+
+        def load_words(dst, src):
+            nc.sync.dma_start(out=dst, in_=src.rearrange("p t i -> p (t i)").bitcast(I32))
+
+        def load_packed_scales(queue, dst, src):
+            for Q in range(4):
+                queue.dma_start(out=dst[32 * Q : 32 * Q + 8, :], in_=src.bitcast(I32)[:, 4 * Q : 4 * Q + 4, :])
+
+        nc.sync.dma_start(idx[:], offs)
+        nc.sync.dma_start(idx2[:], offs2)
+        nc.sync.dma_start(out=w4_raw[:], in_=w4_words.bitcast(I32).rearrange("a p c -> p a c"))
+        load_packed_scales(nc.sync, tab_s, tab_scales)
+        load_words(tab_w[0][:], tab_words[0])
+        for Q in range(4):
+            nc.sync.dma_start(
+                out=w4_raw_s[32 * Q : 32 * Q + 4, :, :],
+                in_=w4_scales.bitcast(I32)[:, 4 * Q : 4 * Q + 4, :].rearrange("a r c -> r a c"),
+            )
+        load_words(tab_w[1][:], tab_words[1])
+        nc.scalar.activation(warm[:], ident[:, 0:1], ACT.Exp)
+
+        late = {}
+
+        def coefs():
+            rows16 = late["rows16"] = queued([P, P], F32, "rows16")
+            nc.gpsimd.memset(rows16[:], 0.0)
+            nc.sync.dma_start(out=rows16[0:8, :], in_=discount.rearrange("(c p) -> c p", p=P))
+            nc.sync.dma_start(out=rows16[8:16, :], in_=reward.rearrange("(c p) -> c p", p=P))
+
+        def turn():
+            rows16 = late["rows16"]
+            turned = psum.tile([P, P], F32, name="turned", tag="X", bufs=4)
+            nc.tensor.transpose(turned[:], rows16[:], ident[:])
+            nc.scalar.copy(coef[:], turned[:, 0:16])
+
+        def load_tab2_scales():
+            late["tab2_s"] = held([P, T2 // 4], I32, "tab2_s", "w4_raw_s")
+            nc.vector.memset(late["tab2_s"][:], 0)
+            load_packed_scales(nc.sync, late["tab2_s"], tab2_scales)
+
+        v_s0 = held([P, S], U8, "v_s0")
+        nc.vector.tensor_copy(v_s0[:], tab_s[:].bitcast(U8).indirect(idx[:]))
+        for Q in range(4):
+            nc.sync.dma_start(out=v_s1[32 * Q : 32 * Q + 4, :], in_=v_s0[:].bitcast(I32)[32 * Q + 4 : 32 * Q + 8, :])
+        v_s = [v_s0[:], v_s1[:].bitcast(U8)]
+        v_w = [held([P, S], U32, f"v_w{a}") for a in range(PASSES)]
+
+        def gather_v(a, J):
+            nc.vector.tensor_copy(
+                v_w[a][:, J * BANK : (J + 1) * BANK], tab_w[a][:].bitcast(U32).indirect(idx[:, 32 * J : 32 * J + 32])
+            )
+
+        w4_w = [held([P, PASSES, 2 * BANK], U8, f"w4_w{A}") for A in range(PASSES)]
+        w4_s = [held([P, PASSES, BANK], U8, f"w4_s{A}") for A in range(PASSES)]
+
+        def perm_w(A):
+            src = w4_raw[:].bitcast(U16)[:, :, A * BANK : (A + 1) * BANK]
+            nc.vector.tensor_copy(
+                w4_w[A][:].bitcast(U16).rearrange("p a (t m) -> p a t m", t=PACK),
+                src.rearrange("p a (m t) -> p a t m", t=PACK),
+            )
+
+        def perm_s(A):
+            src = w4_raw_s[:].bitcast(U8)[:, :, A * BANK : (A + 1) * BANK]
+            nc.vector.tensor_copy(
+                w4_s[A][:].rearrange("p a (t m) -> p a t m", t=PACK),
+                src.rearrange("p a (m t) -> p a t m", t=PACK),
+            )
+
+        def late_loads():
+            late["w1"] = held([P, PASSES, PASSES, PACK, BANK], F32, "w1_raw", "stage")
+            for A in range(PASSES):
+                for a in range(PASSES):
+                    rows = w1[a * BANK : (a + 1) * BANK, A * BANK : (A + 1) * BANK]
+                    nc.sync.dma_start(out=late["w1"][:, A, a], in_=rows.rearrange("(p i) c -> p i c", i=PACK))
+            late["tab2"] = queued([P, PASSES, T2], I32, "tab2_w")
+            nc.sync.dma_start(out=late["tab2"][:], in_=tab2_words.rearrange("a p t i -> p a (t i)").bitcast(I32))
+
+        w1_w = [[held([P, BANK], U32, f"w1_w{A}{a}") for a in range(PASSES)] for A in range(PASSES)]
+        w1_s = [[held([P, BANK], U8, f"w1_s{A}{a}") for a in range(PASSES)] for A in range(PASSES)]
+
+        live = {}
+
+        def cast(A, a, n):
+            if ("g", A, a) not in live:
+                live["g", A, a] = work.tile([P, PACK * BANK], BF16, name="grouped", tag="w1g", bufs=4, align_bytes=64)
+            src = late["w1"][:, A, a].rearrange("p i (m u e) -> p u m i e", u=2, e=2)
+            dst = live["g", A, a][:].rearrange("p (u e m i) -> p u m i e", u=2, e=2, i=PACK)
+            per = len(CAST[A][a]) // 2
+            u, m0 = n // per, (n % per) * (P // per)
+            piece_in, piece_out = src[:, u, m0 : m0 + P // per], dst[:, u, m0 : m0 + P // per]
+            eng = CAST[A][a][n]
+            if eng == "V":
+                nc.vector.tensor_copy(piece_out, piece_in)
+            elif eng == "S":
+                nc.scalar.copy(piece_out, piece_in)
+            else:
+                nc.gpsimd.tensor_scalar(piece_out, piece_in, 1.0, 0.0, ALU.mult, ALU.add)
+
+        def qw(A, a):
+            nc.vector.quantize_mx(out=w1_w[A][a][:].bitcast(FP8X4), scales=w1_s[A][a][:], in_=live["g", A, a][:])
+
+        elu = [[held([P, PACK, BANK], F32, f"elu{A}{J}") for J in range(2)] for A in range(PASSES)]
+
+        def mmb(A, J, t):
+            cols = slice(J * BANK, (J + 1) * BANK)
+            b = live["b", A, J, t] = psum.tile([P, BANK], F32, name="b", tag="X", bufs=4)
+            for a in range(PASSES):
+                nc.tensor.matmul_mx(
+                    out=b[:],
+                    lhsT=w4_w[A][:, a, 2 * P * t : 2 * P * (t + 1)].bitcast(FP4X4),
+                    lhsT_scale=w4_s[A][:, a, P * t : P * (t + 1)],
+                    rhs=v_w[a][:, cols].bitcast(FP8X4),
+                    rhs_scale=v_s[a][:, cols],
+                    start=(a == 0),
+                    stop=(a == PASSES - 1),
+                )
+
+        def p1(A, J, t):
+            neg = live["n", A, J, t] = work.tile([P, BANK], F32, name="neg")
+            if [A, J, t] in P1V:
+                nc.vector.tensor_scalar(neg[:], live["b", A, J, t][:], 0.0, None, ALU.min)
+            else:
+                nc.scalar.activation(neg[:], live["b", A, J, t][:], ACT.Relu, scale=-1.0)
+
+        def p2(A, J, t):
+            ex = live["x", A, J, t] = work.tile([P, BANK], F32, name="ex")
+            nc.scalar.activation(ex[:], live["n", A, J, t][:], ACT.Exp, scale=1.0 if [A, J, t] in P1V else -1.0)
+
+        def p3(A, J, t):
+            nc.vector.scalar_tensor_tensor(
+                elu[A][J][:, t, :], live["x", A, J, t][:], -1.0, live["b", A, J, t][:], ALU.add, ALU.max
+            )
+
+        h_w = [held([P, S], U32, f"h_w{A}") for A in range(PASSES)]
+        h_s = [held([P, S], U8, f"h_s{A}") for A in range(PASSES)]
+
+        def mma(A, c):
+            cols = slice(c * P, (c + 1) * P)
+            acc = live["a", A, c] = psum.tile([P, PACK, P], F32, name="acc", tag="Y", bufs=4)
+            for t in range(PACK):
+                for a in (1, 0):
+                    nc.tensor.matmul_mx(
+                        out=acc[:, t, :],
+                        lhsT=w1_w[A][a][:, P * t : P * (t + 1)].bitcast(FP8X4),
+                        lhsT_scale=w1_s[A][a][:, P * t : P * (t + 1)],
+                        rhs=v_w[a][:, cols].bitcast(FP8X4),
+                        rhs_scale=v_s[a][:, cols],
+                        start=(a == 1),
+                        stop=(a == 0),
+                    )
+
+        def p4(A, c, c0, n, how):
+            if ("h", A, c0) not in live:
+                live["h", A, c0] = work.tile([P, n * BANK], BF16, name="h", align_bytes=64)
+            dst = live["h", A, c0][:, (c - c0) * BANK : (c - c0 + 1) * BANK].rearrange("p (c e t) -> p c t e", e=2, t=PACK)
+            acc = live["a", A, c][:].rearrange("p t (c e) -> p c t e", e=2)
+            gate = elu[A][c // 4][:, :, (c % 4) * P : (c % 4 + 1) * P].rearrange("p t (c e) -> p c t e", e=2)
+            if how == "V":
+                nc.vector.tensor_tensor(dst, acc, gate, ALU.mult)
+            else:
+                plain = work.tile([P, PACK, P], F32, name="plain")
+                nc.scalar.copy(plain[:], live["a", A, c][:])
+                nc.gpsimd.tensor_tensor(dst, plain[:].rearrange("p t (c e) -> p c t e", e=2), gate, ALU.mult)
+
+        def qh(A, c0, n):
+            cols = slice(c0 * P, (c0 + n) * P)
+            nc.vector.quantize_mx(out=h_w[A][:, cols].bitcast(FP8X4), scales=h_s[A][:, cols], in_=live["h", A, c0][:])
+
+        v2_s = held([P, S2], U8, "v2_s")
+        v2_w = [held([P, S2], U32, f"v2_w{A}") for A in range(PASSES)]
+
+        def gather_v2_scales():
+            nc.vector.tensor_copy(v2_s[:], late["tab2_s"][:].bitcast(U8).indirect(idx2[:]))
+
+        def gather_v2(A):
+            nc.vector.tensor_copy(v2_w[A][:], late["tab2"][:, A, :].bitcast(U32).indirect(idx2[:]))
+
+        def mmq(c):
+            cols = slice(c * P, (c + 1) * P)
+            q = live["q", c] = psum.tile([P, S2], F32, name="q", tag="Y", bufs=4)
+            for A in (1, 0):
+                nc.tensor.matmul_mx(
+                    out=q[:],
+                    lhsT=h_w[A][:, cols].bitcast(FP8X4),
+                    lhsT_scale=h_s[A][:, cols],
+                    rhs=v2_w[A][:].bitcast(FP8X4),
+                    rhs_scale=v2_s[4 * A : P, :],
+                    start=(A == 1),
+                    stop=(A == 0),
+                )
+
+        def act(c):
+            scaled = live["s", c] = work.tile([P, S2], F32, name="scaled")
+            nc.scalar.activation(
+                scaled[:], live["q", c][:], ACT.Identity, scale=coef[:, c : c + 1], bias=coef[:, 8 + c : 9 + c]
+            )
+
+        def tr(c):
+            back = live["k", c] = psum.tile([P, PACK, P], F32, name="back", tag="X", bufs=4)
+            for i in range(S2 // P):
+                nc.tensor.transpose(back[:, i, :], live["s", c][:, i * P : (i + 1) * P], ident[:])
+
+        def emit(c, how):
+            res = work.tile([P, PACK, P], F32, name="res")
+            if how == "S":
+                nc.scalar.copy(res[:], live["k", c][:])
+            else:
+                nc.vector.tensor_copy(res[:], live["k", c][:])
+            nc.sync.dma_start(out=out[:, c * P : (c + 1) * P].rearrange("(i p) j -> p i j", p=P), in_=res[:])
+
+        perm_w(1)
+        perm_w(0)
+        gather_v(0, 1)
+        perm_s(1)
+        perm_s(0)
+        gather_v(0, 0)
+        late_loads()
+        gather_v(1, 0)
+        mmb(0, 0, 2)
+        mmb(0, 0, 3)
+        mmb(0, 0, 0)
+        mmb(0, 0, 1)
+        gather_v(1, 1)
+        p1(0, 0, 2)
+        p1(0, 0, 0)
+        p1(0, 0, 3)
+        coefs()
+        p2(0, 0, 2)
+        p1(0, 0, 1)
+        p2(0, 0, 3)
+        cast(0, 0, 0)
+        p2(0, 0, 0)
+        p3(0, 0, 2)
+        p2(0, 0, 1)
+        p3(0, 0, 3)
+        mmb(1, 0, 0)
+        cast(0, 1, 1)
+        p3(0, 0, 0)
+        mmb(1, 0, 1)
+        p3(0, 0, 1)
+        cast(0, 0, 1)
+        p1(1, 0, 0)
+        p1(1, 0, 1)
+        cast(0, 1, 0)
+        p2(1, 0, 0)
+        qw(0, 0)
+        p2(1, 0, 1)
+        qw(0, 1)
+        cast(1, 0, 0)
+        p3(1, 0, 0)
+        mma(0, 2)
+        p3(1, 0, 1)
+        mma(0, 3)
+        cast(1, 0, 1)
+        p4(0, 2, 2, 2, 'V')
+        mma(0, 0)
+        p4(0, 3, 2, 2, 'V')
+        mma(0, 1)
+        p4(0, 0, 0, 2, 'V')
+        cast(1, 1, 0)
+        turn()
+        qw(1, 0)
+        mmb(0, 1, 2)
+        qh(0, 2, 2)
+        mmb(0, 1, 3)
+        cast(1, 1, 1)
+        p4(0, 1, 0, 2, 'V')
+        mmb(0, 1, 0)
+        load_tab2_scales()
+        qh(0, 0, 2)
+        mma(0, 6)
+        gather_v2(1)
+        p1(0, 1, 2)
+        mmb(0, 1, 1)
+        p1(0, 1, 3)
+        qw(1, 1)
+        p2(0, 1, 2)
+        gather_v2(0)
+        mma(1, 0)
+        p2(0, 1, 3)
+        mma(1, 1)
+        p1(0, 1, 0)
+        p3(0, 1, 2)
+        p1(0, 1, 1)
+        mma(0, 7)
+        p3(0, 1, 3)
+        p2(0, 1, 0)
+        mmb(1, 0, 2)
+        gather_v2_scales()
+        p2(0, 1, 1)
+        mmb(1, 0, 3)
+        p1(1, 0, 2)
+        p3(0, 1, 0)
+        p1(1, 0, 3)
+        p3(0, 1, 1)
+        mmb(1, 1, 2)
+        p2(1, 0, 2)
+        mmb(1, 1, 3)
+        p2(1, 0, 3)
+        p4(0, 6, 6, 1, 'V')
+        p1(1, 1, 2)
+        p3(1, 0, 2)
+        mma(1, 2)
+        p1(1, 1, 3)
+        p3(1, 0, 3)
+        mmb(1, 1, 0)
+        p2(1, 1, 2)
+        qh(0, 6, 1)
+        p4(1, 0, 0, 2, 'V')
+        mmb(1, 1, 1)
+        p2(1, 1, 3)
+        p4(1, 1, 0, 2, 'V')
+        mma(1, 3)
+        p1(1, 1, 0)
+        p4(0, 7, 7, 1, 'V')
+        mma(1, 6)
+        p1(1, 1, 1)
+        qh(1, 0, 2)
+        qh(0, 7, 1)
+        p2(1, 1, 0)
+        mmq(0)
+        p4(1, 2, 2, 2, 'V')
+        p2(1, 1, 1)
+        p4(1, 3, 2, 2, 'V')
+        mmq(1)
+        act(0)
+        p3(1, 1, 2)
+        mma(1, 7)
+        act(1)
+        qh(1, 2, 2)
+        tr(0)
+        p3(1, 1, 3)
+        mmq(2)
+        p3(1, 1, 0)
+        emit(0, 'S')
+        tr(1)
+        p3(1, 1, 1)
+        act(2)
+        mmq(3)
+        emit(1, 'S')
+        p4(1, 6, 6, 1, 'V')
+        tr(2)
+        act(3)
+        p4(1, 7, 7, 1, 'V')
+        mma(1, 5)
+        qh(1, 6, 1)
+        qh(1, 7, 1)
+        emit(2, 'V')
+        tr(3)
+        mmq(7)
+        emit(3, 'V')
+        mma(1, 4)
+        act(7)
+        p4(1, 5, 5, 1, 'V')
+        mma(0, 4)
+        p4(1, 4, 4, 1, 'V')
+        tr(7)
+        qh(1, 5, 1)
+        qh(1, 4, 1)
+        emit(7, 'S')
+        mma(0, 5)
+        p4(0, 4, 4, 1, 'V')
+        mmq(6)
+        p4(0, 5, 5, 1, 'V')
+        act(6)
+        qh(0, 4, 1)
+        mmq(4)
+        qh(0, 5, 1)
+        mmq(5)
+        tr(6)
+        act(4)
+        emit(6, 'V')
+        tr(4)
+        act(5)
+        emit(4, 'S')
+        tr(5)
+        emit(5, 'S')

@@ -21,8 +21,8 @@ P = 128
 PACK = 4
 BANK = 512
 PASSES = 2
-CAST = [["VV","VS"],["SS","SS"]]
-P1V = [[0,0,1],[0,0,3]]
+CAST = [["SS","VGGG"],["SS","GGGG"]]
+P1V = [[0,0,1],[1,0,3]]
 
 
 def tile_list_replay_action_targets_kernel(
@@ -79,21 +79,21 @@ def tile_list_replay_action_targets_kernel(
         late = {}
 
         def coefs():
-            rows16 = late["rows16"] = queued([P, P], F32, "rows16")
+            rows16 = late["rows16"] = held([P, P], F32, "rows16", "w4_raw_s")
             nc.gpsimd.memset(rows16[:], 0.0)
             nc.sync.dma_start(out=rows16[0:8, :], in_=discount.rearrange("(c p) -> c p", p=P))
             nc.sync.dma_start(out=rows16[8:16, :], in_=reward.rearrange("(c p) -> c p", p=P))
 
         def turn():
             rows16 = late["rows16"]
-            turned = psum.tile([P, P], F32, name="turned", tag="X", bufs=4)
+            turned = psum.tile([P, P], F32, name="turned", tag="Z", bufs=1)
             nc.tensor.transpose(turned[:], rows16[:], ident[:])
             nc.scalar.copy(coef[:], turned[:, 0:16])
 
-        def load_tab2_scales():
-            late["tab2_s"] = held([P, T2 // 4], I32, "tab2_s", "w4_raw_s")
-            nc.vector.memset(late["tab2_s"][:], 0)
-            load_packed_scales(nc.sync, late["tab2_s"], tab2_scales)
+        def spread():
+            late["row"] = held([P, 2, S], F32, "row", "stage")
+            nc.sync.dma_start(out=late["row"][:, 0, :], in_=discount.partition_broadcast(P))
+            nc.sync.dma_start(out=late["row"][:, 1, :], in_=reward.partition_broadcast(P))
 
         v_s0 = held([P, S], U8, "v_s0")
         nc.vector.tensor_copy(v_s0[:], tab_s[:].bitcast(U8).indirect(idx[:]))
@@ -124,14 +124,17 @@ def tile_list_replay_action_targets_kernel(
                 src.rearrange("p a (m t) -> p a t m", t=PACK),
             )
 
-        def late_loads():
-            late["w1"] = held([P, PASSES, PASSES, PACK, BANK], F32, "w1_raw", "stage")
-            for A in range(PASSES):
-                for a in range(PASSES):
-                    rows = w1[a * BANK : (a + 1) * BANK, A * BANK : (A + 1) * BANK]
-                    nc.sync.dma_start(out=late["w1"][:, A, a], in_=rows.rearrange("(p i) c -> p i c", i=PACK))
-            late["tab2"] = queued([P, PASSES, T2], I32, "tab2_w")
-            nc.sync.dma_start(out=late["tab2"][:], in_=tab2_words.rearrange("a p t i -> p a (t i)").bitcast(I32))
+        late["tab2_s"] = held([P, T2 // 4], I32, "tab2_s")
+        nc.gpsimd.memset(late["tab2_s"][:], 0)
+        load_packed_scales(nc.gpsimd, late["tab2_s"], tab2_scales)
+        late["tab2"] = held([P, PASSES, T2], I32, "tab2_w", "stage")
+        nc.sync.dma_start(out=late["tab2"][:], in_=tab2_words.rearrange("a p t i -> p a (t i)").bitcast(I32))
+
+        def load_w1(A):
+            late["w1", A] = queued([P, PASSES, PACK, BANK], F32, f"w1_raw{A}")
+            for a in range(PASSES):
+                rows = w1[a * BANK : (a + 1) * BANK, A * BANK : (A + 1) * BANK]
+                nc.sync.dma_start(out=late["w1", A][:, a], in_=rows.rearrange("(p i) c -> p i c", i=PACK))
 
         w1_w = [[held([P, BANK], U32, f"w1_w{A}{a}") for a in range(PASSES)] for A in range(PASSES)]
         w1_s = [[held([P, BANK], U8, f"w1_s{A}{a}") for a in range(PASSES)] for A in range(PASSES)]
@@ -141,7 +144,7 @@ def tile_list_replay_action_targets_kernel(
         def cast(A, a, n):
             if ("g", A, a) not in live:
                 live["g", A, a] = work.tile([P, PACK * BANK], BF16, name="grouped", tag="w1g", bufs=4, align_bytes=64)
-            src = late["w1"][:, A, a].rearrange("p i (m u e) -> p u m i e", u=2, e=2)
+            src = late["w1", A][:, a].rearrange("p i (m u e) -> p u m i e", u=2, e=2)
             dst = live["g", A, a][:].rearrange("p (u e m i) -> p u m i e", u=2, e=2, i=PACK)
             per = len(CAST[A][a]) // 2
             u, m0 = n // per, (n % per) * (P // per)
@@ -194,7 +197,7 @@ def tile_list_replay_action_targets_kernel(
 
         def mma(A, c):
             cols = slice(c * P, (c + 1) * P)
-            acc = live["a", A, c] = psum.tile([P, PACK, P], F32, name="acc", tag="Y", bufs=4)
+            acc = live["a", A, c] = psum.tile([P, PACK, P], F32, name="acc", tag="Y", bufs=3)
             for t in range(PACK):
                 for a in (1, 0):
                     nc.tensor.matmul_mx(
@@ -235,7 +238,7 @@ def tile_list_replay_action_targets_kernel(
 
         def mmq(c):
             cols = slice(c * P, (c + 1) * P)
-            q = live["q", c] = psum.tile([P, S2], F32, name="q", tag="Y", bufs=4)
+            q = live["q", c] = psum.tile([P, S2], F32, name="q", tag="Y", bufs=3)
             for A in (1, 0):
                 nc.tensor.matmul_mx(
                     out=q[:],
@@ -254,9 +257,43 @@ def tile_list_replay_action_targets_kernel(
             )
 
         def tr(c):
-            back = live["k", c] = psum.tile([P, PACK, P], F32, name="back", tag="X", bufs=4)
+            back = live["k", c] = psum.tile([P, PACK, P], F32, name="back", tag="Z", bufs=1)
             for i in range(S2 // P):
                 nc.tensor.transpose(back[:, i, :], live["s", c][:, i * P : (i + 1) * P], ident[:])
+
+        def mmd(c):
+            cols = slice(c * P, (c + 1) * P)
+            q = live["q", c] = psum.tile([P, PACK, P], F32, name="qd", tag="Y", bufs=3)
+            for i in range(S2 // P):
+                rows = slice(i * P, (i + 1) * P)
+                for A in (1, 0):
+                    nc.tensor.matmul_mx(
+                        out=q[:, i, :],
+                        lhsT=v2_w[A][:, rows].bitcast(FP8X4),
+                        lhsT_scale=v2_s[4 * A : P, rows],
+                        rhs=h_w[A][:, cols].bitcast(FP8X4),
+                        rhs_scale=h_s[A][:, cols],
+                        start=(A == 1),
+                        stop=(A == 0),
+                    )
+
+        def along(which, c):
+            return late["row"][:, which, c * P : (c + 1) * P].unsqueeze(1).to_broadcast([P, PACK, P])
+
+        def mul(c, how):
+            scaled = live["s", c] = work.tile([P, PACK, P], F32, name="scaled")
+            if how == "S":
+                plain = work.tile([P, PACK, P], F32, name="plain")
+                nc.scalar.copy(plain[:], live["q", c][:])
+                nc.gpsimd.tensor_tensor(scaled[:], plain[:], along(0, c), ALU.mult)
+            else:
+                nc.vector.tensor_tensor(scaled[:], live["q", c][:], along(0, c), ALU.mult)
+
+        def add(c, how):
+            res = work.tile([P, PACK, P], F32, name="res")
+            engine = nc.gpsimd if how == "G" else nc.vector
+            engine.tensor_tensor(res[:], live["s", c][:], along(1, c), ALU.add)
+            nc.sync.dma_start(out=out[:, c * P : (c + 1) * P].rearrange("(i p) j -> p i j", p=P), in_=res[:])
 
         def emit(c, how):
             res = work.tile([P, PACK, P], F32, name="res")
@@ -266,170 +303,165 @@ def tile_list_replay_action_targets_kernel(
                 nc.vector.tensor_copy(res[:], live["k", c][:])
             nc.sync.dma_start(out=out[:, c * P : (c + 1) * P].rearrange("(i p) j -> p i j", p=P), in_=res[:])
 
-        perm_w(1)
         perm_w(0)
+        perm_w(1)
         gather_v(0, 1)
-        perm_s(1)
-        perm_s(0)
         gather_v(0, 0)
-        late_loads()
+        perm_s(0)
+        load_w1(0)
+        perm_s(1)
+        gather_v2_scales()
         gather_v(1, 0)
         mmb(0, 0, 2)
         mmb(0, 0, 3)
         mmb(0, 0, 0)
-        mmb(0, 0, 1)
+        mmb(1, 0, 0)
         gather_v(1, 1)
         p1(0, 0, 2)
-        p1(0, 0, 0)
-        p1(0, 0, 3)
-        coefs()
-        p2(0, 0, 2)
-        p1(0, 0, 1)
-        p2(0, 0, 3)
-        cast(0, 0, 0)
-        p2(0, 0, 0)
-        p3(0, 0, 2)
-        p2(0, 0, 1)
-        p3(0, 0, 3)
-        mmb(1, 0, 0)
-        cast(0, 1, 1)
-        p3(0, 0, 0)
-        mmb(1, 0, 1)
-        p3(0, 0, 1)
-        cast(0, 0, 1)
-        p1(1, 0, 0)
-        p1(1, 0, 1)
-        cast(0, 1, 0)
-        p2(1, 0, 0)
-        qw(0, 0)
-        p2(1, 0, 1)
-        qw(0, 1)
-        cast(1, 0, 0)
-        p3(1, 0, 0)
-        mma(0, 2)
-        p3(1, 0, 1)
-        mma(0, 3)
-        cast(1, 0, 1)
-        p4(0, 2, 2, 2, 'V')
-        mma(0, 0)
-        p4(0, 3, 2, 2, 'V')
-        mma(0, 1)
-        p4(0, 0, 0, 2, 'V')
-        cast(1, 1, 0)
-        turn()
-        qw(1, 0)
-        mmb(0, 1, 2)
-        qh(0, 2, 2)
-        mmb(0, 1, 3)
-        cast(1, 1, 1)
-        p4(0, 1, 0, 2, 'V')
-        mmb(0, 1, 0)
-        load_tab2_scales()
-        qh(0, 0, 2)
-        mma(0, 6)
-        gather_v2(1)
-        p1(0, 1, 2)
-        mmb(0, 1, 1)
-        p1(0, 1, 3)
-        qw(1, 1)
-        p2(0, 1, 2)
         gather_v2(0)
+        load_w1(1)
+        p1(0, 0, 3)
+        p2(0, 0, 2)
+        gather_v2(1)
+        p2(0, 0, 3)
+        p1(1, 0, 0)
+        p3(0, 0, 2)
+        spread()
+        p1(0, 0, 0)
+        p3(0, 0, 3)
+        mmb(1, 0, 1)
+        p2(1, 0, 0)
+        cast(0, 1, 0)
+        mmb(0, 0, 1)
+        p2(0, 0, 0)
+        cast(0, 1, 1)
+        p3(1, 0, 0)
+        p1(1, 0, 1)
+        p3(0, 0, 0)
+        cast(0, 0, 0)
+        mmb(1, 0, 2)
+        cast(0, 1, 2)
+        p1(0, 0, 1)
+        mmb(1, 0, 3)
+        cast(0, 1, 3)
+        p2(1, 0, 1)
+        p1(1, 0, 3)
+        p2(0, 0, 1)
+        qw(0, 1)
+        cast(0, 0, 1)
+        p3(1, 0, 1)
+        cast(1, 1, 0)
+        p3(0, 0, 1)
+        mmb(0, 1, 2)
+        cast(1, 1, 1)
+        p1(1, 0, 2)
+        mmb(0, 1, 3)
+        p2(1, 0, 3)
+        qw(0, 0)
+        mma(0, 0)
+        mma(0, 1)
+        mma(0, 2)
+        p2(1, 0, 2)
+        cast(1, 1, 2)
+        p3(1, 0, 3)
+        cast(1, 0, 0)
+        p3(1, 0, 2)
+        cast(1, 1, 3)
+        p4(0, 0, 0, 2, 'V')
+        mmb(0, 1, 0)
+        cast(1, 0, 1)
+        p4(0, 1, 0, 2, 'V')
+        mmb(0, 1, 1)
+        qw(1, 1)
+        qh(0, 0, 2)
+        p1(0, 1, 2)
+        mma(0, 3)
+        qw(1, 0)
         mma(1, 0)
+        p1(0, 1, 3)
+        p4(0, 2, 2, 2, 'V')
+        p2(0, 1, 2)
+        p4(0, 3, 2, 2, 'V')
         p2(0, 1, 3)
         mma(1, 1)
-        p1(0, 1, 0)
         p3(0, 1, 2)
+        p1(0, 1, 0)
+        mma(1, 2)
+        p4(1, 0, 0, 2, 'V')
         p1(0, 1, 1)
-        mma(0, 7)
-        p3(0, 1, 3)
+        mmb(1, 1, 0)
+        p4(1, 1, 0, 2, 'V')
         p2(0, 1, 0)
-        mmb(1, 0, 2)
-        gather_v2_scales()
+        mma(1, 3)
+        p4(1, 2, 2, 2, 'V')
         p2(0, 1, 1)
-        mmb(1, 0, 3)
-        p1(1, 0, 2)
+        qh(1, 0, 2)
+        mma(0, 4)
+        p1(1, 1, 0)
+        p3(0, 1, 3)
+        mmd(0)
+        p4(1, 3, 2, 2, 'V')
+        p2(1, 1, 0)
+        mmb(1, 1, 1)
         p3(0, 1, 0)
-        p1(1, 0, 3)
+        mmd(1)
+        qh(1, 2, 2)
+        p1(1, 1, 1)
         p3(0, 1, 1)
         mmb(1, 1, 2)
-        p2(1, 0, 2)
-        mmb(1, 1, 3)
-        p2(1, 0, 3)
-        p4(0, 6, 6, 1, 'V')
-        p1(1, 1, 2)
-        p3(1, 0, 2)
-        mma(1, 2)
-        p1(1, 1, 3)
-        p3(1, 0, 3)
-        mmb(1, 1, 0)
-        p2(1, 1, 2)
-        qh(0, 6, 1)
-        p4(1, 0, 0, 2, 'V')
-        mmb(1, 1, 1)
-        p2(1, 1, 3)
-        p4(1, 1, 0, 2, 'V')
-        mma(1, 3)
-        p1(1, 1, 0)
-        p4(0, 7, 7, 1, 'V')
-        mma(1, 6)
-        p1(1, 1, 1)
-        qh(1, 0, 2)
-        qh(0, 7, 1)
-        p2(1, 1, 0)
-        mmq(0)
-        p4(1, 2, 2, 2, 'V')
-        p2(1, 1, 1)
-        p4(1, 3, 2, 2, 'V')
-        mmq(1)
-        act(0)
-        p3(1, 1, 2)
-        mma(1, 7)
-        act(1)
-        qh(1, 2, 2)
-        tr(0)
-        p3(1, 1, 3)
-        mmq(2)
+        mul(0, 'S')
         p3(1, 1, 0)
-        emit(0, 'S')
-        tr(1)
-        p3(1, 1, 1)
-        act(2)
-        mmq(3)
-        emit(1, 'S')
-        p4(1, 6, 6, 1, 'V')
-        tr(2)
-        act(3)
-        p4(1, 7, 7, 1, 'V')
-        mma(1, 5)
-        qh(1, 6, 1)
-        qh(1, 7, 1)
-        emit(2, 'V')
-        tr(3)
-        mmq(7)
-        emit(3, 'V')
-        mma(1, 4)
-        act(7)
-        p4(1, 5, 5, 1, 'V')
-        mma(0, 4)
-        p4(1, 4, 4, 1, 'V')
-        tr(7)
-        qh(1, 5, 1)
-        qh(1, 4, 1)
-        emit(7, 'S')
-        mma(0, 5)
+        p2(1, 1, 1)
+        mmb(1, 1, 3)
+        qh(0, 2, 2)
         p4(0, 4, 4, 1, 'V')
-        mmq(6)
-        p4(0, 5, 5, 1, 'V')
-        act(6)
+        mul(1, 'S')
+        mma(1, 7)
+        p3(1, 1, 1)
+        p1(1, 1, 2)
+        mmd(2)
+        p1(1, 1, 3)
         qh(0, 4, 1)
-        mmq(4)
+        mmd(3)
+        p2(1, 1, 2)
+        p2(1, 1, 3)
+        mul(3, 'V')
+        add(0, 'G')
+        mul(2, 'S')
+        p3(1, 1, 2)
+        mma(0, 5)
+        p3(1, 1, 3)
+        add(1, 'G')
+        mma(0, 6)
+        add(3, 'V')
+        p4(1, 7, 7, 1, 'V')
+        p4(0, 5, 5, 1, 'V')
+        mma(1, 5)
+        qh(1, 7, 1)
         qh(0, 5, 1)
-        mmq(5)
-        tr(6)
-        act(4)
-        emit(6, 'V')
-        tr(4)
-        act(5)
-        emit(4, 'S')
-        tr(5)
-        emit(5, 'S')
+        mma(0, 7)
+        add(2, 'G')
+        p4(0, 6, 6, 1, 'V')
+        p4(1, 5, 5, 1, 'V')
+        mma(1, 6)
+        qh(0, 6, 1)
+        qh(1, 5, 1)
+        mma(1, 4)
+        p4(0, 7, 7, 1, 'V')
+        p4(1, 6, 6, 1, 'V')
+        mmd(5)
+        qh(0, 7, 1)
+        p4(1, 4, 4, 1, 'V')
+        mmd(7)
+        qh(1, 6, 1)
+        mul(5, 'V')
+        mmd(6)
+        qh(1, 4, 1)
+        mul(7, 'V')
+        add(5, 'G')
+        mmd(4)
+        mul(6, 'V')
+        add(7, 'V')
+        mul(4, 'V')
+        add(6, 'V')
+        add(4, 'V')

@@ -21,8 +21,9 @@ P = 128
 PACK = 4
 BANK = 512
 PASSES = 2
-CAST = [["SS","VGGG"],["SS","GGGG"]]
-P1V = [[0,0,1],[1,0,3]]
+CAST = [["VV","SS"],["VV","SS"]]
+CHUNKED = [[0,1],[1,1]]
+P1V = [[0,0,1]]
 
 
 def tile_list_replay_action_targets_kernel(
@@ -79,14 +80,14 @@ def tile_list_replay_action_targets_kernel(
         late = {}
 
         def coefs():
-            rows16 = late["rows16"] = held([P, P], F32, "rows16", "w4_raw_s")
+            rows16 = late["rows16"] = held([P, P], F32, "rows16", "w4_raw")
             nc.gpsimd.memset(rows16[:], 0.0)
             nc.sync.dma_start(out=rows16[0:8, :], in_=discount.rearrange("(c p) -> c p", p=P))
             nc.sync.dma_start(out=rows16[8:16, :], in_=reward.rearrange("(c p) -> c p", p=P))
 
         def turn():
             rows16 = late["rows16"]
-            turned = psum.tile([P, P], F32, name="turned", tag="Z", bufs=1)
+            turned = psum.tile([P, P], F32, name="turned", tag="X", bufs=4)
             nc.tensor.transpose(turned[:], rows16[:], ident[:])
             nc.scalar.copy(coef[:], turned[:, 0:16])
 
@@ -124,14 +125,17 @@ def tile_list_replay_action_targets_kernel(
                 src.rearrange("p a (m t) -> p a t m", t=PACK),
             )
 
-        late["tab2_s"] = held([P, T2 // 4], I32, "tab2_s")
-        nc.gpsimd.memset(late["tab2_s"][:], 0)
-        load_packed_scales(nc.gpsimd, late["tab2_s"], tab2_scales)
-        late["tab2"] = held([P, PASSES, T2], I32, "tab2_w", "stage")
-        nc.sync.dma_start(out=late["tab2"][:], in_=tab2_words.rearrange("a p t i -> p a (t i)").bitcast(I32))
+        def load_tab2_scales():
+            late["tab2_s"] = held([P, T2 // 4], I32, "tab2_s", "w4_raw_s")
+            nc.vector.memset(late["tab2_s"][:], 0)
+            load_packed_scales(nc.sync, late["tab2_s"], tab2_scales)
+
+        def load_tab2():
+            late["tab2"] = queued([P, PASSES, T2], I32, "tab2_w")
+            nc.sync.dma_start(out=late["tab2"][:], in_=tab2_words.rearrange("a p t i -> p a (t i)").bitcast(I32))
 
         def load_w1(A):
-            late["w1", A] = queued([P, PASSES, PACK, BANK], F32, f"w1_raw{A}")
+            late["w1", A] = held([P, PASSES, PACK, BANK], F32, "w1_raw0", "stage") if A == 0 else queued([P, PASSES, PACK, BANK], F32, "w1_raw1")
             for a in range(PASSES):
                 rows = w1[a * BANK : (a + 1) * BANK, A * BANK : (A + 1) * BANK]
                 nc.sync.dma_start(out=late["w1", A][:, a], in_=rows.rearrange("(p i) c -> p i c", i=PACK))
@@ -165,6 +169,20 @@ def tile_list_replay_action_targets_kernel(
         def mmb(A, J, t):
             cols = slice(J * BANK, (J + 1) * BANK)
             b = live["b", A, J, t] = psum.tile([P, BANK], F32, name="b", tag="X", bufs=4)
+            if [A, J] in CHUNKED:
+                cols = slice(J * BANK + t * P, J * BANK + (t + 1) * P)
+                for u in range(PACK):
+                    for a in range(PASSES):
+                        nc.tensor.matmul_mx(
+                            out=b[:, u * P : (u + 1) * P],
+                            lhsT=w4_w[A][:, a, 2 * P * u : 2 * P * (u + 1)].bitcast(FP4X4),
+                            lhsT_scale=w4_s[A][:, a, P * u : P * (u + 1)],
+                            rhs=v_w[a][:, cols].bitcast(FP8X4),
+                            rhs_scale=v_s[a][:, cols],
+                            start=(a == 0),
+                            stop=(a == PASSES - 1),
+                        )
+                return
             for a in range(PASSES):
                 nc.tensor.matmul_mx(
                     out=b[:],
@@ -188,6 +206,16 @@ def tile_list_replay_action_targets_kernel(
             nc.scalar.activation(ex[:], live["n", A, J, t][:], ACT.Exp, scale=1.0 if [A, J, t] in P1V else -1.0)
 
         def p3(A, J, t):
+            if [A, J] in CHUNKED:
+                nc.vector.scalar_tensor_tensor(
+                    elu[A][J][:, :, t * P : (t + 1) * P],
+                    live["x", A, J, t][:].rearrange("p (u j) -> p u j", u=PACK),
+                    -1.0,
+                    live["b", A, J, t][:].rearrange("p (u j) -> p u j", u=PACK),
+                    ALU.add,
+                    ALU.max,
+                )
+                return
             nc.vector.scalar_tensor_tensor(
                 elu[A][J][:, t, :], live["x", A, J, t][:], -1.0, live["b", A, J, t][:], ALU.add, ALU.max
             )
@@ -197,7 +225,7 @@ def tile_list_replay_action_targets_kernel(
 
         def mma(A, c):
             cols = slice(c * P, (c + 1) * P)
-            acc = live["a", A, c] = psum.tile([P, PACK, P], F32, name="acc", tag="Y", bufs=3)
+            acc = live["a", A, c] = psum.tile([P, PACK, P], F32, name="acc", tag="Y", bufs=4)
             for t in range(PACK):
                 for a in (1, 0):
                     nc.tensor.matmul_mx(
@@ -238,7 +266,7 @@ def tile_list_replay_action_targets_kernel(
 
         def mmq(c):
             cols = slice(c * P, (c + 1) * P)
-            q = live["q", c] = psum.tile([P, S2], F32, name="q", tag="Y", bufs=3)
+            q = live["q", c] = psum.tile([P, S2], F32, name="q", tag="Y", bufs=4)
             for A in (1, 0):
                 nc.tensor.matmul_mx(
                     out=q[:],
@@ -257,13 +285,13 @@ def tile_list_replay_action_targets_kernel(
             )
 
         def tr(c):
-            back = live["k", c] = psum.tile([P, PACK, P], F32, name="back", tag="Z", bufs=1)
+            back = live["k", c] = psum.tile([P, PACK, P], F32, name="back", tag="X", bufs=4)
             for i in range(S2 // P):
                 nc.tensor.transpose(back[:, i, :], live["s", c][:, i * P : (i + 1) * P], ident[:])
 
         def mmd(c):
             cols = slice(c * P, (c + 1) * P)
-            q = live["q", c] = psum.tile([P, PACK, P], F32, name="qd", tag="Y", bufs=3)
+            q = live["q", c] = psum.tile([P, PACK, P], F32, name="qd", tag="Y", bufs=4)
             for i in range(S2 // P):
                 rows = slice(i * P, (i + 1) * P)
                 for A in (1, 0):
@@ -305,163 +333,165 @@ def tile_list_replay_action_targets_kernel(
 
         perm_w(0)
         perm_w(1)
+        coefs()
+        load_w1(0)
         gather_v(0, 1)
         gather_v(0, 0)
         perm_s(0)
-        load_w1(0)
         perm_s(1)
-        gather_v2_scales()
+        load_w1(1)
+        load_tab2_scales()
         gather_v(1, 0)
         mmb(0, 0, 2)
         mmb(0, 0, 3)
-        mmb(0, 0, 0)
-        mmb(1, 0, 0)
-        gather_v(1, 1)
-        p1(0, 0, 2)
-        gather_v2(0)
-        load_w1(1)
-        p1(0, 0, 3)
-        p2(0, 0, 2)
-        gather_v2(1)
-        p2(0, 0, 3)
-        p1(1, 0, 0)
-        p3(0, 0, 2)
-        spread()
-        p1(0, 0, 0)
-        p3(0, 0, 3)
-        mmb(1, 0, 1)
-        p2(1, 0, 0)
-        cast(0, 1, 0)
         mmb(0, 0, 1)
-        p2(0, 0, 0)
+        gather_v(1, 1)
+        mmb(0, 1, 0)
+        p1(0, 0, 2)
+        cast(0, 0, 0)
+        p1(0, 0, 3)
+        cast(0, 0, 1)
+        p2(0, 0, 2)
+        p2(0, 0, 3)
+        p1(0, 0, 1)
+        load_tab2()
+        p1(0, 1, 0)
+        qw(0, 0)
+        cast(0, 1, 0)
+        p3(0, 0, 2)
+        p3(0, 0, 3)
+        mmb(1, 0, 3)
+        p2(0, 1, 0)
+        cast(1, 0, 0)
+        mmb(1, 0, 0)
+        p1(1, 0, 3)
+        cast(1, 0, 1)
+        p1(1, 0, 0)
+        p3(0, 1, 0)
+        p2(1, 0, 3)
+        qw(1, 0)
+        p2(1, 0, 0)
+        mmb(0, 0, 0)
+        p3(1, 0, 3)
         cast(0, 1, 1)
         p3(1, 0, 0)
-        p1(1, 0, 1)
-        p3(0, 0, 0)
-        cast(0, 0, 0)
-        mmb(1, 0, 2)
-        cast(0, 1, 2)
-        p1(0, 0, 1)
-        mmb(1, 0, 3)
-        cast(0, 1, 3)
-        p2(1, 0, 1)
-        p1(1, 0, 3)
+        mmb(0, 1, 1)
+        gather_v2_scales()
         p2(0, 0, 1)
+        mmb(1, 0, 1)
+        spread()
+        p1(0, 0, 0)
         qw(0, 1)
-        cast(0, 0, 1)
-        p3(1, 0, 1)
         cast(1, 1, 0)
         p3(0, 0, 1)
-        mmb(0, 1, 2)
+        mma(0, 2)
+        gather_v2(1)
+        mma(0, 3)
+        p2(0, 0, 0)
+        turn()
         cast(1, 1, 1)
-        p1(1, 0, 2)
-        mmb(0, 1, 3)
-        p2(1, 0, 3)
-        qw(0, 0)
+        gather_v2(0)
         mma(0, 0)
         mma(0, 1)
-        mma(0, 2)
-        p2(1, 0, 2)
-        cast(1, 1, 2)
-        p3(1, 0, 3)
-        cast(1, 0, 0)
-        p3(1, 0, 2)
-        cast(1, 1, 3)
-        p4(0, 0, 0, 2, 'V')
-        mmb(0, 1, 0)
-        cast(1, 0, 1)
-        p4(0, 1, 0, 2, 'V')
-        mmb(0, 1, 1)
-        qw(1, 1)
-        qh(0, 0, 2)
-        p1(0, 1, 2)
-        mma(0, 3)
-        qw(1, 0)
-        mma(1, 0)
-        p1(0, 1, 3)
-        p4(0, 2, 2, 2, 'V')
-        p2(0, 1, 2)
-        p4(0, 3, 2, 2, 'V')
-        p2(0, 1, 3)
-        mma(1, 1)
-        p3(0, 1, 2)
-        p1(0, 1, 0)
-        mma(1, 2)
-        p4(1, 0, 0, 2, 'V')
+        p3(0, 0, 0)
         p1(0, 1, 1)
-        mmb(1, 1, 0)
-        p4(1, 1, 0, 2, 'V')
-        p2(0, 1, 0)
-        mma(1, 3)
-        p4(1, 2, 2, 2, 'V')
+        qw(1, 1)
+        p1(1, 0, 1)
+        mmb(1, 0, 2)
+        p4(0, 2, 2, 2, 'V')
         p2(0, 1, 1)
-        qh(1, 0, 2)
-        mma(0, 4)
-        p1(1, 1, 0)
-        p3(0, 1, 3)
-        mmd(0)
-        p4(1, 3, 2, 2, 'V')
-        p2(1, 1, 0)
-        mmb(1, 1, 1)
-        p3(0, 1, 0)
-        mmd(1)
-        qh(1, 2, 2)
-        p1(1, 1, 1)
+        p4(0, 3, 2, 2, 'V')
+        p2(1, 0, 1)
+        mma(1, 0)
         p3(0, 1, 1)
-        mmb(1, 1, 2)
-        mul(0, 'S')
-        p3(1, 1, 0)
-        p2(1, 1, 1)
-        mmb(1, 1, 3)
+        p1(1, 0, 2)
+        mma(1, 1)
         qh(0, 2, 2)
+        p3(1, 0, 1)
+        mmb(0, 1, 2)
+        p2(1, 0, 2)
+        p4(0, 0, 0, 2, 'V')
+        mmb(0, 1, 3)
+        p4(0, 1, 0, 2, 'V')
+        p1(0, 1, 2)
+        mma(0, 4)
+        p3(1, 0, 2)
+        p2(0, 1, 2)
+        qh(0, 0, 2)
+        mmb(1, 1, 1)
+        p4(1, 0, 0, 2, 'V')
+        p1(0, 1, 3)
+        mma(1, 2)
+        p4(1, 1, 0, 2, 'V')
+        p1(1, 1, 1)
+        p3(0, 1, 2)
+        mma(1, 3)
+        p2(0, 1, 3)
+        qh(1, 0, 2)
+        mmb(1, 1, 2)
+        p2(1, 1, 1)
         p4(0, 4, 4, 1, 'V')
-        mul(1, 'S')
-        mma(1, 7)
+        mmd(0)
+        p3(0, 1, 3)
+        mmd(1)
+        qh(0, 4, 1)
+        mul(0, 'S')
         p3(1, 1, 1)
+        p4(1, 2, 2, 2, 'V')
+        mmb(1, 1, 0)
+        mma(0, 7)
         p1(1, 1, 2)
+        p4(1, 3, 2, 2, 'V')
+        mul(1, 'V')
+        p2(1, 1, 2)
+        mmb(1, 1, 3)
+        qh(1, 2, 2)
+        p1(1, 1, 0)
+        add(0, 'G')
+        p4(0, 7, 7, 1, 'V')
+        mma(1, 4)
         mmd(2)
         p1(1, 1, 3)
-        qh(0, 4, 1)
-        mmd(3)
-        p2(1, 1, 2)
-        p2(1, 1, 3)
-        mul(3, 'V')
-        add(0, 'G')
-        mul(2, 'S')
         p3(1, 1, 2)
-        mma(0, 5)
-        p3(1, 1, 3)
+        mmq(3)
+        p2(1, 1, 0)
+        qh(0, 7, 1)
         add(1, 'G')
-        mma(0, 6)
-        add(3, 'V')
-        p4(1, 7, 7, 1, 'V')
-        p4(0, 5, 5, 1, 'V')
+        mul(2, 'S')
+        p3(1, 1, 0)
+        mma(0, 5)
+        act(3)
+        p2(1, 1, 3)
+        p4(1, 4, 4, 1, 'V')
         mma(1, 5)
-        qh(1, 7, 1)
-        qh(0, 5, 1)
-        mma(0, 7)
+        tr(3)
+        p4(0, 5, 5, 1, 'V')
+        p3(1, 1, 3)
+        emit(3, 'S')
+        mma(0, 6)
         add(2, 'G')
-        p4(0, 6, 6, 1, 'V')
-        p4(1, 5, 5, 1, 'V')
         mma(1, 6)
-        qh(0, 6, 1)
+        qh(1, 4, 1)
+        mma(1, 7)
+        qh(0, 5, 1)
+        p4(1, 5, 5, 1, 'V')
+        p4(0, 6, 6, 1, 'V')
+        mmq(4)
         qh(1, 5, 1)
-        mma(1, 4)
-        p4(0, 7, 7, 1, 'V')
         p4(1, 6, 6, 1, 'V')
         mmd(5)
-        qh(0, 7, 1)
-        p4(1, 4, 4, 1, 'V')
-        mmd(7)
+        act(4)
+        qh(0, 6, 1)
+        p4(1, 7, 7, 1, 'V')
+        tr(4)
         qh(1, 6, 1)
         mul(5, 'V')
         mmd(6)
-        qh(1, 4, 1)
-        mul(7, 'V')
+        qh(1, 7, 1)
+        emit(4, 'V')
         add(5, 'G')
-        mmd(4)
+        mmd(7)
         mul(6, 'V')
-        add(7, 'V')
-        mul(4, 'V')
+        mul(7, 'V')
         add(6, 'V')
-        add(4, 'V')
+        add(7, 'V')

@@ -1,7 +1,6 @@
 from contextlib import ExitStack
 
 import concourse.mybir as mybir
-from concourse.masks import make_identity
 
 K, H, T, S, T2, S2 = 1024, 1024, 4096, 1024, 1024, 512
 FLOPS = 2 * K * H * S * 2 + 2 * H * S2 * S
@@ -19,11 +18,19 @@ ACT = mybir.ActivationFunctionType
 
 P = 128
 PACK = 4
-BANK = 512
-PASSES = 2
-CAST = [["VV","SS"],["VV","SS"]]
-CHUNKED = [[0,1],[1,1]]
-P1V = [[0,0,1]]
+PASS = P * PACK
+PASSES = K // PASS
+LIST_ROWS = 16
+
+GATE_BANKS = 4
+LINEAR_BANKS = 4
+
+GATE_ORDER = [(half, n) for part in range(2) for half in range(2) for n in range(4 * part, 4 * part + 4)]
+HIDDEN_ORDER = [(half, n) for part in range(2) for half in range(2) for n in range(4 * part, 4 * part + 4)]
+RUNS = [(0, 2), (2, 2), (4, 1), (5, 1), (6, 1), (7, 1)]
+CAST_ENGINES = "VVVSSVSS"
+EPILOGUE = ["SG", "SG", "VG", "VG", "VG", "VV", "VV", "VV"]
+SCHEDULE = "cvcgggcgcgqwqcccsgwqhcgqbhgghhgghhhhgttgghhtgghhhthhhtttt"
 
 
 def tile_list_replay_action_targets_kernel(
@@ -38,460 +45,248 @@ def tile_list_replay_action_targets_kernel(
         def held(shape, dtype, name, tag=None):
             return keep.tile(shape, dtype, name=name, tag=tag or name, align_bytes=64)
 
-        idx = keep.tile([P, S // 16], U16, name="idx")
-        idx2 = keep.tile([P, S2 // 16], U16, name="idx2")
-        tab_s = held([P, T // 4], I32, "tab_s", "stage")
-        w4_raw = held([P, PASSES, H // 2], I32, "w4_raw")
-        w4_raw_s = held([P, PASSES, H // 4], I32, "w4_raw_s")
         def queued(shape, dtype, name):
             return keep.tile(shape, dtype, name=name, tag="queued", bufs=3, align_bytes=64)
 
+        def mx_sum(acc, operands):
+            for n, (lhs, lhs_scale, rhs, rhs_scale) in enumerate(operands):
+                nc.tensor.matmul_mx(
+                    out=acc,
+                    lhsT=lhs,
+                    lhsT_scale=lhs_scale,
+                    rhs=rhs,
+                    rhs_scale=rhs_scale,
+                    start=(n == 0),
+                    stop=(n == len(operands) - 1),
+                )
+
+        def load_both_planes(dst, src):
+            for quad in range(4):
+                nc.sync.dma_start(
+                    out=dst[32 * quad : 32 * quad + 8, :], in_=src.bitcast(I32)[:, 4 * quad : 4 * quad + 4, :]
+                )
+
+        def load_w1(dst, half):
+            for a in range(PASSES):
+                rows = w1[a * PASS : (a + 1) * PASS, half * PASS : (half + 1) * PASS]
+                nc.sync.dma_start(out=dst[:, a], in_=rows.rearrange("(p i) c -> p i c", i=PACK))
+
+        idx = keep.tile([P, S // LIST_ROWS], U16, name="idx")
+        idx2 = keep.tile([P, S2 // LIST_ROWS], U16, name="idx2")
+        tab_s = held([P, T // 4], I32, "tab_s", "stage")
+        w4_raw = held([P, PASSES, H // 2], I32, "w4_raw")
+        w4_raw_s = held([P, PASSES, H // 4], I32, "w4_raw_s")
         v_s1 = queued([P, S // 4], I32, "v_s1")
         tab_w = [queued([P, T], I32, f"tab_w{a}") for a in range(PASSES)]
-        coef = held([P, 16], F32, "coef")
-        ident = held([P, P], F32, "ident")
-        warm = held([P, 1], F32, "warm")
+        warm = held([P, 2], F32, "warm")
 
         nc.vector.memset(tab_s[:], 0)
         nc.vector.memset(w4_raw_s[:], 0)
         nc.vector.memset(v_s1[:], 0)
-        make_identity(nc, ident[:])
-
-        def load_words(dst, src):
-            nc.sync.dma_start(out=dst, in_=src.rearrange("p t i -> p (t i)").bitcast(I32))
-
-        def load_packed_scales(queue, dst, src):
-            for Q in range(4):
-                queue.dma_start(out=dst[32 * Q : 32 * Q + 8, :], in_=src.bitcast(I32)[:, 4 * Q : 4 * Q + 4, :])
+        nc.gpsimd.memset(warm[:, 0:1], 0.0)
+        nc.scalar.activation(warm[:, 1:2], warm[:, 0:1], ACT.Exp)
 
         nc.sync.dma_start(idx[:], offs)
         nc.sync.dma_start(idx2[:], offs2)
         nc.sync.dma_start(out=w4_raw[:], in_=w4_words.bitcast(I32).rearrange("a p c -> p a c"))
-        load_packed_scales(nc.sync, tab_s, tab_scales)
-        load_words(tab_w[0][:], tab_words[0])
-        for Q in range(4):
+        load_both_planes(tab_s, tab_scales)
+        nc.sync.dma_start(out=tab_w[0][:], in_=tab_words[0].rearrange("p t i -> p (t i)").bitcast(I32))
+        for quad in range(4):
             nc.sync.dma_start(
-                out=w4_raw_s[32 * Q : 32 * Q + 4, :, :],
-                in_=w4_scales.bitcast(I32)[:, 4 * Q : 4 * Q + 4, :].rearrange("a r c -> r a c"),
+                out=w4_raw_s[32 * quad : 32 * quad + 4, :, :],
+                in_=w4_scales.bitcast(I32)[:, 4 * quad : 4 * quad + 4, :].rearrange("a s c -> s a c"),
             )
-        load_words(tab_w[1][:], tab_words[1])
-        nc.scalar.activation(warm[:], ident[:, 0:1], ACT.Exp)
-
-        late = {}
-
-        def coefs():
-            rows16 = late["rows16"] = held([P, P], F32, "rows16", "w4_raw")
-            nc.gpsimd.memset(rows16[:], 0.0)
-            nc.sync.dma_start(out=rows16[0:8, :], in_=discount.rearrange("(c p) -> c p", p=P))
-            nc.sync.dma_start(out=rows16[8:16, :], in_=reward.rearrange("(c p) -> c p", p=P))
-
-        def turn():
-            rows16 = late["rows16"]
-            turned = psum.tile([P, P], F32, name="turned", tag="X", bufs=4)
-            nc.tensor.transpose(turned[:], rows16[:], ident[:])
-            nc.scalar.copy(coef[:], turned[:, 0:16])
-
-        def spread():
-            late["row"] = held([P, 2, S], F32, "row", "stage")
-            nc.sync.dma_start(out=late["row"][:, 0, :], in_=discount.partition_broadcast(P))
-            nc.sync.dma_start(out=late["row"][:, 1, :], in_=reward.partition_broadcast(P))
+        nc.sync.dma_start(out=tab_w[1][:], in_=tab_words[1].rearrange("p t i -> p (t i)").bitcast(I32))
 
         v_s0 = held([P, S], U8, "v_s0")
         nc.vector.tensor_copy(v_s0[:], tab_s[:].bitcast(U8).indirect(idx[:]))
-        for Q in range(4):
-            nc.sync.dma_start(out=v_s1[32 * Q : 32 * Q + 4, :], in_=v_s0[:].bitcast(I32)[32 * Q + 4 : 32 * Q + 8, :])
+        for quad in range(4):
+            nc.sync.dma_start(
+                out=v_s1[32 * quad : 32 * quad + 4, :], in_=v_s0[:].bitcast(I32)[32 * quad + 4 : 32 * quad + 8, :]
+            )
         v_s = [v_s0[:], v_s1[:].bitcast(U8)]
         v_w = [held([P, S], U32, f"v_w{a}") for a in range(PASSES)]
 
-        def gather_v(a, J):
+        def gather_states(a, part):
+            entries = idx[:, part * PASS // LIST_ROWS : (part + 1) * PASS // LIST_ROWS]
             nc.vector.tensor_copy(
-                v_w[a][:, J * BANK : (J + 1) * BANK], tab_w[a][:].bitcast(U32).indirect(idx[:, 32 * J : 32 * J + 32])
+                v_w[a][:, part * PASS : (part + 1) * PASS], tab_w[a][:].bitcast(U32).indirect(entries)
             )
 
-        w4_w = [held([P, PASSES, 2 * BANK], U8, f"w4_w{A}") for A in range(PASSES)]
-        w4_s = [held([P, PASSES, BANK], U8, f"w4_s{A}") for A in range(PASSES)]
-
-        def perm_w(A):
-            src = w4_raw[:].bitcast(U16)[:, :, A * BANK : (A + 1) * BANK]
+        def regroup(dst, src, half):
             nc.vector.tensor_copy(
-                w4_w[A][:].bitcast(U16).rearrange("p a (t m) -> p a t m", t=PACK),
-                src.rearrange("p a (m t) -> p a t m", t=PACK),
+                dst.rearrange("p a (t m) -> p a t m", t=PACK),
+                src[:, :, half * PASS : (half + 1) * PASS].rearrange("p a (m t) -> p a t m", t=PACK),
             )
 
-        def perm_s(A):
-            src = w4_raw_s[:].bitcast(U8)[:, :, A * BANK : (A + 1) * BANK]
-            nc.vector.tensor_copy(
-                w4_s[A][:].rearrange("p a (t m) -> p a t m", t=PACK),
-                src.rearrange("p a (m t) -> p a t m", t=PACK),
-            )
+        w4_w = [held([P, PASSES, 2 * PASS], U8, f"w4_w{half}") for half in range(2)]
+        w4_s = [held([P, PASSES, PASS], U8, f"w4_s{half}") for half in range(2)]
+        for half in range(2):
+            regroup(w4_w[half][:].bitcast(U16), w4_raw[:].bitcast(U16), half)
+        w1_raw = [held([P, PASSES, PACK, PASS], F32, "w1_raw0", "stage")]
+        load_w1(w1_raw[0], 0)
+        gather_states(0, 0)
+        for half in range(2):
+            regroup(w4_s[half][:], w4_raw_s[:].bitcast(U8), half)
+        gather_states(0, 1)
+        w1_raw.append(queued([P, PASSES, PACK, PASS], F32, "w1_raw1"))
+        load_w1(w1_raw[1], 1)
+        tab2_s = held([P, T2 // 4], I32, "tab2_s", "w4_raw_s")
+        nc.vector.memset(tab2_s[:], 0)
+        load_both_planes(tab2_s, tab2_scales)
+        gather_states(1, 0)
 
-        def load_tab2_scales():
-            late["tab2_s"] = held([P, T2 // 4], I32, "tab2_s", "w4_raw_s")
-            nc.vector.memset(late["tab2_s"][:], 0)
-            load_packed_scales(nc.sync, late["tab2_s"], tab2_scales)
-
-        def load_tab2():
-            late["tab2"] = queued([P, PASSES, T2], I32, "tab2_w")
-            nc.sync.dma_start(out=late["tab2"][:], in_=tab2_words.rearrange("a p t i -> p a (t i)").bitcast(I32))
-
-        def load_w1(A):
-            late["w1", A] = held([P, PASSES, PACK, BANK], F32, "w1_raw0", "stage") if A == 0 else queued([P, PASSES, PACK, BANK], F32, "w1_raw1")
-            for a in range(PASSES):
-                rows = w1[a * BANK : (a + 1) * BANK, A * BANK : (A + 1) * BANK]
-                nc.sync.dma_start(out=late["w1", A][:, a], in_=rows.rearrange("(p i) c -> p i c", i=PACK))
-
-        w1_w = [[held([P, BANK], U32, f"w1_w{A}{a}") for a in range(PASSES)] for A in range(PASSES)]
-        w1_s = [[held([P, BANK], U8, f"w1_s{A}{a}") for a in range(PASSES)] for A in range(PASSES)]
-
-        live = {}
-
-        def cast(A, a, n):
-            if ("g", A, a) not in live:
-                live["g", A, a] = work.tile([P, PACK * BANK], BF16, name="grouped", tag="w1g", bufs=4, align_bytes=64)
-            src = late["w1", A][:, a].rearrange("p i (m u e) -> p u m i e", u=2, e=2)
-            dst = live["g", A, a][:].rearrange("p (u e m i) -> p u m i e", u=2, e=2, i=PACK)
-            per = len(CAST[A][a]) // 2
-            u, m0 = n // per, (n % per) * (P // per)
-            piece_in, piece_out = src[:, u, m0 : m0 + P // per], dst[:, u, m0 : m0 + P // per]
-            eng = CAST[A][a][n]
-            if eng == "V":
-                nc.vector.tensor_copy(piece_out, piece_in)
-            elif eng == "S":
-                nc.scalar.copy(piece_out, piece_in)
-            else:
-                nc.gpsimd.tensor_scalar(piece_out, piece_in, 1.0, 0.0, ALU.mult, ALU.add)
-
-        def qw(A, a):
-            nc.vector.quantize_mx(out=w1_w[A][a][:].bitcast(FP8X4), scales=w1_s[A][a][:], in_=live["g", A, a][:])
-
-        elu = [[held([P, PACK, BANK], F32, f"elu{A}{J}") for J in range(2)] for A in range(PASSES)]
-
-        def mmb(A, J, t):
-            cols = slice(J * BANK, (J + 1) * BANK)
-            b = live["b", A, J, t] = psum.tile([P, BANK], F32, name="b", tag="X", bufs=4)
-            if [A, J] in CHUNKED:
-                cols = slice(J * BANK + t * P, J * BANK + (t + 1) * P)
-                for u in range(PACK):
-                    for a in range(PASSES):
-                        nc.tensor.matmul_mx(
-                            out=b[:, u * P : (u + 1) * P],
-                            lhsT=w4_w[A][:, a, 2 * P * u : 2 * P * (u + 1)].bitcast(FP4X4),
-                            lhsT_scale=w4_s[A][:, a, P * u : P * (u + 1)],
-                            rhs=v_w[a][:, cols].bitcast(FP8X4),
-                            rhs_scale=v_s[a][:, cols],
-                            start=(a == 0),
-                            stop=(a == PASSES - 1),
-                        )
-                return
-            for a in range(PASSES):
-                nc.tensor.matmul_mx(
-                    out=b[:],
-                    lhsT=w4_w[A][:, a, 2 * P * t : 2 * P * (t + 1)].bitcast(FP4X4),
-                    lhsT_scale=w4_s[A][:, a, P * t : P * (t + 1)],
-                    rhs=v_w[a][:, cols].bitcast(FP8X4),
-                    rhs_scale=v_s[a][:, cols],
-                    start=(a == 0),
-                    stop=(a == PASSES - 1),
-                )
-
-        def p1(A, J, t):
-            neg = live["n", A, J, t] = work.tile([P, BANK], F32, name="neg")
-            if [A, J, t] in P1V:
-                nc.vector.tensor_scalar(neg[:], live["b", A, J, t][:], 0.0, None, ALU.min)
-            else:
-                nc.scalar.activation(neg[:], live["b", A, J, t][:], ACT.Relu, scale=-1.0)
-
-        def p2(A, J, t):
-            ex = live["x", A, J, t] = work.tile([P, BANK], F32, name="ex")
-            nc.scalar.activation(ex[:], live["n", A, J, t][:], ACT.Exp, scale=1.0 if [A, J, t] in P1V else -1.0)
-
-        def p3(A, J, t):
-            if [A, J] in CHUNKED:
-                nc.vector.scalar_tensor_tensor(
-                    elu[A][J][:, :, t * P : (t + 1) * P],
-                    live["x", A, J, t][:].rearrange("p (u j) -> p u j", u=PACK),
-                    -1.0,
-                    live["b", A, J, t][:].rearrange("p (u j) -> p u j", u=PACK),
-                    ALU.add,
-                    ALU.max,
-                )
-                return
-            nc.vector.scalar_tensor_tensor(
-                elu[A][J][:, t, :], live["x", A, J, t][:], -1.0, live["b", A, J, t][:], ALU.add, ALU.max
-            )
-
-        h_w = [held([P, S], U32, f"h_w{A}") for A in range(PASSES)]
-        h_s = [held([P, S], U8, f"h_s{A}") for A in range(PASSES)]
-
-        def mma(A, c):
-            cols = slice(c * P, (c + 1) * P)
-            acc = live["a", A, c] = psum.tile([P, PACK, P], F32, name="acc", tag="Y", bufs=4)
-            for t in range(PACK):
-                for a in (1, 0):
-                    nc.tensor.matmul_mx(
-                        out=acc[:, t, :],
-                        lhsT=w1_w[A][a][:, P * t : P * (t + 1)].bitcast(FP8X4),
-                        lhsT_scale=w1_s[A][a][:, P * t : P * (t + 1)],
-                        rhs=v_w[a][:, cols].bitcast(FP8X4),
-                        rhs_scale=v_s[a][:, cols],
-                        start=(a == 1),
-                        stop=(a == 0),
-                    )
-
-        def p4(A, c, c0, n, how):
-            if ("h", A, c0) not in live:
-                live["h", A, c0] = work.tile([P, n * BANK], BF16, name="h", align_bytes=64)
-            dst = live["h", A, c0][:, (c - c0) * BANK : (c - c0 + 1) * BANK].rearrange("p (c e t) -> p c t e", e=2, t=PACK)
-            acc = live["a", A, c][:].rearrange("p t (c e) -> p c t e", e=2)
-            gate = elu[A][c // 4][:, :, (c % 4) * P : (c % 4 + 1) * P].rearrange("p t (c e) -> p c t e", e=2)
-            if how == "V":
-                nc.vector.tensor_tensor(dst, acc, gate, ALU.mult)
-            else:
-                plain = work.tile([P, PACK, P], F32, name="plain")
-                nc.scalar.copy(plain[:], live["a", A, c][:])
-                nc.gpsimd.tensor_tensor(dst, plain[:].rearrange("p t (c e) -> p c t e", e=2), gate, ALU.mult)
-
-        def qh(A, c0, n):
-            cols = slice(c0 * P, (c0 + n) * P)
-            nc.vector.quantize_mx(out=h_w[A][:, cols].bitcast(FP8X4), scales=h_s[A][:, cols], in_=live["h", A, c0][:])
-
+        w1_w = [[held([P, PASS], U32, f"w1_w{half}{a}") for a in range(PASSES)] for half in range(2)]
+        w1_s = [[held([P, PASS], U8, f"w1_s{half}{a}") for a in range(PASSES)] for half in range(2)]
         v2_s = held([P, S2], U8, "v2_s")
-        v2_w = [held([P, S2], U32, f"v2_w{A}") for A in range(PASSES)]
+        v2_w = [held([P, S2], U32, f"v2_w{half}") for half in range(2)]
+        elu = [[held([P, PACK, PASS], F32, f"elu{half}{part}") for part in range(2)] for half in range(2)]
+        h_w = {first: held([P, 2, count * P], U32, f"h_w{first}") for first, count in RUNS}
+        h_s = {first: held([P, 2, count * P], U8, f"h_s{first}") for first, count in RUNS}
+        run_of = {chunk: run for run in RUNS for chunk in range(run[0], run[0] + run[1])}
+        value_banks = [(first, count, bank) for first, count in RUNS for bank in range(count)]
+        live = {}
+        tiles_done = {first: 0 for first, count in RUNS}
 
-        def gather_v2_scales():
-            nc.vector.tensor_copy(v2_s[:], late["tab2_s"][:].bitcast(U8).indirect(idx2[:]))
+        def last_state_gather(n):
+            gather_states(1, 1)
+            live["tab2_w"] = queued([P, 2, T2], I32, "tab2_w")
+            nc.sync.dma_start(out=live["tab2_w"][:], in_=tab2_words.rearrange("a p t i -> p a (t i)").bitcast(I32))
 
-        def gather_v2(A):
-            nc.vector.tensor_copy(v2_w[A][:], late["tab2"][:, A, :].bitcast(U32).indirect(idx2[:]))
+        def gather_action_scales(n):
+            nc.vector.tensor_copy(v2_s[:], tab2_s[:].bitcast(U8).indirect(idx2[:]))
 
-        def mmq(c):
-            cols = slice(c * P, (c + 1) * P)
-            q = live["q", c] = psum.tile([P, S2], F32, name="q", tag="Y", bufs=4)
-            for A in (1, 0):
-                nc.tensor.matmul_mx(
-                    out=q[:],
-                    lhsT=h_w[A][:, cols].bitcast(FP8X4),
-                    lhsT_scale=h_s[A][:, cols],
-                    rhs=v2_w[A][:].bitcast(FP8X4),
-                    rhs_scale=v2_s[4 * A : P, :],
-                    start=(A == 1),
-                    stop=(A == 0),
-                )
+        def gather_action_words(half):
+            nc.vector.tensor_copy(v2_w[half][:], live["tab2_w"][:, half, :].bitcast(U32).indirect(idx2[:]))
 
-        def act(c):
-            scaled = live["s", c] = work.tile([P, S2], F32, name="scaled")
-            nc.scalar.activation(
-                scaled[:], live["q", c][:], ACT.Identity, scale=coef[:, c : c + 1], bias=coef[:, 8 + c : 9 + c]
+        def load_rows(n):
+            live["rows"] = held([P, 2, S], F32, "rows", "stage")
+            nc.sync.dma_start(out=live["rows"][:, 0, :], in_=discount.partition_broadcast(P))
+            nc.sync.dma_start(out=live["rows"][:, 1, :], in_=reward.partition_broadcast(P))
+
+        def cast_w1(n):
+            half, a, u = n // 4, n // 2 % 2, n % 2
+            if u == 0:
+                live["grouped", half, a] = work.tile([P, PACK * PASS], BF16, name="grouped", align_bytes=64)
+            src = w1_raw[half][:, a].rearrange("p i (m u e) -> p u m i e", u=2, e=2)[:, u]
+            dst = live["grouped", half, a][:].rearrange("p (u e m i) -> p u m i e", u=2, e=2, i=PACK)[:, u]
+            if CAST_ENGINES[n] == "V":
+                nc.vector.tensor_copy(dst, src)
+            else:
+                nc.scalar.copy(dst, src)
+
+        def quantise_w1(n):
+            half, a = n // 2, n % 2
+            nc.vector.quantize_mx(
+                out=w1_w[half][a][:].bitcast(FP8X4), scales=w1_s[half][a][:], in_=live["grouped", half, a][:]
             )
 
-        def tr(c):
-            back = live["k", c] = psum.tile([P, PACK, P], F32, name="back", tag="X", bufs=4)
-            for i in range(S2 // P):
-                nc.tensor.transpose(back[:, i, :], live["s", c][:, i * P : (i + 1) * P], ident[:])
-
-        def mmd(c):
-            cols = slice(c * P, (c + 1) * P)
-            q = live["q", c] = psum.tile([P, PACK, P], F32, name="qd", tag="Y", bufs=4)
-            for i in range(S2 // P):
-                rows = slice(i * P, (i + 1) * P)
-                for A in (1, 0):
-                    nc.tensor.matmul_mx(
-                        out=q[:, i, :],
-                        lhsT=v2_w[A][:, rows].bitcast(FP8X4),
-                        lhsT_scale=v2_s[4 * A : P, rows],
-                        rhs=h_w[A][:, cols].bitcast(FP8X4),
-                        rhs_scale=h_s[A][:, cols],
-                        start=(A == 1),
-                        stop=(A == 0),
+        def gate(n):
+            half, tile = GATE_ORDER[n]
+            part, t = tile // PACK, tile % PACK
+            states = slice(part * PASS, (part + 1) * PASS)
+            b = psum.tile([P, PASS], F32, name="b", tag="gate", bufs=GATE_BANKS)
+            mx_sum(
+                b[:],
+                [
+                    (
+                        w4_w[half][:, a, 2 * P * t : 2 * P * (t + 1)].bitcast(FP4X4),
+                        w4_s[half][:, a, P * t : P * (t + 1)],
+                        v_w[a][:, states].bitcast(FP8X4),
+                        v_s[a][:, states],
                     )
+                    for a in range(PASSES)
+                ],
+            )
+            clamped = work.tile([P, PASS], F32, name="clamped")
+            grown = work.tile([P, PASS], F32, name="grown")
+            nc.scalar.activation(clamped[:], b[:], ACT.Relu, scale=-1.0)
+            nc.scalar.activation(grown[:], clamped[:], ACT.Exp, scale=-1.0)
+            nc.vector.scalar_tensor_tensor(elu[half][part][:, t, :], grown[:], -1.0, b[:], ALU.add, ALU.max)
 
-        def along(which, c):
-            return late["row"][:, which, c * P : (c + 1) * P].unsqueeze(1).to_broadcast([P, PACK, P])
+        def hidden(n):
+            half, chunk = HIDDEN_ORDER[n]
+            first, count = run_of[chunk]
+            states = slice(chunk * P, (chunk + 1) * P)
+            acc = psum.tile([P, PACK, P], F32, name="acc", tag="linear_or_value", bufs=LINEAR_BANKS)
+            for t in range(PACK):
+                mx_sum(
+                    acc[:, t, :],
+                    [
+                        (
+                            w1_w[half][a][:, P * t : P * (t + 1)].bitcast(FP8X4),
+                            w1_s[half][a][:, P * t : P * (t + 1)],
+                            v_w[a][:, states].bitcast(FP8X4),
+                            v_s[a][:, states],
+                        )
+                        for a in (1, 0)
+                    ],
+                )
+            if tiles_done[first] == 0:
+                live["h", first] = work.tile([P, 2, count, PASS], BF16, name="h", bufs=len(RUNS), align_bytes=64)
+            h = live["h", first]
+            in_part = chunk % PACK
+            nc.vector.tensor_tensor(
+                h[:, half, chunk - first, :].rearrange("p (c e t) -> p c t e", e=2, t=PACK),
+                acc[:].rearrange("p t (c e) -> p c t e", e=2),
+                elu[half][chunk // PACK][:, :, in_part * P : (in_part + 1) * P].rearrange("p t (c e) -> p c t e", e=2),
+                ALU.mult,
+            )
+            tiles_done[first] += 1
+            if tiles_done[first] == 2 * count:
+                nc.vector.quantize_mx(
+                    out=h_w[first][:].rearrange("p a j -> p (a j)").bitcast(FP8X4),
+                    scales=h_s[first][:].rearrange("p a j -> p (a j)"),
+                    in_=h[:].rearrange("p a n w -> p (a n w)"),
+                )
 
-        def mul(c, how):
-            scaled = live["s", c] = work.tile([P, PACK, P], F32, name="scaled")
-            if how == "S":
-                plain = work.tile([P, PACK, P], F32, name="plain")
-                nc.scalar.copy(plain[:], live["q", c][:])
-                nc.gpsimd.tensor_tensor(scaled[:], plain[:], along(0, c), ALU.mult)
+        def targets(n):
+            first, count, bank = value_banks[n]
+            row_tiles = PACK // count
+            states = slice(first * P, (first + count) * P)
+            shape = [P, row_tiles, count * P]
+            q = psum.tile(shape, F32, name="q", tag="linear_or_value", bufs=LINEAR_BANKS)
+            for i in range(row_tiles):
+                actions = slice((bank * row_tiles + i) * P, (bank * row_tiles + i + 1) * P)
+                mx_sum(
+                    q[:, i, :],
+                    [
+                        (
+                            v2_w[half][:, actions].bitcast(FP8X4),
+                            v2_s[4 * half : P, actions],
+                            h_w[first][:, half].bitcast(FP8X4),
+                            h_s[first][:, half],
+                        )
+                        for half in (1, 0)
+                    ],
+                )
+            factor = live["rows"][:, 0, states].unsqueeze(1).to_broadcast(shape)
+            offset = live["rows"][:, 1, states].unsqueeze(1).to_broadcast(shape)
+            scaled = work.tile(shape, F32, name="scaled")
+            if EPILOGUE[n][0] == "S":
+                plain = work.tile(shape, F32, name="plain")
+                nc.scalar.copy(plain[:], q[:])
+                nc.gpsimd.tensor_tensor(scaled[:], plain[:], factor, ALU.mult)
             else:
-                nc.vector.tensor_tensor(scaled[:], live["q", c][:], along(0, c), ALU.mult)
+                nc.vector.tensor_tensor(scaled[:], q[:], factor, ALU.mult)
+            result = work.tile(shape, F32, name="result")
+            adder = nc.gpsimd if EPILOGUE[n][1] == "G" else nc.vector
+            adder.tensor_tensor(result[:], scaled[:], offset, ALU.add)
+            rows = out[bank * row_tiles * P : (bank + 1) * row_tiles * P, states]
+            nc.sync.dma_start(out=rows.rearrange("(i p) j -> p i j", p=P), in_=result[:])
 
-        def add(c, how):
-            res = work.tile([P, PACK, P], F32, name="res")
-            engine = nc.gpsimd if how == "G" else nc.vector
-            engine.tensor_tensor(res[:], live["s", c][:], along(1, c), ALU.add)
-            nc.sync.dma_start(out=out[:, c * P : (c + 1) * P].rearrange("(i p) j -> p i j", p=P), in_=res[:])
-
-        def emit(c, how):
-            res = work.tile([P, PACK, P], F32, name="res")
-            if how == "S":
-                nc.scalar.copy(res[:], live["k", c][:])
-            else:
-                nc.vector.tensor_copy(res[:], live["k", c][:])
-            nc.sync.dma_start(out=out[:, c * P : (c + 1) * P].rearrange("(i p) j -> p i j", p=P), in_=res[:])
-
-        perm_w(0)
-        perm_w(1)
-        coefs()
-        load_w1(0)
-        gather_v(0, 1)
-        gather_v(0, 0)
-        perm_s(0)
-        perm_s(1)
-        load_w1(1)
-        load_tab2_scales()
-        gather_v(1, 0)
-        mmb(0, 0, 2)
-        mmb(0, 0, 3)
-        mmb(0, 0, 1)
-        gather_v(1, 1)
-        mmb(0, 1, 0)
-        p1(0, 0, 2)
-        cast(0, 0, 0)
-        p1(0, 0, 3)
-        cast(0, 0, 1)
-        p2(0, 0, 2)
-        p2(0, 0, 3)
-        p1(0, 0, 1)
-        load_tab2()
-        p1(0, 1, 0)
-        qw(0, 0)
-        cast(0, 1, 0)
-        p3(0, 0, 2)
-        p3(0, 0, 3)
-        mmb(1, 0, 3)
-        p2(0, 1, 0)
-        cast(1, 0, 0)
-        mmb(1, 0, 0)
-        p1(1, 0, 3)
-        cast(1, 0, 1)
-        p1(1, 0, 0)
-        p3(0, 1, 0)
-        p2(1, 0, 3)
-        qw(1, 0)
-        p2(1, 0, 0)
-        mmb(0, 0, 0)
-        p3(1, 0, 3)
-        cast(0, 1, 1)
-        p3(1, 0, 0)
-        mmb(0, 1, 1)
-        gather_v2_scales()
-        p2(0, 0, 1)
-        mmb(1, 0, 1)
-        spread()
-        p1(0, 0, 0)
-        qw(0, 1)
-        cast(1, 1, 0)
-        p3(0, 0, 1)
-        mma(0, 2)
-        gather_v2(1)
-        mma(0, 3)
-        p2(0, 0, 0)
-        turn()
-        cast(1, 1, 1)
-        gather_v2(0)
-        mma(0, 0)
-        mma(0, 1)
-        p3(0, 0, 0)
-        p1(0, 1, 1)
-        qw(1, 1)
-        p1(1, 0, 1)
-        mmb(1, 0, 2)
-        p4(0, 2, 2, 2, 'V')
-        p2(0, 1, 1)
-        p4(0, 3, 2, 2, 'V')
-        p2(1, 0, 1)
-        mma(1, 0)
-        p3(0, 1, 1)
-        p1(1, 0, 2)
-        mma(1, 1)
-        qh(0, 2, 2)
-        p3(1, 0, 1)
-        mmb(0, 1, 2)
-        p2(1, 0, 2)
-        p4(0, 0, 0, 2, 'V')
-        mmb(0, 1, 3)
-        p4(0, 1, 0, 2, 'V')
-        p1(0, 1, 2)
-        mma(0, 4)
-        p3(1, 0, 2)
-        p2(0, 1, 2)
-        qh(0, 0, 2)
-        mmb(1, 1, 1)
-        p4(1, 0, 0, 2, 'V')
-        p1(0, 1, 3)
-        mma(1, 2)
-        p4(1, 1, 0, 2, 'V')
-        p1(1, 1, 1)
-        p3(0, 1, 2)
-        mma(1, 3)
-        p2(0, 1, 3)
-        qh(1, 0, 2)
-        mmb(1, 1, 2)
-        p2(1, 1, 1)
-        p4(0, 4, 4, 1, 'V')
-        mmd(0)
-        p3(0, 1, 3)
-        mmd(1)
-        qh(0, 4, 1)
-        mul(0, 'S')
-        p3(1, 1, 1)
-        p4(1, 2, 2, 2, 'V')
-        mmb(1, 1, 0)
-        mma(0, 7)
-        p1(1, 1, 2)
-        p4(1, 3, 2, 2, 'V')
-        mul(1, 'V')
-        p2(1, 1, 2)
-        mmb(1, 1, 3)
-        qh(1, 2, 2)
-        p1(1, 1, 0)
-        add(0, 'G')
-        p4(0, 7, 7, 1, 'V')
-        mma(1, 4)
-        mmd(2)
-        p1(1, 1, 3)
-        p3(1, 1, 2)
-        mmq(3)
-        p2(1, 1, 0)
-        qh(0, 7, 1)
-        add(1, 'G')
-        mul(2, 'S')
-        p3(1, 1, 0)
-        mma(0, 5)
-        act(3)
-        p2(1, 1, 3)
-        p4(1, 4, 4, 1, 'V')
-        mma(1, 5)
-        tr(3)
-        p4(0, 5, 5, 1, 'V')
-        p3(1, 1, 3)
-        emit(3, 'S')
-        mma(0, 6)
-        add(2, 'G')
-        mma(1, 6)
-        qh(1, 4, 1)
-        mma(1, 7)
-        qh(0, 5, 1)
-        p4(1, 5, 5, 1, 'V')
-        p4(0, 6, 6, 1, 'V')
-        mmq(4)
-        qh(1, 5, 1)
-        p4(1, 6, 6, 1, 'V')
-        mmd(5)
-        act(4)
-        qh(0, 6, 1)
-        p4(1, 7, 7, 1, 'V')
-        tr(4)
-        qh(1, 6, 1)
-        mul(5, 'V')
-        mmd(6)
-        qh(1, 7, 1)
-        emit(4, 'V')
-        add(5, 'G')
-        mmd(7)
-        mul(6, 'V')
-        mul(7, 'V')
-        add(6, 'V')
-        add(7, 'V')
+        steps = {
+            "v": last_state_gather,
+            "s": gather_action_scales,
+            "w": gather_action_words,
+            "b": load_rows,
+            "c": cast_w1,
+            "q": quantise_w1,
+            "g": gate,
+            "h": hidden,
+            "t": targets,
+        }
+        taken = {letter: 0 for letter in steps}
+        for letter in SCHEDULE:
+            steps[letter](taken[letter])
+            taken[letter] += 1

@@ -1,6 +1,7 @@
 from contextlib import ExitStack
 
 import concourse.mybir as mybir
+from concourse.masks import make_identity
 
 K, H, T, S, T2, S2 = 1024, 1024, 4096, 1024, 1024, 512
 FLOPS = 2 * K * H * S * 2 + 2 * H * S2 * S
@@ -22,15 +23,11 @@ PASS = P * PACK
 PASSES = K // PASS
 LIST_ROWS = 16
 
-GATE_BANKS = 4
-LINEAR_BANKS = 4
+GATE_BANKS = 3
+LINEAR_BANKS = 3
+TURN_BANKS = 2
 
-GATE_ORDER = [(half, n) for part in range(2) for half in range(2) for n in range(4 * part, 4 * part + 4)]
-HIDDEN_ORDER = [(half, n) for part in range(2) for half in range(2) for n in range(4 * part, 4 * part + 4)]
-RUNS = [(0, 2), (2, 2), (4, 1), (5, 1), (6, 1), (7, 1)]
-CAST_ENGINES = "VVVSSVSS"
-EPILOGUE = ["SG", "SG", "VG", "VG", "VG", "VV", "VV", "VV"]
-SCHEDULE = "cvcgggcgcgqwqcccsgwqhcgqbhgghhgghhhhgttgghhtgghhhthhhtttt"
+QUADS = [(half, part) for half in range(2) for part in range(2)]
 
 
 def tile_list_replay_action_targets_kernel(
@@ -60,12 +57,6 @@ def tile_list_replay_action_targets_kernel(
                     stop=(n == len(operands) - 1),
                 )
 
-        def load_both_planes(dst, src):
-            for quad in range(4):
-                nc.sync.dma_start(
-                    out=dst[32 * quad : 32 * quad + 8, :], in_=src.bitcast(I32)[:, 4 * quad : 4 * quad + 4, :]
-                )
-
         def load_w1(dst, half):
             for a in range(PASSES):
                 rows = w1[a * PASS : (a + 1) * PASS, half * PASS : (half + 1) * PASS]
@@ -78,18 +69,21 @@ def tile_list_replay_action_targets_kernel(
         w4_raw_s = held([P, PASSES, H // 4], I32, "w4_raw_s")
         v_s1 = queued([P, S // 4], I32, "v_s1")
         tab_w = [queued([P, T], I32, f"tab_w{a}") for a in range(PASSES)]
-        warm = held([P, 2], F32, "warm")
+        identity = held([P, P], F32, "identity")
+        per_state = held([P, 2 * S // P], F32, "per_state")
 
         nc.vector.memset(tab_s[:], 0)
         nc.vector.memset(w4_raw_s[:], 0)
         nc.vector.memset(v_s1[:], 0)
-        nc.gpsimd.memset(warm[:, 0:1], 0.0)
-        nc.scalar.activation(warm[:, 1:2], warm[:, 0:1], ACT.Exp)
+        make_identity(nc, identity[:])
 
         nc.sync.dma_start(idx[:], offs)
-        nc.sync.dma_start(idx2[:], offs2)
         nc.sync.dma_start(out=w4_raw[:], in_=w4_words.bitcast(I32).rearrange("a p c -> p a c"))
-        load_both_planes(tab_s, tab_scales)
+        nc.sync.dma_start(idx2[:], offs2)
+        for quad in range(4):
+            nc.sync.dma_start(
+                out=tab_s[32 * quad : 32 * quad + 8, :], in_=tab_scales.bitcast(I32)[:, 4 * quad : 4 * quad + 4, :]
+            )
         nc.sync.dma_start(out=tab_w[0][:], in_=tab_words[0].rearrange("p t i -> p (t i)").bitcast(I32))
         for quad in range(4):
             nc.sync.dma_start(
@@ -125,65 +119,40 @@ def tile_list_replay_action_targets_kernel(
             regroup(w4_w[half][:].bitcast(U16), w4_raw[:].bitcast(U16), half)
         w1_raw = [held([P, PASSES, PACK, PASS], F32, "w1_raw0", "stage")]
         load_w1(w1_raw[0], 0)
-        gather_states(0, 0)
         for half in range(2):
             regroup(w4_s[half][:], w4_raw_s[:].bitcast(U8), half)
+        gather_states(0, 0)
         gather_states(0, 1)
         w1_raw.append(queued([P, PASSES, PACK, PASS], F32, "w1_raw1"))
         load_w1(w1_raw[1], 1)
         tab2_s = held([P, T2 // 4], I32, "tab2_s", "w4_raw_s")
-        nc.vector.memset(tab2_s[:], 0)
-        load_both_planes(tab2_s, tab2_scales)
-        gather_states(1, 0)
+        nc.gpsimd.memset(tab2_s[:], 0)
+        for quad in range(4):
+            nc.sync.dma_start(
+                out=tab2_s[32 * quad : 32 * quad + 8, :], in_=tab2_scales.bitcast(I32)[:, 4 * quad : 4 * quad + 4, :]
+            )
 
         w1_w = [[held([P, PASS], U32, f"w1_w{half}{a}") for a in range(PASSES)] for half in range(2)]
         w1_s = [[held([P, PASS], U8, f"w1_s{half}{a}") for a in range(PASSES)] for half in range(2)]
+        grouped = [[held([P, PACK * PASS], BF16, f"grouped{half}{a}") for a in range(PASSES)] for half in range(2)]
         v2_s = held([P, S2], U8, "v2_s")
         v2_w = [held([P, S2], U32, f"v2_w{half}") for half in range(2)]
-        elu = [[held([P, PACK, PASS], F32, f"elu{half}{part}") for part in range(2)] for half in range(2)]
-        h_w = {first: held([P, 2, count * P], U32, f"h_w{first}") for first, count in RUNS}
-        h_s = {first: held([P, 2, count * P], U8, f"h_s{first}") for first, count in RUNS}
-        run_of = {chunk: run for run in RUNS for chunk in range(run[0], run[0] + run[1])}
-        value_banks = [(first, count, bank) for first, count in RUNS for bank in range(count)]
-        live = {}
-        tiles_done = {first: 0 for first, count in RUNS}
+        elu = {quad: held([P, PACK, PASS], F32, f"elu{quad[0]}{quad[1]}") for quad in QUADS}
+        h = {quad: held([P, PACK * PASS], BF16, f"h{quad[0]}{quad[1]}") for quad in QUADS}
+        h_w = {quad: held([P, PASS], U32, f"h_w{quad[0]}{quad[1]}") for quad in QUADS}
+        h_s = {quad: held([P, PASS], U8, f"h_s{quad[0]}{quad[1]}") for quad in QUADS}
 
-        def last_state_gather(n):
-            gather_states(1, 1)
-            live["tab2_w"] = queued([P, 2, T2], I32, "tab2_w")
-            nc.sync.dma_start(out=live["tab2_w"][:], in_=tab2_words.rearrange("a p t i -> p a (t i)").bitcast(I32))
-
-        def gather_action_scales(n):
-            nc.vector.tensor_copy(v2_s[:], tab2_s[:].bitcast(U8).indirect(idx2[:]))
-
-        def gather_action_words(half):
-            nc.vector.tensor_copy(v2_w[half][:], live["tab2_w"][:, half, :].bitcast(U32).indirect(idx2[:]))
-
-        def load_rows(n):
-            live["rows"] = held([P, 2, S], F32, "rows", "stage")
-            nc.sync.dma_start(out=live["rows"][:, 0, :], in_=discount.partition_broadcast(P))
-            nc.sync.dma_start(out=live["rows"][:, 1, :], in_=reward.partition_broadcast(P))
-
-        def cast_w1(n):
-            half, a, u = n // 4, n // 2 % 2, n % 2
-            if u == 0:
-                live["grouped", half, a] = work.tile([P, PACK * PASS], BF16, name="grouped", align_bytes=64)
+        def cast_w1(half, a, u, copy):
             src = w1_raw[half][:, a].rearrange("p i (m u e) -> p u m i e", u=2, e=2)[:, u]
-            dst = live["grouped", half, a][:].rearrange("p (u e m i) -> p u m i e", u=2, e=2, i=PACK)[:, u]
-            if CAST_ENGINES[n] == "V":
-                nc.vector.tensor_copy(dst, src)
-            else:
-                nc.scalar.copy(dst, src)
+            dst = grouped[half][a][:].rearrange("p (u e m i) -> p u m i e", u=2, e=2, i=PACK)[:, u]
+            copy(dst, src)
 
-        def quantise_w1(n):
-            half, a = n // 2, n % 2
-            nc.vector.quantize_mx(
-                out=w1_w[half][a][:].bitcast(FP8X4), scales=w1_s[half][a][:], in_=live["grouped", half, a][:]
-            )
+        def quantise_w1(half, a):
+            nc.vector.quantize_mx(out=w1_w[half][a][:].bitcast(FP8X4), scales=w1_s[half][a][:], in_=grouped[half][a][:])
 
         def gate(n):
-            half, tile = GATE_ORDER[n]
-            part, t = tile // PACK, tile % PACK
+            half, part = QUADS[n // PACK]
+            t = n % PACK
             states = slice(part * PASS, (part + 1) * PASS)
             b = psum.tile([P, PASS], F32, name="b", tag="gate", bufs=GATE_BANKS)
             mx_sum(
@@ -202,13 +171,13 @@ def tile_list_replay_action_targets_kernel(
             grown = work.tile([P, PASS], F32, name="grown")
             nc.scalar.activation(clamped[:], b[:], ACT.Relu, scale=-1.0)
             nc.scalar.activation(grown[:], clamped[:], ACT.Exp, scale=-1.0)
-            nc.vector.scalar_tensor_tensor(elu[half][part][:, t, :], grown[:], -1.0, b[:], ALU.add, ALU.max)
+            nc.vector.scalar_tensor_tensor(elu[half, part][:, t, :], grown[:], -1.0, b[:], ALU.add, ALU.max)
 
         def hidden(n):
-            half, chunk = HIDDEN_ORDER[n]
-            first, count = run_of[chunk]
-            states = slice(chunk * P, (chunk + 1) * P)
-            acc = psum.tile([P, PACK, P], F32, name="acc", tag="linear_or_value", bufs=LINEAR_BANKS)
+            half, part = QUADS[n // PACK]
+            in_part = n % PACK
+            states = slice(part * PASS + in_part * P, part * PASS + (in_part + 1) * P)
+            acc = psum.tile([P, PACK, P], F32, name="acc", tag="linear", bufs=LINEAR_BANKS)
             for t in range(PACK):
                 mx_sum(
                     acc[:, t, :],
@@ -222,71 +191,97 @@ def tile_list_replay_action_targets_kernel(
                         for a in (1, 0)
                     ],
                 )
-            if tiles_done[first] == 0:
-                live["h", first] = work.tile([P, 2, count, PASS], BF16, name="h", bufs=len(RUNS), align_bytes=64)
-            h = live["h", first]
-            in_part = chunk % PACK
             nc.vector.tensor_tensor(
-                h[:, half, chunk - first, :].rearrange("p (c e t) -> p c t e", e=2, t=PACK),
+                h[half, part][:, in_part * PASS : (in_part + 1) * PASS].rearrange("p (c e t) -> p c t e", e=2, t=PACK),
                 acc[:].rearrange("p t (c e) -> p c t e", e=2),
-                elu[half][chunk // PACK][:, :, in_part * P : (in_part + 1) * P].rearrange("p t (c e) -> p c t e", e=2),
+                elu[half, part][:, :, in_part * P : (in_part + 1) * P].rearrange("p t (c e) -> p c t e", e=2),
                 ALU.mult,
             )
-            tiles_done[first] += 1
-            if tiles_done[first] == 2 * count:
-                nc.vector.quantize_mx(
-                    out=h_w[first][:].rearrange("p a j -> p (a j)").bitcast(FP8X4),
-                    scales=h_s[first][:].rearrange("p a j -> p (a j)"),
-                    in_=h[:].rearrange("p a n w -> p (a n w)"),
-                )
 
-        def targets(n):
-            first, count, bank = value_banks[n]
-            row_tiles = PACK // count
-            states = slice(first * P, (first + count) * P)
-            shape = [P, row_tiles, count * P]
-            q = psum.tile(shape, F32, name="q", tag="linear_or_value", bufs=LINEAR_BANKS)
-            for i in range(row_tiles):
-                actions = slice((bank * row_tiles + i) * P, (bank * row_tiles + i + 1) * P)
-                mx_sum(
-                    q[:, i, :],
-                    [
-                        (
-                            v2_w[half][:, actions].bitcast(FP8X4),
-                            v2_s[4 * half : P, actions],
-                            h_w[first][:, half].bitcast(FP8X4),
-                            h_s[first][:, half],
-                        )
-                        for half in (1, 0)
-                    ],
-                )
-            factor = live["rows"][:, 0, states].unsqueeze(1).to_broadcast(shape)
-            offset = live["rows"][:, 1, states].unsqueeze(1).to_broadcast(shape)
-            scaled = work.tile(shape, F32, name="scaled")
-            if EPILOGUE[n][0] == "S":
-                plain = work.tile(shape, F32, name="plain")
-                nc.scalar.copy(plain[:], q[:])
-                nc.gpsimd.tensor_tensor(scaled[:], plain[:], factor, ALU.mult)
-            else:
-                nc.vector.tensor_tensor(scaled[:], q[:], factor, ALU.mult)
-            result = work.tile(shape, F32, name="result")
-            adder = nc.gpsimd if EPILOGUE[n][1] == "G" else nc.vector
-            adder.tensor_tensor(result[:], scaled[:], offset, ALU.add)
-            rows = out[bank * row_tiles * P : (bank + 1) * row_tiles * P, states]
-            nc.sync.dma_start(out=rows.rearrange("(i p) j -> p i j", p=P), in_=result[:])
+        def quantise_h(quad, first, count):
+            nc.vector.quantize_mx(
+                out=h_w[quad][:, first * P : (first + count) * P].bitcast(FP8X4),
+                scales=h_s[quad][:, first * P : (first + count) * P],
+                in_=h[quad][:, first * PASS : (first + count) * PASS],
+            )
 
-        steps = {
-            "v": last_state_gather,
-            "s": gather_action_scales,
-            "w": gather_action_words,
-            "b": load_rows,
-            "c": cast_w1,
-            "q": quantise_w1,
-            "g": gate,
-            "h": hidden,
-            "t": targets,
-        }
-        taken = {letter: 0 for letter in steps}
-        for letter in SCHEDULE:
-            steps[letter](taken[letter])
-            taken[letter] += 1
+        def targets(chunk):
+            part, in_part = chunk // PACK, chunk % PACK
+            states = slice(in_part * P, (in_part + 1) * P)
+            q = psum.tile([P, S2], F32, name="q", tag="gate", bufs=GATE_BANKS)
+            mx_sum(
+                q[:],
+                [
+                    (
+                        h_w[half, part][:, states].bitcast(FP8X4),
+                        h_s[half, part][:, states],
+                        v2_w[half][:].bitcast(FP8X4),
+                        v2_s[4 * half : P, :],
+                    )
+                    for half in (1, 0)
+                ],
+            )
+            scaled[chunk] = work.tile([P, S2], F32, name="scaled")
+            nc.scalar.activation(
+                scaled[chunk][:],
+                q[:],
+                ACT.Identity,
+                bias=per_state[:, chunks + chunk : chunks + chunk + 1],
+                scale=per_state[:, chunk : chunk + 1],
+            )
+
+        def store(chunk, copy):
+            turned = psum.tile([P, PACK, P], F32, name="turned", tag="turned", bufs=TURN_BANKS)
+            for i in range(PACK):
+                nc.tensor.transpose(turned[:, i, :], scaled[chunk][:, i * P : (i + 1) * P], identity[:])
+            result = work.tile([P, PACK, P], F32, name="result")
+            copy(result[:], turned[:])
+            columns = out[:, chunk * P : (chunk + 1) * P]
+            nc.sync.dma_start(out=columns.rearrange("(i p) j -> p i j", p=P), in_=result[:])
+
+        chunks = S // P
+        scaled = {}
+        on_vector, on_scalar = nc.vector.tensor_copy, nc.scalar.copy
+        gather_states(1, 0)
+        gate(0)
+        gather_states(1, 1)
+        tab2_w = queued([P, 2, T2], I32, "tab2_w")
+        nc.sync.dma_start(out=tab2_w[:], in_=tab2_words.rearrange("a p t i -> p a (t i)").bitcast(I32))
+        for a in range(PASSES):
+            cast_w1(0, a, 0, on_vector)
+            gate(1 + a)
+            cast_w1(0, a, 1, on_vector)
+            quantise_w1(0, a)
+        gate(3)
+        for n in range(PACK, 4 * PACK):
+            gate(n)
+            hidden(n - PACK)
+            if n >= 3 * PACK:
+                if n % 2 == 1:
+                    quantise_h(QUADS[2], n % PACK - 1, 2)
+            elif n % PACK == PACK - 1:
+                quantise_h(QUADS[n // PACK - 1], 0, PACK)
+            if 6 <= n < 10:
+                cast_w1(1, (n - 6) // 2, n % 2, on_scalar)
+                if n % 2 == 1:
+                    quantise_w1(1, (n - 6) // 2)
+            if n == 5:
+                nc.vector.tensor_copy(v2_s[:], tab2_s[:].bitcast(U8).indirect(idx2[:]))
+                rows = held([P, P], F32, "rows", "w4_raw_s")
+                nc.gpsimd.memset(rows[:], 0.0)
+                nc.sync.dma_start(out=rows[0:chunks, :], in_=discount.rearrange("(c p) -> c p", p=P))
+                nc.sync.dma_start(out=rows[chunks : 2 * chunks, :], in_=reward.rearrange("(c p) -> c p", p=P))
+                turned_rows = psum.tile([P, PACK, P], F32, name="turned", tag="turned", bufs=TURN_BANKS)
+                nc.tensor.transpose(turned_rows[:, 0, :], rows[:], identity[:])
+                nc.scalar.copy(per_state[:], turned_rows[:, 0, 0 : 2 * chunks])
+
+            if n in (10, 11):
+                nc.vector.tensor_copy(v2_w[n - 10][:], tab2_w[:, n - 10, :].bitcast(U32).indirect(idx2[:]))
+        for chunk in range(chunks):
+            if chunk < PACK:
+                hidden(3 * PACK + chunk)
+                quantise_h(QUADS[3], chunk, 1)
+            targets(chunk)
+            if chunk > 0:
+                store(chunk - 1, on_scalar if chunk < PACK else on_vector)
+        store(chunks - 1, on_vector)

@@ -23,9 +23,7 @@ PASS = P * PACK
 PASSES = K // PASS
 LIST_ROWS = 16
 
-GATE_BANKS = 3
-LINEAR_BANKS = 3
-TURN_BANKS = 2
+RING_BANKS = 4
 
 QUADS = [(half, part) for half in range(2) for part in range(2)]
 
@@ -42,8 +40,8 @@ def tile_list_replay_action_targets_kernel(
         def held(shape, dtype, name, tag=None):
             return keep.tile(shape, dtype, name=name, tag=tag or name, align_bytes=64)
 
-        def queued(shape, dtype, name):
-            return keep.tile(shape, dtype, name=name, tag="queued", bufs=3, align_bytes=64)
+        def queued(shape, dtype, name, ring):
+            return keep.tile(shape, dtype, name=name, tag=ring, bufs=2, align_bytes=64)
 
         def mx_sum(acc, operands):
             for n, (lhs, lhs_scale, rhs, rhs_scale) in enumerate(operands):
@@ -62,43 +60,51 @@ def tile_list_replay_action_targets_kernel(
                 rows = w1[a * PASS : (a + 1) * PASS, half * PASS : (half + 1) * PASS]
                 nc.sync.dma_start(out=dst[:, a], in_=rows.rearrange("(p i) c -> p i c", i=PACK))
 
+        def place_rows(dst, first, src, a):
+            return [
+                (dst[32 * quad + first : 32 * quad + first + 4, :], src[16 * a + 4 * quad : 16 * a + 4 * quad + 4, :])
+                for quad in range(4)
+            ]
+
         idx = keep.tile([P, S // LIST_ROWS], U16, name="idx")
         idx2 = keep.tile([P, S2 // LIST_ROWS], U16, name="idx2")
-        tab_s = held([P, T // 4], I32, "tab_s", "stage")
-        w4_raw = held([P, PASSES, H // 2], I32, "w4_raw")
+        tab_s = queued([P, T // 4], I32, "tab_s", "early")
+        w4_raw = queued([P, PASSES, H // 2], I32, "w4_raw", "early")
         w4_raw_s = held([P, PASSES, H // 4], I32, "w4_raw_s")
-        v_s1 = queued([P, S // 4], I32, "v_s1")
-        tab_w = [queued([P, T], I32, f"tab_w{a}") for a in range(PASSES)]
+        v_planes = [queued([P, S // 4], I32, "v_s0", "late"), held([P, S // 4], I32, "v_s1")]
+        tab_w = [queued([P, T], I32, "tab_w0", "late"), queued([P, T], I32, "tab_w1", "early")]
+        tab2_s = held([P, T2 // 4], I32, "tab2_s")
         identity = held([P, P], F32, "identity")
         per_state = held([P, 2 * S // P], F32, "per_state")
 
-        nc.vector.memset(tab_s[:], 0)
         nc.vector.memset(w4_raw_s[:], 0)
-        nc.vector.memset(v_s1[:], 0)
+        nc.vector.memset(v_planes[0][:], 0)
+        nc.vector.memset(tab2_s[:], 0)
+        nc.vector.memset(tab_s[32:64, :], 0)
+        nc.vector.memset(tab_s[64:P, :], 0)
+        nc.gpsimd.memset(v_planes[1][:], 0)
         make_identity(nc, identity[:])
 
         nc.sync.dma_start(idx[:], offs)
+        nc.sync.dma_start(out=tab_s[0:32, :], in_=tab_scales.bitcast(I32).rearrange("a q c -> (a q) c"))
         nc.sync.dma_start(out=w4_raw[:], in_=w4_words.bitcast(I32).rearrange("a p c -> p a c"))
         nc.sync.dma_start(idx2[:], offs2)
-        for quad in range(4):
-            nc.sync.dma_start(
-                out=tab_s[32 * quad : 32 * quad + 8, :], in_=tab_scales.bitcast(I32)[:, 4 * quad : 4 * quad + 4, :]
-            )
-        nc.sync.dma_start(out=tab_w[0][:], in_=tab_words[0].rearrange("p t i -> p (t i)").bitcast(I32))
         for quad in range(4):
             nc.sync.dma_start(
                 out=w4_raw_s[32 * quad : 32 * quad + 4, :, :],
                 in_=w4_scales.bitcast(I32)[:, 4 * quad : 4 * quad + 4, :].rearrange("a s c -> s a c"),
             )
-        nc.sync.dma_start(out=tab_w[1][:], in_=tab_words[1].rearrange("p t i -> p (t i)").bitcast(I32))
+        nc.sync.dma_start(out=tab_w[0][:], in_=tab_words[0].rearrange("p t i -> p (t i)").bitcast(I32))
+        nc.sync.dma_start(out=tab2_s[0:32, :], in_=tab2_scales.bitcast(I32).rearrange("a q c -> (a q) c"))
 
-        v_s0 = held([P, S], U8, "v_s0")
-        nc.vector.tensor_copy(v_s0[:], tab_s[:].bitcast(U8).indirect(idx[:]))
-        for quad in range(4):
-            nc.sync.dma_start(
-                out=v_s1[32 * quad : 32 * quad + 4, :], in_=v_s0[:].bitcast(I32)[32 * quad + 4 : 32 * quad + 8, :]
-            )
-        v_s = [v_s0[:], v_s1[:].bitcast(U8)]
+        v_rows = held([P, S], U8, "v_rows")
+        nc.vector.tensor_copy(v_rows[:], tab_s[:].bitcast(U8).indirect(idx[:]))
+        moves = [move for a in range(PASSES) for move in place_rows(v_planes[a], 0, v_rows[:].bitcast(I32), a)]
+        for n, (dst, src) in enumerate(moves):
+            if n == 3:
+                nc.sync.dma_start(out=tab_w[1][:], in_=tab_words[1].rearrange("p t i -> p (t i)").bitcast(I32))
+            nc.sync.dma_start(out=dst, in_=src)
+        v_s = [plane[:].bitcast(U8) for plane in v_planes]
         v_w = [held([P, S], U32, f"v_w{a}") for a in range(PASSES)]
 
         def gather_states(a, part):
@@ -117,25 +123,20 @@ def tile_list_replay_action_targets_kernel(
         w4_s = [held([P, PASSES, PASS], U8, f"w4_s{half}") for half in range(2)]
         for half in range(2):
             regroup(w4_w[half][:].bitcast(U16), w4_raw[:].bitcast(U16), half)
-        w1_raw = [held([P, PASSES, PACK, PASS], F32, "w1_raw0", "stage")]
+        w1_raw = [queued([P, PASSES, PACK, PASS], F32, "w1_raw0", "early")]
         load_w1(w1_raw[0], 0)
         for half in range(2):
             regroup(w4_s[half][:], w4_raw_s[:].bitcast(U8), half)
         gather_states(0, 0)
         gather_states(0, 1)
-        w1_raw.append(queued([P, PASSES, PACK, PASS], F32, "w1_raw1"))
+        w1_raw.append(queued([P, PASSES, PACK, PASS], F32, "w1_raw1", "late"))
         load_w1(w1_raw[1], 1)
-        tab2_s = held([P, T2 // 4], I32, "tab2_s", "w4_raw_s")
-        nc.gpsimd.memset(tab2_s[:], 0)
-        for quad in range(4):
-            nc.sync.dma_start(
-                out=tab2_s[32 * quad : 32 * quad + 8, :], in_=tab2_scales.bitcast(I32)[:, 4 * quad : 4 * quad + 4, :]
-            )
+        v2_rows = held([P, S2], U8, "v2_rows")
+        nc.vector.tensor_copy(v2_rows[:], tab2_s[:].bitcast(U8).indirect(idx2[:]))
 
         w1_w = [[held([P, PASS], U32, f"w1_w{half}{a}") for a in range(PASSES)] for half in range(2)]
         w1_s = [[held([P, PASS], U8, f"w1_s{half}{a}") for a in range(PASSES)] for half in range(2)]
         grouped = [[held([P, PACK * PASS], BF16, f"grouped{half}{a}") for a in range(PASSES)] for half in range(2)]
-        v2_s = held([P, S2], U8, "v2_s")
         v2_w = [held([P, S2], U32, f"v2_w{half}") for half in range(2)]
         elu = {quad: held([P, PACK, PASS], F32, f"elu{quad[0]}{quad[1]}") for quad in QUADS}
         h = {quad: held([P, PACK * PASS], BF16, f"h{quad[0]}{quad[1]}") for quad in QUADS}
@@ -154,7 +155,7 @@ def tile_list_replay_action_targets_kernel(
             half, part = QUADS[n // PACK]
             t = n % PACK
             states = slice(part * PASS, (part + 1) * PASS)
-            b = psum.tile([P, PASS], F32, name="b", tag="gate", bufs=GATE_BANKS)
+            b = psum.tile([P, PASS], F32, name="b", tag="gate_or_value", bufs=3)
             mx_sum(
                 b[:],
                 [
@@ -177,7 +178,7 @@ def tile_list_replay_action_targets_kernel(
             half, part = QUADS[n // PACK]
             in_part = n % PACK
             states = slice(part * PASS + in_part * P, part * PASS + (in_part + 1) * P)
-            acc = psum.tile([P, PACK, P], F32, name="acc", tag="linear", bufs=LINEAR_BANKS)
+            acc = psum.tile([P, PACK, P], F32, name="acc", tag="linear", bufs=3)
             for t in range(PACK):
                 mx_sum(
                     acc[:, t, :],
@@ -208,7 +209,7 @@ def tile_list_replay_action_targets_kernel(
         def targets(chunk):
             part, in_part = chunk // PACK, chunk % PACK
             states = slice(in_part * P, (in_part + 1) * P)
-            q = psum.tile([P, S2], F32, name="q", tag="gate", bufs=GATE_BANKS)
+            q = psum.tile([P, S2], F32, name="q", tag="gate_or_value", bufs=3)
             mx_sum(
                 q[:],
                 [
@@ -221,23 +222,27 @@ def tile_list_replay_action_targets_kernel(
                     for half in (1, 0)
                 ],
             )
-            scaled[chunk] = work.tile([P, S2], F32, name="scaled")
-            nc.scalar.activation(
-                scaled[chunk][:],
-                q[:],
-                ACT.Identity,
-                bias=per_state[:, chunks + chunk : chunks + chunk + 1],
-                scale=per_state[:, chunk : chunk + 1],
-            )
+            scaled[chunk] = work.tile([P, S2], F32, name="scaled", bufs=6)
+            factor = per_state[:, chunk : chunk + 1]
+            offset = per_state[:, chunks + chunk : chunks + chunk + 1]
+            if part == 1 and chunk % 2 == 1:
+                nc.vector.tensor_scalar(scaled[chunk][:], q[:], factor, offset, ALU.mult, ALU.add)
+            else:
+                nc.scalar.activation(scaled[chunk][:], q[:], ACT.Identity, bias=offset, scale=factor)
 
-        def store(chunk, copy):
-            turned = psum.tile([P, PACK, P], F32, name="turned", tag="turned", bufs=TURN_BANKS)
-            for i in range(PACK):
-                nc.tensor.transpose(turned[:, i, :], scaled[chunk][:, i * P : (i + 1) * P], identity[:])
-            result = work.tile([P, PACK, P], F32, name="result")
-            copy(result[:], turned[:])
-            columns = out[:, chunk * P : (chunk + 1) * P]
-            nc.sync.dma_start(out=columns.rearrange("(i p) j -> p i j", p=P), in_=result[:])
+        def store(first):
+            for bank in range(2):
+                ring, banks = ("turned", 2) if first % 4 == 0 else ("linear", 3)
+                turned = psum.tile([P, 2, 2, P], F32, name="turned", tag=ring, bufs=banks)
+                for i in range(2):
+                    actions = slice((2 * bank + i) * P, (2 * bank + i + 1) * P)
+                    for e in range(2):
+                        nc.tensor.transpose(turned[:, i, e, :], scaled[first + e][:, actions], identity[:])
+                result = work.tile([P, 2, 2 * P], F32, name="result")
+                copy = on_vector if first > 0 and bank == 1 else on_scalar
+                copy(result[:], turned[:].rearrange("p i e j -> p i (e j)"))
+                block = out[2 * bank * P : 2 * (bank + 1) * P, first * P : (first + 2) * P]
+                nc.sync.dma_start(out=block.rearrange("(i p) j -> p i j", p=P), in_=result[:])
 
         chunks = S // P
         scaled = {}
@@ -245,8 +250,14 @@ def tile_list_replay_action_targets_kernel(
         gather_states(1, 0)
         gate(0)
         gather_states(1, 1)
-        tab2_w = queued([P, 2, T2], I32, "tab2_w")
+        tab2_w = queued([P, 2, T2], I32, "tab2_w", "early")
         nc.sync.dma_start(out=tab2_w[:], in_=tab2_words.rearrange("a p t i -> p a (t i)").bitcast(I32))
+        v2_plane = queued([P, S2 // 4], I32, "v2_s", "early")
+        nc.gpsimd.memset(v2_plane[:], 0)
+        for a in range(PASSES):
+            for dst, src in place_rows(v2_plane, 4 * a, v2_rows[:].bitcast(I32), a):
+                nc.sync.dma_start(out=dst, in_=src)
+        v2_s = v2_plane[:].bitcast(U8)
         for a in range(PASSES):
             cast_w1(0, a, 0, on_vector)
             gate(1 + a)
@@ -265,23 +276,25 @@ def tile_list_replay_action_targets_kernel(
                 cast_w1(1, (n - 6) // 2, n % 2, on_scalar)
                 if n % 2 == 1:
                     quantise_w1(1, (n - 6) // 2)
-            if n == 5:
-                nc.vector.tensor_copy(v2_s[:], tab2_s[:].bitcast(U8).indirect(idx2[:]))
-                rows = held([P, P], F32, "rows", "w4_raw_s")
+            if n == 10:
+                rows = queued([P, P], F32, "rows", "late")
                 nc.gpsimd.memset(rows[:], 0.0)
                 nc.sync.dma_start(out=rows[0:chunks, :], in_=discount.rearrange("(c p) -> c p", p=P))
                 nc.sync.dma_start(out=rows[chunks : 2 * chunks, :], in_=reward.rearrange("(c p) -> c p", p=P))
-                turned_rows = psum.tile([P, PACK, P], F32, name="turned", tag="turned", bufs=TURN_BANKS)
+                turned_rows = psum.tile([P, PACK, P], F32, name="turned", tag="turned", bufs=2)
                 nc.tensor.transpose(turned_rows[:, 0, :], rows[:], identity[:])
                 nc.scalar.copy(per_state[:], turned_rows[:, 0, 0 : 2 * chunks])
 
-            if n in (10, 11):
-                nc.vector.tensor_copy(v2_w[n - 10][:], tab2_w[:, n - 10, :].bitcast(U32).indirect(idx2[:]))
-        for chunk in range(chunks):
-            if chunk < PACK:
-                hidden(3 * PACK + chunk)
-                quantise_h(QUADS[3], chunk, 1)
+            if n in (9, 11):
+                nc.vector.tensor_copy(v2_w[n // 11][:], tab2_w[:, n // 11, :].bitcast(U32).indirect(idx2[:]))
+        for first in range(0, PACK, 2):
+            targets(first)
+            targets(first + 1)
+            for in_part in (first, first + 1):
+                hidden(3 * PACK + in_part)
+                quantise_h(QUADS[3], in_part, 1)
+            store(first)
+        for chunk in range(PACK, chunks):
             targets(chunk)
-            if chunk > 0:
-                store(chunk - 1, on_scalar if chunk < PACK else on_vector)
-        store(chunks - 1, on_vector)
+        for first in range(PACK, chunks, 2):
+            store(first)

@@ -69,7 +69,7 @@ def tile_list_replay_action_targets_kernel(
         idx = keep.tile([P, S // LIST_ROWS], U16, name="idx")
         idx2 = keep.tile([P, S2 // LIST_ROWS], U16, name="idx2")
         tab_s = queued([P, T // 4], I32, "tab_s", "early")
-        w4_raw = queued([P, PASSES, H // 2], I32, "w4_raw", "early")
+        w4_raw = [queued([P, PASSES, PASS // 2], I32, "w4_raw0", "early")]
         w4_raw_s = held([P, PASSES, H // 4], I32, "w4_raw_s")
         v_planes = [queued([P, S // 4], I32, "v_s0", "late"), held([P, S // 4], I32, "v_s1")]
         tab_w = [queued([P, T], I32, "tab_w0", "late"), queued([P, T], I32, "tab_w1", "early")]
@@ -87,7 +87,8 @@ def tile_list_replay_action_targets_kernel(
 
         nc.sync.dma_start(idx[:], offs)
         nc.sync.dma_start(out=tab_s[0:32, :], in_=tab_scales.bitcast(I32).rearrange("a q c -> (a q) c"))
-        nc.sync.dma_start(out=w4_raw[:], in_=w4_words.bitcast(I32).rearrange("a p c -> p a c"))
+        w4_rows = w4_words.bitcast(I32).rearrange("a p (h c) -> h p a c", h=2)
+        nc.sync.dma_start(out=w4_raw[0][:], in_=w4_rows[0])
         nc.sync.dma_start(idx2[:], offs2)
         for quad in range(4):
             nc.sync.dma_start(
@@ -113,20 +114,21 @@ def tile_list_replay_action_targets_kernel(
                 v_w[a][:, part * PASS : (part + 1) * PASS], tab_w[a][:].bitcast(U32).indirect(entries)
             )
 
-        def regroup(dst, src, half):
+        def regroup(dst, src):
             nc.vector.tensor_copy(
                 dst.rearrange("p a (t m) -> p a t m", t=PACK),
-                src[:, :, half * PASS : (half + 1) * PASS].rearrange("p a (m t) -> p a t m", t=PACK),
+                src.rearrange("p a (m t) -> p a t m", t=PACK),
             )
 
         w4_w = [held([P, PASSES, 2 * PASS], U8, f"w4_w{half}") for half in range(2)]
         w4_s = [held([P, PASSES, PASS], U8, f"w4_s{half}") for half in range(2)]
-        for half in range(2):
-            regroup(w4_w[half][:].bitcast(U16), w4_raw[:].bitcast(U16), half)
+        regroup(w4_w[0][:].bitcast(U16), w4_raw[0][:].bitcast(U16))
         w1_raw = [queued([P, PASSES, PACK, PASS], F32, "w1_raw0", "early")]
         load_w1(w1_raw[0], 0)
         for half in range(2):
-            regroup(w4_s[half][:], w4_raw_s[:].bitcast(U8), half)
+            regroup(w4_s[half][:], w4_raw_s[:].bitcast(U8)[:, :, half * PASS : (half + 1) * PASS])
+        w4_raw.append(held([P, PASSES, PASS // 2], I32, "w4_raw1", "w4_raw_s"))
+        nc.sync.dma_start(out=w4_raw[1][:], in_=w4_rows[1])
         gather_states(0, 0)
         gather_states(0, 1)
         w1_raw.append(queued([P, PASSES, PACK, PASS], F32, "w1_raw1", "late"))
@@ -225,10 +227,38 @@ def tile_list_replay_action_targets_kernel(
             scaled[chunk] = work.tile([P, S2], F32, name="scaled", bufs=6)
             factor = per_state[:, chunk : chunk + 1]
             offset = per_state[:, chunks + chunk : chunks + chunk + 1]
-            if part == 1 and chunk % 2 == 1:
-                nc.vector.tensor_scalar(scaled[chunk][:], q[:], factor, offset, ALU.mult, ALU.add)
-            else:
-                nc.scalar.activation(scaled[chunk][:], q[:], ACT.Identity, bias=offset, scale=factor)
+            nc.scalar.activation(scaled[chunk][:], q[:], ACT.Identity, bias=offset, scale=factor)
+
+        def targets_in_place(chunk):
+            part, in_part = chunk // PACK, chunk % PACK
+            states = slice(in_part * P, (in_part + 1) * P)
+            shape = [P, PACK, P]
+            q = psum.tile(shape, F32, name="q", tag="gate_or_value", bufs=3)
+            for i in range(PACK):
+                actions = slice(i * P, (i + 1) * P)
+                mx_sum(
+                    q[:, i, :],
+                    [
+                        (
+                            v2_w[half][:, actions].bitcast(FP8X4),
+                            v2_s[4 * half : P, actions],
+                            h_w[half, part][:, states].bitcast(FP8X4),
+                            h_s[half, part][:, states],
+                        )
+                        for half in (0, 1)
+                    ],
+                )
+            last = slice((chunk - turned_chunks) * P, (chunk - turned_chunks + 1) * P)
+            scaled[chunk] = work.tile(shape, F32, name="scaled", bufs=6)
+            nc.vector.tensor_tensor(scaled[chunk][:], q[:], spread[:, 0, last].unsqueeze(1).to_broadcast(shape), ALU.mult)
+
+        def store_in_place(chunk):
+            shape = [P, PACK, P]
+            last = slice((chunk - turned_chunks) * P, (chunk - turned_chunks + 1) * P)
+            result = work.tile(shape, F32, name="result", bufs=8)
+            nc.vector.tensor_tensor(result[:], scaled[chunk][:], spread[:, 1, last].unsqueeze(1).to_broadcast(shape), ALU.add)
+            columns = out[:, chunk * P : (chunk + 1) * P]
+            nc.sync.dma_start(out=columns.rearrange("(i p) j -> p i j", p=P), in_=result[:])
 
         def store(first):
             for bank in range(2):
@@ -238,13 +268,13 @@ def tile_list_replay_action_targets_kernel(
                     actions = slice((2 * bank + i) * P, (2 * bank + i + 1) * P)
                     for e in range(2):
                         nc.tensor.transpose(turned[:, i, e, :], scaled[first + e][:, actions], identity[:])
-                result = work.tile([P, 2, 2 * P], F32, name="result")
-                copy = on_vector if first > 0 and bank == 1 else on_scalar
-                copy(result[:], turned[:].rearrange("p i e j -> p i (e j)"))
+                result = work.tile([P, 2, 2 * P], F32, name="result", bufs=8)
+                nc.scalar.copy(result[:], turned[:].rearrange("p i e j -> p i (e j)"))
                 block = out[2 * bank * P : 2 * (bank + 1) * P, first * P : (first + 2) * P]
                 nc.sync.dma_start(out=block.rearrange("(i p) j -> p i j", p=P), in_=result[:])
 
         chunks = S // P
+        turned_chunks = PACK
         scaled = {}
         on_vector, on_scalar = nc.vector.tensor_copy, nc.scalar.copy
         gather_states(1, 0)
@@ -264,6 +294,7 @@ def tile_list_replay_action_targets_kernel(
             cast_w1(0, a, 1, on_vector)
             quantise_w1(0, a)
         gate(3)
+        regroup(w4_w[1][:].bitcast(U16), w4_raw[1][:].bitcast(U16))
         for n in range(PACK, 4 * PACK):
             gate(n)
             hidden(n - PACK)
@@ -281,6 +312,9 @@ def tile_list_replay_action_targets_kernel(
                 nc.gpsimd.memset(rows[:], 0.0)
                 nc.sync.dma_start(out=rows[0:chunks, :], in_=discount.rearrange("(c p) -> c p", p=P))
                 nc.sync.dma_start(out=rows[chunks : 2 * chunks, :], in_=reward.rearrange("(c p) -> c p", p=P))
+                spread = held([P, 2, PASS], F32, "spread", "grouped01")
+                nc.sync.dma_start(out=spread[:, 0, :], in_=discount[turned_chunks * P :].partition_broadcast(P))
+                nc.sync.dma_start(out=spread[:, 1, :], in_=reward[turned_chunks * P :].partition_broadcast(P))
                 turned_rows = psum.tile([P, PACK, P], F32, name="turned", tag="turned", bufs=2)
                 nc.tensor.transpose(turned_rows[:, 0, :], rows[:], identity[:])
                 nc.scalar.copy(per_state[:], turned_rows[:, 0, 0 : 2 * chunks])
@@ -294,7 +328,8 @@ def tile_list_replay_action_targets_kernel(
                 hidden(3 * PACK + in_part)
                 quantise_h(QUADS[3], in_part, 1)
             store(first)
-        for chunk in range(PACK, chunks):
-            targets(chunk)
-        for first in range(PACK, chunks, 2):
-            store(first)
+        for first in range(turned_chunks, chunks, 2):
+            targets_in_place(first)
+            targets_in_place(first + 1)
+            store_in_place(first)
+            store_in_place(first + 1)

@@ -211,7 +211,8 @@ def tile_list_replay_action_targets_kernel(
         def targets(chunk):
             part, in_part = chunk // PACK, chunk % PACK
             states = slice(in_part * P, (in_part + 1) * P)
-            q = psum.tile([P, S2], F32, name="q", tag="gate_or_value", bufs=3)
+            ring, banks = ("turned", 2) if chunk < 2 else ("gate_or_value", 3)
+            q = psum.tile([P, S2], F32, name="q", tag=ring, bufs=banks)
             mx_sum(
                 q[:],
                 [
@@ -256,7 +257,8 @@ def tile_list_replay_action_targets_kernel(
             shape = [P, PACK, P]
             last = slice((chunk - turned_chunks) * P, (chunk - turned_chunks + 1) * P)
             result = work.tile(shape, F32, name="result", bufs=8)
-            nc.vector.tensor_tensor(result[:], scaled[chunk][:], spread[:, 1, last].unsqueeze(1).to_broadcast(shape), ALU.add)
+            adder = nc.gpsimd if chunk < chunks - 2 else nc.vector
+            adder.tensor_tensor(result[:], scaled[chunk][:], spread[:, 1, last].unsqueeze(1).to_broadcast(shape), ALU.add)
             columns = out[:, chunk * P : (chunk + 1) * P]
             nc.sync.dma_start(out=columns.rearrange("(i p) j -> p i j", p=P), in_=result[:])
 
@@ -296,13 +298,18 @@ def tile_list_replay_action_targets_kernel(
         gate(3)
         regroup(w4_w[1][:].bitcast(U16), w4_raw[1][:].bitcast(U16))
         for n in range(PACK, 4 * PACK):
+            if n in (12, 14):
+                hidden(n - PACK)
+                hidden(n - PACK + 1)
+                quantise_h(QUADS[2], n % PACK, 2)
+            if n == 12:
+                targets(0)
+                targets(1)
             gate(n)
-            hidden(n - PACK)
-            if n >= 3 * PACK:
-                if n % 2 == 1:
-                    quantise_h(QUADS[2], n % PACK - 1, 2)
-            elif n % PACK == PACK - 1:
-                quantise_h(QUADS[n // PACK - 1], 0, PACK)
+            if n < 3 * PACK:
+                hidden(n - PACK)
+                if n % PACK == PACK - 1:
+                    quantise_h(QUADS[n // PACK - 1], 0, PACK)
             if 6 <= n < 10:
                 cast_w1(1, (n - 6) // 2, n % 2, on_scalar)
                 if n % 2 == 1:
@@ -321,15 +328,15 @@ def tile_list_replay_action_targets_kernel(
 
             if n in (9, 11):
                 nc.vector.tensor_copy(v2_w[n // 11][:], tab2_w[:, n // 11, :].bitcast(U32).indirect(idx2[:]))
-        for first in range(0, PACK, 2):
-            targets(first)
-            targets(first + 1)
-            for in_part in (first, first + 1):
-                hidden(3 * PACK + in_part)
-                quantise_h(QUADS[3], in_part, 1)
-            store(first)
-        for first in range(turned_chunks, chunks, 2):
-            targets_in_place(first)
-            targets_in_place(first + 1)
-            store_in_place(first)
-            store_in_place(first + 1)
+        store(0)
+        targets(2)
+        targets(3)
+        for in_part in range(PACK):
+            hidden(3 * PACK + in_part)
+            quantise_h(QUADS[3], in_part, 1)
+        for chunk in range(turned_chunks, chunks):
+            targets_in_place(chunk)
+            if chunk == turned_chunks + 1:
+                store(2)
+        for chunk in range(turned_chunks, chunks):
+            store_in_place(chunk)

@@ -23,9 +23,18 @@ PASS = P * PACK
 PASSES = K // PASS
 LIST_ROWS = 16
 
-RING_BANKS = 4
+QUADRANT = 32
+SCALE_ROWS = 32
+
+GATE_RING = ("gate", 3)
+LINEAR_RING = ("linear", 3)
+SPARE_RING = ("spare", 2)
 
 QUADS = [(half, part) for half in range(2) for part in range(2)]
+FIRST_LATE_CAST = 6
+ROWS_GATE = 10
+ACTION_GATES = (9, 11)
+MOVES_AHEAD = 3
 
 
 def tile_list_replay_action_targets_kernel(
@@ -42,6 +51,9 @@ def tile_list_replay_action_targets_kernel(
 
         def queued(shape, dtype, name, ring):
             return keep.tile(shape, dtype, name=name, tag=ring, bufs=2, align_bytes=64)
+
+        def bank(shape, name, ring):
+            return psum.tile(shape, F32, name=name, tag=ring[0], bufs=ring[1])
 
         def mx_sum(acc, operands):
             for n, (lhs, lhs_scale, rhs, rhs_scale) in enumerate(operands):
@@ -62,8 +74,11 @@ def tile_list_replay_action_targets_kernel(
 
         def place_rows(dst, first, src, a):
             return [
-                (dst[32 * quad + first : 32 * quad + first + 4, :], src[16 * a + 4 * quad : 16 * a + 4 * quad + 4, :])
-                for quad in range(4)
+                (
+                    dst[QUADRANT * quadrant + first : QUADRANT * quadrant + first + 4, :],
+                    src[16 * a + 4 * quadrant : 16 * a + 4 * quadrant + 4, :],
+                )
+                for quadrant in range(4)
             ]
 
         idx = keep.tile([P, S // LIST_ROWS], U16, name="idx")
@@ -75,34 +90,34 @@ def tile_list_replay_action_targets_kernel(
         tab_w = [queued([P, T], I32, "tab_w0", "late"), queued([P, T], I32, "tab_w1", "early")]
         tab2_s = held([P, T2 // 4], I32, "tab2_s")
         identity = held([P, P], F32, "identity")
-        per_state = held([P, 2 * S // P], F32, "per_state")
+        per_state = held([P, 2 * PACK], F32, "per_state")
 
         nc.vector.memset(w4_raw_s[:], 0)
         nc.vector.memset(v_planes[0][:], 0)
         nc.vector.memset(tab2_s[:], 0)
-        nc.vector.memset(tab_s[32:64, :], 0)
-        nc.vector.memset(tab_s[64:P, :], 0)
+        nc.vector.memset(tab_s[SCALE_ROWS : 2 * QUADRANT, :], 0)
+        nc.vector.memset(tab_s[2 * QUADRANT : P, :], 0)
         nc.gpsimd.memset(v_planes[1][:], 0)
         make_identity(nc, identity[:])
 
         nc.sync.dma_start(idx[:], offs)
-        nc.sync.dma_start(out=tab_s[0:32, :], in_=tab_scales.bitcast(I32).rearrange("a q c -> (a q) c"))
+        nc.sync.dma_start(out=tab_s[0:SCALE_ROWS, :], in_=tab_scales.bitcast(I32).rearrange("a q c -> (a q) c"))
         w4_rows = w4_words.bitcast(I32).rearrange("a p (h c) -> h p a c", h=2)
         nc.sync.dma_start(out=w4_raw[0][:], in_=w4_rows[0])
         nc.sync.dma_start(idx2[:], offs2)
-        for quad in range(4):
+        for quadrant in range(4):
             nc.sync.dma_start(
-                out=w4_raw_s[32 * quad : 32 * quad + 4, :, :],
-                in_=w4_scales.bitcast(I32)[:, 4 * quad : 4 * quad + 4, :].rearrange("a s c -> s a c"),
+                out=w4_raw_s[QUADRANT * quadrant : QUADRANT * quadrant + 4, :, :],
+                in_=w4_scales.bitcast(I32)[:, 4 * quadrant : 4 * quadrant + 4, :].rearrange("a s c -> s a c"),
             )
         nc.sync.dma_start(out=tab_w[0][:], in_=tab_words[0].rearrange("p t i -> p (t i)").bitcast(I32))
-        nc.sync.dma_start(out=tab2_s[0:32, :], in_=tab2_scales.bitcast(I32).rearrange("a q c -> (a q) c"))
+        nc.sync.dma_start(out=tab2_s[0:SCALE_ROWS, :], in_=tab2_scales.bitcast(I32).rearrange("a q c -> (a q) c"))
 
         v_rows = held([P, S], U8, "v_rows")
         nc.vector.tensor_copy(v_rows[:], tab_s[:].bitcast(U8).indirect(idx[:]))
         moves = [move for a in range(PASSES) for move in place_rows(v_planes[a], 0, v_rows[:].bitcast(I32), a)]
         for n, (dst, src) in enumerate(moves):
-            if n == 3:
+            if n == MOVES_AHEAD:
                 nc.sync.dma_start(out=tab_w[1][:], in_=tab_words[1].rearrange("p t i -> p (t i)").bitcast(I32))
             nc.sync.dma_start(out=dst, in_=src)
         v_s = [plane[:].bitcast(U8) for plane in v_planes]
@@ -145,19 +160,23 @@ def tile_list_replay_action_targets_kernel(
         h_w = {quad: held([P, PASS], U32, f"h_w{quad[0]}{quad[1]}") for quad in QUADS}
         h_s = {quad: held([P, PASS], U8, f"h_s{quad[0]}{quad[1]}") for quad in QUADS}
 
+        scaled = {}
+
         def cast_w1(half, a, u, copy):
             src = w1_raw[half][:, a].rearrange("p i (m u e) -> p u m i e", u=2, e=2)[:, u]
             dst = grouped[half][a][:].rearrange("p (u e m i) -> p u m i e", u=2, e=2, i=PACK)[:, u]
             copy(dst, src)
 
         def quantise_w1(half, a):
-            nc.vector.quantize_mx(out=w1_w[half][a][:].bitcast(FP8X4), scales=w1_s[half][a][:], in_=grouped[half][a][:])
+            nc.vector.quantize_mx(
+                out=w1_w[half][a][:].bitcast(FP8X4), scales=w1_s[half][a][:], in_=grouped[half][a][:]
+            )
 
         def gate(n):
             half, part = QUADS[n // PACK]
             t = n % PACK
             states = slice(part * PASS, (part + 1) * PASS)
-            b = psum.tile([P, PASS], F32, name="b", tag="gate_or_value", bufs=3)
+            b = bank([P, PASS], "b", GATE_RING)
             mx_sum(
                 b[:],
                 [
@@ -180,7 +199,7 @@ def tile_list_replay_action_targets_kernel(
             half, part = QUADS[n // PACK]
             in_part = n % PACK
             states = slice(part * PASS + in_part * P, part * PASS + (in_part + 1) * P)
-            acc = psum.tile([P, PACK, P], F32, name="acc", tag="linear", bufs=3)
+            acc = bank([P, PACK, P], "acc", LINEAR_RING)
             for t in range(PACK):
                 mx_sum(
                     acc[:, t, :],
@@ -208,17 +227,15 @@ def tile_list_replay_action_targets_kernel(
                 in_=h[quad][:, first * PASS : (first + count) * PASS],
             )
 
-        def targets(chunk):
-            part, in_part = chunk // PACK, chunk % PACK
-            states = slice(in_part * P, (in_part + 1) * P)
-            ring, banks = ("turned", 2) if chunk < 2 else ("gate_or_value", 3)
-            q = psum.tile([P, S2], F32, name="q", tag=ring, bufs=banks)
+        def targets_by_state(chunk):
+            states = slice(chunk * P, (chunk + 1) * P)
+            q = bank([P, S2], "q", SPARE_RING if chunk < 2 else GATE_RING)
             mx_sum(
                 q[:],
                 [
                     (
-                        h_w[half, part][:, states].bitcast(FP8X4),
-                        h_s[half, part][:, states],
+                        h_w[half, 0][:, states].bitcast(FP8X4),
+                        h_s[half, 0][:, states],
                         v2_w[half][:].bitcast(FP8X4),
                         v2_s[4 * half : P, :],
                     )
@@ -227,14 +244,26 @@ def tile_list_replay_action_targets_kernel(
             )
             scaled[chunk] = work.tile([P, S2], F32, name="scaled", bufs=6)
             factor = per_state[:, chunk : chunk + 1]
-            offset = per_state[:, chunks + chunk : chunks + chunk + 1]
+            offset = per_state[:, PACK + chunk : PACK + chunk + 1]
             nc.scalar.activation(scaled[chunk][:], q[:], ACT.Identity, bias=offset, scale=factor)
 
-        def targets_in_place(chunk):
-            part, in_part = chunk // PACK, chunk % PACK
+        def turn_and_store(first, ring):
+            for pair in range(2):
+                turned = bank([P, 2, 2, P], "turned", ring)
+                for i in range(2):
+                    actions = slice((2 * pair + i) * P, (2 * pair + i + 1) * P)
+                    for e in range(2):
+                        nc.tensor.transpose(turned[:, i, e, :], scaled[first + e][:, actions], identity[:])
+                result = work.tile([P, 2, 2 * P], F32, name="result", bufs=8)
+                nc.scalar.copy(result[:], turned[:].rearrange("p i e j -> p i (e j)"))
+                block = out[2 * pair * P : 2 * (pair + 1) * P, first * P : (first + 2) * P]
+                nc.sync.dma_start(out=block.rearrange("(i p) j -> p i j", p=P), in_=result[:])
+
+        by_action = [P, PACK, P]
+
+        def discount_by_action(in_part):
             states = slice(in_part * P, (in_part + 1) * P)
-            shape = [P, PACK, P]
-            q = psum.tile(shape, F32, name="q", tag="gate_or_value", bufs=3)
+            q = bank(by_action, "q", GATE_RING)
             for i in range(PACK):
                 actions = slice(i * P, (i + 1) * P)
                 mx_sum(
@@ -243,42 +272,23 @@ def tile_list_replay_action_targets_kernel(
                         (
                             v2_w[half][:, actions].bitcast(FP8X4),
                             v2_s[4 * half : P, actions],
-                            h_w[half, part][:, states].bitcast(FP8X4),
-                            h_s[half, part][:, states],
+                            h_w[half, 1][:, states].bitcast(FP8X4),
+                            h_s[half, 1][:, states],
                         )
                         for half in (0, 1)
                     ],
                 )
-            last = slice((chunk - turned_chunks) * P, (chunk - turned_chunks + 1) * P)
-            scaled[chunk] = work.tile(shape, F32, name="scaled", bufs=6)
-            nc.vector.tensor_tensor(scaled[chunk][:], q[:], spread[:, 0, last].unsqueeze(1).to_broadcast(shape), ALU.mult)
+            scaled[PACK + in_part] = work.tile(by_action, F32, name="scaled", bufs=6)
+            factor = spread[:, 0, states].unsqueeze(1).to_broadcast(by_action)
+            nc.vector.tensor_tensor(scaled[PACK + in_part][:], q[:], factor, ALU.mult)
 
-        def store_in_place(chunk):
-            shape = [P, PACK, P]
-            last = slice((chunk - turned_chunks) * P, (chunk - turned_chunks + 1) * P)
-            result = work.tile(shape, F32, name="result", bufs=8)
-            adder = nc.gpsimd if chunk < chunks - 2 else nc.vector
-            adder.tensor_tensor(result[:], scaled[chunk][:], spread[:, 1, last].unsqueeze(1).to_broadcast(shape), ALU.add)
-            columns = out[:, chunk * P : (chunk + 1) * P]
+        def reward_and_store(in_part):
+            offset = spread[:, 1, in_part * P : (in_part + 1) * P].unsqueeze(1).to_broadcast(by_action)
+            result = work.tile(by_action, F32, name="result", bufs=8)
+            nc.vector.tensor_tensor(result[:], scaled[PACK + in_part][:], offset, ALU.add)
+            columns = out[:, PASS + in_part * P : PASS + (in_part + 1) * P]
             nc.sync.dma_start(out=columns.rearrange("(i p) j -> p i j", p=P), in_=result[:])
 
-        def store(first):
-            for bank in range(2):
-                ring, banks = ("turned", 2) if first % 4 == 0 else ("linear", 3)
-                turned = psum.tile([P, 2, 2, P], F32, name="turned", tag=ring, bufs=banks)
-                for i in range(2):
-                    actions = slice((2 * bank + i) * P, (2 * bank + i + 1) * P)
-                    for e in range(2):
-                        nc.tensor.transpose(turned[:, i, e, :], scaled[first + e][:, actions], identity[:])
-                result = work.tile([P, 2, 2 * P], F32, name="result", bufs=8)
-                nc.scalar.copy(result[:], turned[:].rearrange("p i e j -> p i (e j)"))
-                block = out[2 * bank * P : 2 * (bank + 1) * P, first * P : (first + 2) * P]
-                nc.sync.dma_start(out=block.rearrange("(i p) j -> p i j", p=P), in_=result[:])
-
-        chunks = S // P
-        turned_chunks = PACK
-        scaled = {}
-        on_vector, on_scalar = nc.vector.tensor_copy, nc.scalar.copy
         gather_states(1, 0)
         gate(0)
         gather_states(1, 1)
@@ -290,53 +300,59 @@ def tile_list_replay_action_targets_kernel(
             for dst, src in place_rows(v2_plane, 4 * a, v2_rows[:].bitcast(I32), a):
                 nc.sync.dma_start(out=dst, in_=src)
         v2_s = v2_plane[:].bitcast(U8)
+
         for a in range(PASSES):
-            cast_w1(0, a, 0, on_vector)
+            cast_w1(0, a, 0, nc.vector.tensor_copy)
             gate(1 + a)
-            cast_w1(0, a, 1, on_vector)
+            cast_w1(0, a, 1, nc.vector.tensor_copy)
             quantise_w1(0, a)
-        gate(3)
+        gate(PACK - 1)
         regroup(w4_w[1][:].bitcast(U16), w4_raw[1][:].bitcast(U16))
-        for n in range(PACK, 4 * PACK):
-            if n in (12, 14):
-                hidden(n - PACK)
-                hidden(n - PACK + 1)
-                quantise_h(QUADS[2], n % PACK, 2)
-            if n == 12:
-                targets(0)
-                targets(1)
+
+        for n in range(PACK, 3 * PACK):
             gate(n)
-            if n < 3 * PACK:
-                hidden(n - PACK)
-                if n % PACK == PACK - 1:
-                    quantise_h(QUADS[n // PACK - 1], 0, PACK)
-            if 6 <= n < 10:
-                cast_w1(1, (n - 6) // 2, n % 2, on_scalar)
-                if n % 2 == 1:
-                    quantise_w1(1, (n - 6) // 2)
-            if n == 10:
+            hidden(n - PACK)
+            if n % PACK == PACK - 1:
+                quantise_h(QUADS[n // PACK - 1], 0, PACK)
+            if FIRST_LATE_CAST <= n < FIRST_LATE_CAST + 2 * PASSES:
+                a, u = divmod(n - FIRST_LATE_CAST, 2)
+                cast_w1(1, a, u, nc.scalar.copy)
+                if u == 1:
+                    quantise_w1(1, a)
+            if n == ROWS_GATE:
                 rows = queued([P, P], F32, "rows", "late")
                 nc.gpsimd.memset(rows[:], 0.0)
-                nc.sync.dma_start(out=rows[0:chunks, :], in_=discount.rearrange("(c p) -> c p", p=P))
-                nc.sync.dma_start(out=rows[chunks : 2 * chunks, :], in_=reward.rearrange("(c p) -> c p", p=P))
+                nc.sync.dma_start(out=rows[0:PACK, :], in_=discount[0:PASS].rearrange("(c p) -> c p", p=P))
+                nc.sync.dma_start(out=rows[PACK : 2 * PACK, :], in_=reward[0:PASS].rearrange("(c p) -> c p", p=P))
                 spread = held([P, 2, PASS], F32, "spread", "grouped01")
-                nc.sync.dma_start(out=spread[:, 0, :], in_=discount[turned_chunks * P :].partition_broadcast(P))
-                nc.sync.dma_start(out=spread[:, 1, :], in_=reward[turned_chunks * P :].partition_broadcast(P))
-                turned_rows = psum.tile([P, PACK, P], F32, name="turned", tag="turned", bufs=2)
+                nc.sync.dma_start(out=spread[:, 0, :], in_=discount[PASS:].partition_broadcast(P))
+                nc.sync.dma_start(out=spread[:, 1, :], in_=reward[PASS:].partition_broadcast(P))
+                turned_rows = bank([P, PACK, P], "turned", SPARE_RING)
                 nc.tensor.transpose(turned_rows[:, 0, :], rows[:], identity[:])
-                nc.scalar.copy(per_state[:], turned_rows[:, 0, 0 : 2 * chunks])
+                nc.scalar.copy(per_state[:], turned_rows[:, 0, 0 : 2 * PACK])
+            if n in ACTION_GATES:
+                half = ACTION_GATES.index(n)
+                nc.vector.tensor_copy(v2_w[half][:], tab2_w[:, half, :].bitcast(U32).indirect(idx2[:]))
 
-            if n in (9, 11):
-                nc.vector.tensor_copy(v2_w[n // 11][:], tab2_w[:, n // 11, :].bitcast(U32).indirect(idx2[:]))
-        store(0)
-        targets(2)
-        targets(3)
+        for first in range(0, PACK, 2):
+            hidden(2 * PACK + first)
+            hidden(2 * PACK + first + 1)
+            quantise_h(QUADS[2], first, 2)
+            if first == 0:
+                targets_by_state(0)
+                targets_by_state(1)
+            gate(3 * PACK + first)
+            gate(3 * PACK + first + 1)
+        turn_and_store(0, SPARE_RING)
+        targets_by_state(2)
+        targets_by_state(3)
+
         for in_part in range(PACK):
             hidden(3 * PACK + in_part)
             quantise_h(QUADS[3], in_part, 1)
-        for chunk in range(turned_chunks, chunks):
-            targets_in_place(chunk)
-            if chunk == turned_chunks + 1:
-                store(2)
-        for chunk in range(turned_chunks, chunks):
-            store_in_place(chunk)
+        for in_part in range(PACK):
+            discount_by_action(in_part)
+            if in_part == 1:
+                turn_and_store(2, LINEAR_RING)
+        for in_part in range(PACK):
+            reward_and_store(in_part)

@@ -161,6 +161,7 @@ def tile_list_replay_action_targets_kernel(
         h_s = {quad: held([P, PASS], U8, f"h_s{quad[0]}{quad[1]}") for quad in QUADS}
 
         scaled = {}
+        discounted = {}
 
         def cast_w1(half, a, u, copy):
             src = w1_raw[half][:, a].rearrange("p i (m u e) -> p u m i e", u=2, e=2)[:, u]
@@ -259,13 +260,13 @@ def tile_list_replay_action_targets_kernel(
                 block = out[2 * pair * P : 2 * (pair + 1) * P, first * P : (first + 2) * P]
                 nc.sync.dma_start(out=block.rearrange("(i p) j -> p i j", p=P), in_=result[:])
 
-        by_action = [P, PACK, P]
+        by_action = [P, 2, 2 * P]
 
-        def discount_by_action(in_part):
-            states = slice(in_part * P, (in_part + 1) * P)
+        def discount_by_action(first, pair):
+            states = slice(first * P, (first + 2) * P)
             q = bank(by_action, "q", GATE_RING)
-            for i in range(PACK):
-                actions = slice(i * P, (i + 1) * P)
+            for i in range(2):
+                actions = slice((2 * pair + i) * P, (2 * pair + i + 1) * P)
                 mx_sum(
                     q[:, i, :],
                     [
@@ -278,16 +279,16 @@ def tile_list_replay_action_targets_kernel(
                         for half in (0, 1)
                     ],
                 )
-            scaled[PACK + in_part] = work.tile(by_action, F32, name="scaled", bufs=6)
+            discounted[first, pair] = work.tile(by_action, F32, name="scaled", bufs=6)
             factor = spread[:, 0, states].unsqueeze(1).to_broadcast(by_action)
-            nc.vector.tensor_tensor(scaled[PACK + in_part][:], q[:], factor, ALU.mult)
+            nc.vector.tensor_tensor(discounted[first, pair][:], q[:], factor, ALU.mult)
 
-        def reward_and_store(in_part):
-            offset = spread[:, 1, in_part * P : (in_part + 1) * P].unsqueeze(1).to_broadcast(by_action)
+        def reward_and_store(first, pair):
+            offset = spread[:, 1, first * P : (first + 2) * P].unsqueeze(1).to_broadcast(by_action)
             result = work.tile(by_action, F32, name="result", bufs=8)
-            nc.vector.tensor_tensor(result[:], scaled[PACK + in_part][:], offset, ALU.add)
-            columns = out[:, PASS + in_part * P : PASS + (in_part + 1) * P]
-            nc.sync.dma_start(out=columns.rearrange("(i p) j -> p i j", p=P), in_=result[:])
+            nc.vector.tensor_tensor(result[:], discounted[first, pair][:], offset, ALU.add)
+            block = out[2 * pair * P : 2 * (pair + 1) * P, PASS + first * P : PASS + (first + 2) * P]
+            nc.sync.dma_start(out=block.rearrange("(i p) j -> p i j", p=P), in_=result[:])
 
         gather_states(1, 0)
         gate(0)
@@ -347,12 +348,15 @@ def tile_list_replay_action_targets_kernel(
         targets_by_state(2)
         targets_by_state(3)
 
-        for in_part in range(PACK):
-            hidden(3 * PACK + in_part)
-            quantise_h(QUADS[3], in_part, 1)
-        for in_part in range(PACK):
-            discount_by_action(in_part)
-            if in_part == 1:
+        for first in range(0, PACK, 2):
+            hidden(3 * PACK + first)
+            hidden(3 * PACK + first + 1)
+            quantise_h(QUADS[3], first, 2)
+        for first in range(0, PACK, 2):
+            for pair in range(2):
+                discount_by_action(first, pair)
+            if first == 0:
                 turn_and_store(2, LINEAR_RING)
-        for in_part in range(PACK):
-            reward_and_store(in_part)
+        for first in range(0, PACK, 2):
+            for pair in range(2):
+                reward_and_store(first, pair)

@@ -25,16 +25,15 @@ LIST_ROWS = 16
 
 QUADRANT = 32
 SCALE_ROWS = 32
-
 GATE_RING = ("gate", 3)
 LINEAR_RING = ("linear", 3)
 SPARE_RING = ("spare", 2)
+TABLE_BYTES = 4 * T
 
 QUADS = [(half, part) for half in range(2) for part in range(2)]
 FIRST_LATE_CAST = 6
-ROWS_GATE = 10
 ACTION_GATES = (9, 11)
-MOVES_AHEAD = 3
+TURNED = 4
 
 
 def tile_list_replay_action_targets_kernel(
@@ -43,14 +42,15 @@ def tile_list_replay_action_targets_kernel(
     nc = tc.nc
     with ExitStack() as ctx:
         keep = ctx.enter_context(tc.tile_pool(name="keep", bufs=1))
+        arena = ctx.enter_context(tc.tile_pool(name="arena", bufs=1))
         work = ctx.enter_context(tc.tile_pool(name="work", bufs=4))
         psum = ctx.enter_context(tc.psum_pool(name="psum", bufs=1))
 
         def held(shape, dtype, name, tag=None):
             return keep.tile(shape, dtype, name=name, tag=tag or name, align_bytes=64)
 
-        def queued(shape, dtype, name, ring):
-            return keep.tile(shape, dtype, name=name, tag=ring, bufs=2, align_bytes=64)
+        def placed(shape, dtype, name, offset):
+            return arena.tile(shape, dtype, name=name, offset=offset, align_bytes=64)
 
         def bank(shape, name, ring):
             return psum.tile(shape, F32, name=name, tag=ring[0], bufs=ring[1])
@@ -67,60 +67,67 @@ def tile_list_replay_action_targets_kernel(
                     stop=(n == len(operands) - 1),
                 )
 
-        def load_w1(dst, half):
-            for a in range(PASSES):
-                rows = w1[a * PASS : (a + 1) * PASS, half * PASS : (half + 1) * PASS]
-                nc.sync.dma_start(out=dst[:, a], in_=rows.rearrange("(p i) c -> p i c", i=PACK))
+        def load_w1(dst, half, a):
+            rows = w1[a * PASS : (a + 1) * PASS, half * PASS : (half + 1) * PASS]
+            nc.sync.dma_start(out=dst[:, a], in_=rows.rearrange("(p i) c -> p i c", i=PACK))
 
         def place_rows(dst, first, src, a):
-            return [
-                (
-                    dst[QUADRANT * quadrant + first : QUADRANT * quadrant + first + 4, :],
-                    src[16 * a + 4 * quadrant : 16 * a + 4 * quadrant + 4, :],
+            for quadrant in range(4):
+                nc.sync.dma_start(
+                    out=dst[QUADRANT * quadrant + first : QUADRANT * quadrant + first + 4, :],
+                    in_=src[16 * a + 4 * quadrant : 16 * a + 4 * quadrant + 4, :],
                 )
-                for quadrant in range(4)
-            ]
+
+        def load_rows(dst, scales, engine):
+            engine.memset(dst[SCALE_ROWS : 2 * QUADRANT, :], 0)
+            engine.memset(dst[2 * QUADRANT : P, :], 0)
+            nc.sync.dma_start(out=dst[0:SCALE_ROWS, :], in_=scales.bitcast(I32).rearrange("a q c -> (a q) c"))
 
         idx = keep.tile([P, S // LIST_ROWS], U16, name="idx")
         idx2 = keep.tile([P, S2 // LIST_ROWS], U16, name="idx2")
-        tab_s = queued([P, T // 4], I32, "tab_s", "early")
-        w4_raw = [queued([P, PASSES, PASS // 2], I32, "w4_raw0", "early")]
-        w4_raw_s = held([P, PASSES, H // 4], I32, "w4_raw_s")
-        v_planes = [queued([P, S // 4], I32, "v_s0", "late"), held([P, S // 4], I32, "v_s1")]
-        tab_w = [queued([P, T], I32, "tab_w0", "late"), queued([P, T], I32, "tab_w1", "early")]
+        tab_s = held([P, T // 4], I32, "tab_s")
         tab2_s = held([P, T2 // 4], I32, "tab2_s")
+        w4_raw_s = held([P, H // 4], I32, "w4_raw_s")
+        w4_raw = [held([P, PASSES, PASS // 2], I32, "w4_raw0", "w4_raw")]
+        tab_w = [held([P, T], I32, "tab_w0", "table")]
+        planes = [held([P, (S + H) // 4], I32, f"planes{a}") for a in range(PASSES)]
         identity = held([P, P], F32, "identity")
-        per_state = held([P, 2 * PACK], F32, "per_state")
-
-        nc.vector.memset(w4_raw_s[:], 0)
-        nc.vector.memset(v_planes[0][:], 0)
-        nc.vector.memset(tab2_s[:], 0)
-        nc.vector.memset(tab_s[SCALE_ROWS : 2 * QUADRANT, :], 0)
-        nc.vector.memset(tab_s[2 * QUADRANT : P, :], 0)
-        nc.gpsimd.memset(v_planes[1][:], 0)
-        make_identity(nc, identity[:])
 
         nc.sync.dma_start(idx[:], offs)
-        nc.sync.dma_start(out=tab_s[0:SCALE_ROWS, :], in_=tab_scales.bitcast(I32).rearrange("a q c -> (a q) c"))
+        load_rows(tab_s, tab_scales, nc.vector)
+        load_rows(w4_raw_s, w4_scales, nc.gpsimd)
+        nc.sync.dma_start(idx2[:], offs2)
+        for a in range(PASSES):
+            nc.gpsimd.memset(planes[a][:], 0)
+        load_rows(tab2_s, tab2_scales, nc.gpsimd)
         w4_rows = w4_words.bitcast(I32).rearrange("a p (h c) -> h p a c", h=2)
         nc.sync.dma_start(out=w4_raw[0][:], in_=w4_rows[0])
-        nc.sync.dma_start(idx2[:], offs2)
-        for quadrant in range(4):
-            nc.sync.dma_start(
-                out=w4_raw_s[QUADRANT * quadrant : QUADRANT * quadrant + 4, :, :],
-                in_=w4_scales.bitcast(I32)[:, 4 * quadrant : 4 * quadrant + 4, :].rearrange("a s c -> s a c"),
-            )
         nc.sync.dma_start(out=tab_w[0][:], in_=tab_words[0].rearrange("p t i -> p (t i)").bitcast(I32))
-        nc.sync.dma_start(out=tab2_s[0:SCALE_ROWS, :], in_=tab2_scales.bitcast(I32).rearrange("a q c -> (a q) c"))
+        make_identity(nc, identity[:])
 
-        v_rows = held([P, S], U8, "v_rows")
+        def regroup(dst, src):
+            nc.vector.tensor_copy(
+                dst.rearrange("p a (t m) -> p a t m", t=PACK),
+                src.rearrange("p a (m t) -> p a t m", t=PACK),
+            )
+
+        v_rows = placed([P, S], U8, "v_rows", TABLE_BYTES - S // 2)
+        rows = held([P, S + H], U8, "rows")
+        regroup(
+            rows[:, S:].rearrange("p (h c) -> p h c", h=2),
+            w4_raw_s[:].bitcast(U8).rearrange("p (h c) -> p h c", h=2),
+        )
         nc.vector.tensor_copy(v_rows[:], tab_s[:].bitcast(U8).indirect(idx[:]))
-        moves = [move for a in range(PASSES) for move in place_rows(v_planes[a], 0, v_rows[:].bitcast(I32), a)]
-        for n, (dst, src) in enumerate(moves):
-            if n == MOVES_AHEAD:
-                nc.sync.dma_start(out=tab_w[1][:], in_=tab_words[1].rearrange("p t i -> p (t i)").bitcast(I32))
-            nc.sync.dma_start(out=dst, in_=src)
-        v_s = [plane[:].bitcast(U8) for plane in v_planes]
+        nc.vector.tensor_copy(rows[:, 0:S].bitcast(I32), v_rows[:].bitcast(I32))
+        place_rows(planes[0], 0, rows[:].bitcast(I32), 0)
+        tab_w.append(placed([P, T], I32, "tab_w1", 0))
+        nc.sync.dma_start(out=tab_w[1][:], in_=tab_words[1].rearrange("p t i -> p (t i)").bitcast(I32))
+        place_rows(planes[1], 0, rows[:].bitcast(I32), 1)
+        w1_raw = [placed([P, PASSES, PACK, PASS], F32, "w1_raw0", TABLE_BYTES)]
+        for a in range(PASSES):
+            load_w1(w1_raw[0], 0, a)
+        v_s = [plane[:].bitcast(U8)[:, 0:S] for plane in planes]
+        w4_s = [plane[:].bitcast(U8)[:, S:] for plane in planes]
         v_w = [held([P, S], U32, f"v_w{a}") for a in range(PASSES)]
 
         def gather_states(a, part):
@@ -129,27 +136,17 @@ def tile_list_replay_action_targets_kernel(
                 v_w[a][:, part * PASS : (part + 1) * PASS], tab_w[a][:].bitcast(U32).indirect(entries)
             )
 
-        def regroup(dst, src):
-            nc.vector.tensor_copy(
-                dst.rearrange("p a (t m) -> p a t m", t=PACK),
-                src.rearrange("p a (m t) -> p a t m", t=PACK),
-            )
-
         w4_w = [held([P, PASSES, 2 * PASS], U8, f"w4_w{half}") for half in range(2)]
-        w4_s = [held([P, PASSES, PASS], U8, f"w4_s{half}") for half in range(2)]
         regroup(w4_w[0][:].bitcast(U16), w4_raw[0][:].bitcast(U16))
-        w1_raw = [queued([P, PASSES, PACK, PASS], F32, "w1_raw0", "early")]
-        load_w1(w1_raw[0], 0)
-        for half in range(2):
-            regroup(w4_s[half][:], w4_raw_s[:].bitcast(U8)[:, :, half * PASS : (half + 1) * PASS])
-        w4_raw.append(held([P, PASSES, PASS // 2], I32, "w4_raw1", "w4_raw_s"))
+        w4_raw.append(held([P, PASSES, PASS // 2], I32, "w4_raw1", "w4_raw"))
         nc.sync.dma_start(out=w4_raw[1][:], in_=w4_rows[1])
-        gather_states(0, 0)
-        gather_states(0, 1)
-        w1_raw.append(queued([P, PASSES, PACK, PASS], F32, "w1_raw1", "late"))
-        load_w1(w1_raw[1], 1)
         v2_rows = held([P, S2], U8, "v2_rows")
         nc.vector.tensor_copy(v2_rows[:], tab2_s[:].bitcast(U8).indirect(idx2[:]))
+        gather_states(0, 0)
+        gather_states(0, 1)
+        w1_raw.append(held([P, PASSES, PACK, PASS], F32, "w1_raw1", "table"))
+        for a in range(PASSES):
+            load_w1(w1_raw[1], 1, a)
 
         w1_w = [[held([P, PASS], U32, f"w1_w{half}{a}") for a in range(PASSES)] for half in range(2)]
         w1_s = [[held([P, PASS], U8, f"w1_s{half}{a}") for a in range(PASSES)] for half in range(2)]
@@ -160,30 +157,30 @@ def tile_list_replay_action_targets_kernel(
         h_w = {quad: held([P, PASS], U32, f"h_w{quad[0]}{quad[1]}") for quad in QUADS}
         h_s = {quad: held([P, PASS], U8, f"h_s{quad[0]}{quad[1]}") for quad in QUADS}
 
+        products = {}
         scaled = {}
-        discounted = {}
 
-        def cast_w1(half, a, u, copy):
-            src = w1_raw[half][:, a].rearrange("p i (m u e) -> p u m i e", u=2, e=2)[:, u]
-            dst = grouped[half][a][:].rearrange("p (u e m i) -> p u m i e", u=2, e=2, i=PACK)[:, u]
-            copy(dst, src)
+        def w1_views(half, a):
+            src = w1_raw[half][:, a].rearrange("p i (m u e) -> p u m i e", u=2, e=2)
+            dst = grouped[half][a][:].rearrange("p (u e m i) -> p u m i e", u=2, e=2, i=PACK)
+            return dst, src
 
         def quantise_w1(half, a):
             nc.vector.quantize_mx(
                 out=w1_w[half][a][:].bitcast(FP8X4), scales=w1_s[half][a][:], in_=grouped[half][a][:]
             )
 
-        def gate(n):
+        def gate(n, ring=GATE_RING):
             half, part = QUADS[n // PACK]
             t = n % PACK
             states = slice(part * PASS, (part + 1) * PASS)
-            b = bank([P, PASS], "b", GATE_RING)
+            b = bank([P, PASS], "b", ring)
             mx_sum(
                 b[:],
                 [
                     (
                         w4_w[half][:, a, 2 * P * t : 2 * P * (t + 1)].bitcast(FP4X4),
-                        w4_s[half][:, a, P * t : P * (t + 1)],
+                        w4_s[a][:, half * PASS + P * t : half * PASS + P * (t + 1)],
                         v_w[a][:, states].bitcast(FP8X4),
                         v_s[a][:, states],
                     )
@@ -191,16 +188,16 @@ def tile_list_replay_action_targets_kernel(
                 ],
             )
             clamped = work.tile([P, PASS], F32, name="clamped")
-            grown = work.tile([P, PASS], F32, name="grown")
+            grown = work.tile([P, PASS], F32, name="grown", bufs=6)
             nc.scalar.activation(clamped[:], b[:], ACT.Relu, scale=-1.0)
             nc.scalar.activation(grown[:], clamped[:], ACT.Exp, scale=-1.0)
             nc.vector.scalar_tensor_tensor(elu[half, part][:, t, :], grown[:], -1.0, b[:], ALU.add, ALU.max)
 
-        def hidden(n):
+        def hidden(n, ring=LINEAR_RING):
             half, part = QUADS[n // PACK]
             in_part = n % PACK
             states = slice(part * PASS + in_part * P, part * PASS + (in_part + 1) * P)
-            acc = bank([P, PACK, P], "acc", LINEAR_RING)
+            acc = bank([P, PACK, P], "acc", ring)
             for t in range(PACK):
                 mx_sum(
                     acc[:, t, :],
@@ -228,15 +225,16 @@ def tile_list_replay_action_targets_kernel(
                 in_=h[quad][:, first * PASS : (first + count) * PASS],
             )
 
-        def targets_by_state(chunk):
-            states = slice(chunk * P, (chunk + 1) * P)
-            q = bank([P, S2], "q", SPARE_RING if chunk < 2 else GATE_RING)
+        def targets_by_state(chunk, ring=SPARE_RING):
+            part, in_part = divmod(chunk, PACK)
+            states = slice(in_part * P, (in_part + 1) * P)
+            q = bank([P, S2], "q", ring)
             mx_sum(
                 q[:],
                 [
                     (
-                        h_w[half, 0][:, states].bitcast(FP8X4),
-                        h_s[half, 0][:, states],
+                        h_w[half, part][:, states].bitcast(FP8X4),
+                        h_s[half, part][:, states],
                         v2_w[half][:].bitcast(FP8X4),
                         v2_s[4 * half : P, :],
                     )
@@ -244,11 +242,11 @@ def tile_list_replay_action_targets_kernel(
                 ],
             )
             scaled[chunk] = work.tile([P, S2], F32, name="scaled", bufs=6)
-            factor = per_state[:, chunk : chunk + 1]
-            offset = per_state[:, PACK + chunk : PACK + chunk + 1]
+            factor = per_state[:, 0, chunk : chunk + 1]
+            offset = per_state[:, 1, chunk : chunk + 1]
             nc.scalar.activation(scaled[chunk][:], q[:], ACT.Identity, bias=offset, scale=factor)
 
-        def turn_and_store(first, ring):
+        def turn_and_store(first, ring=SPARE_RING):
             for pair in range(2):
                 turned = bank([P, 2, 2, P], "turned", ring)
                 for i in range(2):
@@ -262,9 +260,10 @@ def tile_list_replay_action_targets_kernel(
 
         by_action = [P, 2, 2 * P]
 
-        def discount_by_action(first, pair):
-            states = slice(first * P, (first + 2) * P)
-            q = bank(by_action, "q", GATE_RING)
+        def targets_by_action(first, pair, ring=GATE_RING):
+            states = slice((first - PACK) * P, (first - PACK + 2) * P)
+            spread_states = slice((first - TURNED) * P, (first - TURNED + 2) * P)
+            q = bank(by_action, "q", ring)
             for i in range(2):
                 actions = slice((2 * pair + i) * P, (2 * pair + i + 1) * P)
                 mx_sum(
@@ -276,40 +275,43 @@ def tile_list_replay_action_targets_kernel(
                             h_w[half, 1][:, states].bitcast(FP8X4),
                             h_s[half, 1][:, states],
                         )
-                        for half in (0, 1)
+                        for half in (1, 0)
                     ],
                 )
-            discounted[first, pair] = work.tile(by_action, F32, name="scaled", bufs=6)
-            factor = spread[:, 0, states].unsqueeze(1).to_broadcast(by_action)
-            nc.vector.tensor_tensor(discounted[first, pair][:], q[:], factor, ALU.mult)
+            discounted = work.tile(by_action, F32, name="scaled", bufs=6)
+            nc.vector.tensor_tensor(discounted[:], q[:], spread[:, 0, spread_states].unsqueeze(1).to_broadcast(by_action), ALU.mult)
+            products[first, pair] = discounted
 
         def reward_and_store(first, pair):
-            offset = spread[:, 1, first * P : (first + 2) * P].unsqueeze(1).to_broadcast(by_action)
             result = work.tile(by_action, F32, name="result", bufs=8)
-            nc.vector.tensor_tensor(result[:], discounted[first, pair][:], offset, ALU.add)
-            block = out[2 * pair * P : 2 * (pair + 1) * P, PASS + first * P : PASS + (first + 2) * P]
+            offset = spread[:, 1, (first - TURNED) * P : (first - TURNED + 2) * P].unsqueeze(1).to_broadcast(by_action)
+            nc.vector.tensor_tensor(result[:], products[first, pair][:], offset, ALU.add)
+            block = out[2 * pair * P : 2 * (pair + 1) * P, first * P : (first + 2) * P]
             nc.sync.dma_start(out=block.rearrange("(i p) j -> p i j", p=P), in_=result[:])
 
         gather_states(1, 0)
-        gate(0)
         gather_states(1, 1)
-        tab2_w = queued([P, 2, T2], I32, "tab2_w", "early")
+        tab2_w = placed([P, 2, T2], I32, "tab2_w", 0)
         nc.sync.dma_start(out=tab2_w[:], in_=tab2_words.rearrange("a p t i -> p a (t i)").bitcast(I32))
-        v2_plane = queued([P, S2 // 4], I32, "v2_s", "early")
+        per_state = placed([P, 2, 2 * PACK], F32, "per_state", TABLE_BYTES // 2)
+        spread = placed([P, 2, S - TURNED * P], F32, "spread", TABLE_BYTES // 2 + 64)
+        for n, values in enumerate((discount, reward)):
+            with nc.allow_non_contiguous_dma(reason="one value a partition for each chunk"):
+                nc.sync.dma_start(out=per_state[:, n, 0:TURNED], in_=values[0 : TURNED * P].rearrange("(c p) -> p c", p=P))
+            nc.sync.dma_start(out=spread[:, n, :], in_=values[TURNED * P :].partition_broadcast(P))
+        v2_plane = placed([P, S2 // 4], I32, "v2_plane", TABLE_BYTES - S)
         nc.gpsimd.memset(v2_plane[:], 0)
         for a in range(PASSES):
-            for dst, src in place_rows(v2_plane, 4 * a, v2_rows[:].bitcast(I32), a):
-                nc.sync.dma_start(out=dst, in_=src)
+            place_rows(v2_plane, 4 * a, v2_rows[:].bitcast(I32), a)
         v2_s = v2_plane[:].bitcast(U8)
 
         for a in range(PASSES):
-            cast_w1(0, a, 0, nc.vector.tensor_copy)
-            gate(1 + a)
-            cast_w1(0, a, 1, nc.vector.tensor_copy)
+            nc.vector.tensor_copy(*w1_views(0, a))
+            gate(a, SPARE_RING)
             quantise_w1(0, a)
-        gate(PACK - 1)
+        gate(2, LINEAR_RING)
+        gate(3, LINEAR_RING)
         regroup(w4_w[1][:].bitcast(U16), w4_raw[1][:].bitcast(U16))
-
         for n in range(PACK, 3 * PACK):
             gate(n)
             hidden(n - PACK)
@@ -317,24 +319,13 @@ def tile_list_replay_action_targets_kernel(
                 quantise_h(QUADS[n // PACK - 1], 0, PACK)
             if FIRST_LATE_CAST <= n < FIRST_LATE_CAST + 2 * PASSES:
                 a, u = divmod(n - FIRST_LATE_CAST, 2)
-                cast_w1(1, a, u, nc.scalar.copy)
+                dst, src = w1_views(1, a)
+                nc.scalar.copy(dst[:, u], src[:, u])
                 if u == 1:
                     quantise_w1(1, a)
-            if n == ROWS_GATE:
-                rows = queued([P, P], F32, "rows", "late")
-                nc.gpsimd.memset(rows[:], 0.0)
-                nc.sync.dma_start(out=rows[0:PACK, :], in_=discount[0:PASS].rearrange("(c p) -> c p", p=P))
-                nc.sync.dma_start(out=rows[PACK : 2 * PACK, :], in_=reward[0:PASS].rearrange("(c p) -> c p", p=P))
-                spread = held([P, 2, PASS], F32, "spread", "grouped01")
-                nc.sync.dma_start(out=spread[:, 0, :], in_=discount[PASS:].partition_broadcast(P))
-                nc.sync.dma_start(out=spread[:, 1, :], in_=reward[PASS:].partition_broadcast(P))
-                turned_rows = bank([P, PACK, P], "turned", SPARE_RING)
-                nc.tensor.transpose(turned_rows[:, 0, :], rows[:], identity[:])
-                nc.scalar.copy(per_state[:], turned_rows[:, 0, 0 : 2 * PACK])
             if n in ACTION_GATES:
                 half = ACTION_GATES.index(n)
                 nc.vector.tensor_copy(v2_w[half][:], tab2_w[:, half, :].bitcast(U32).indirect(idx2[:]))
-
         for first in range(0, PACK, 2):
             hidden(2 * PACK + first)
             hidden(2 * PACK + first + 1)
@@ -345,18 +336,17 @@ def tile_list_replay_action_targets_kernel(
             gate(3 * PACK + first)
             gate(3 * PACK + first + 1)
         turn_and_store(0, SPARE_RING)
-        targets_by_state(2)
-        targets_by_state(3)
-
+        targets_by_state(2, GATE_RING)
+        targets_by_state(3, GATE_RING)
         for first in range(0, PACK, 2):
             hidden(3 * PACK + first)
             hidden(3 * PACK + first + 1)
             quantise_h(QUADS[3], first, 2)
-        for first in range(0, PACK, 2):
+        for first in (4, 6):
             for pair in range(2):
-                discount_by_action(first, pair)
-            if first == 0:
+                targets_by_action(first, pair)
+            if first == 4:
                 turn_and_store(2, LINEAR_RING)
-        for first in range(0, PACK, 2):
+        for first in (4, 6):
             for pair in range(2):
                 reward_and_store(first, pair)

@@ -326,27 +326,33 @@ def tile_list_replay_action_targets_kernel(
             if n in ACTION_GATES:
                 half = ACTION_GATES.index(n)
                 nc.vector.tensor_copy(v2_w[half][:], tab2_w[:, half, :].bitcast(U32).indirect(idx2[:]))
-        for first in range(0, PACK, 2):
-            hidden(2 * PACK + first)
-            hidden(2 * PACK + first + 1)
-            quantise_h(QUADS[2], first, 2)
-            if first == 0:
-                targets_by_state(0)
-                targets_by_state(1)
-            gate(3 * PACK + first)
-            gate(3 * PACK + first + 1)
-        turn_and_store(0, SPARE_RING)
-        targets_by_state(2, GATE_RING)
+        gate(12, SPARE_RING)
+        hidden(8, LINEAR_RING)
+        hidden(9, LINEAR_RING)
+        gate(13, SPARE_RING)
+        quantise_h(QUADS[2], 0, 2)
+        hidden(10, LINEAR_RING)
+        gate(14, GATE_RING)
+        hidden(11, LINEAR_RING)
+        gate(15, GATE_RING)
+        quantise_h(QUADS[2], 2, 2)
+        targets_by_state(0, GATE_RING)
+        targets_by_state(1, SPARE_RING)
+        hidden(12, LINEAR_RING)
+        hidden(13, LINEAR_RING)
+        targets_by_state(2, SPARE_RING)
         targets_by_state(3, GATE_RING)
-        for first in range(0, PACK, 2):
-            hidden(3 * PACK + first)
-            hidden(3 * PACK + first + 1)
-            quantise_h(QUADS[3], first, 2)
-        for first in (4, 6):
-            for pair in range(2):
-                targets_by_action(first, pair)
-            if first == 4:
-                turn_and_store(2, LINEAR_RING)
-        for first in (4, 6):
-            for pair in range(2):
-                reward_and_store(first, pair)
+        quantise_h(QUADS[3], 0, 2)
+        hidden(14, LINEAR_RING)
+        hidden(15, LINEAR_RING)
+        turn_and_store(0, GATE_RING)
+        targets_by_action(4, 0, LINEAR_RING)
+        targets_by_action(4, 1, LINEAR_RING)
+        quantise_h(QUADS[3], 2, 2)
+        turn_and_store(2, SPARE_RING)
+        reward_and_store(4, 0)
+        targets_by_action(6, 0, GATE_RING)
+        reward_and_store(4, 1)
+        targets_by_action(6, 1, LINEAR_RING)
+        reward_and_store(6, 0)
+        reward_and_store(6, 1)

@@ -33,6 +33,7 @@ TABLE_BYTES = 4 * T
 QUADS = [(half, part) for half in range(2) for part in range(2)]
 FIRST_LATE_CAST = 6
 ACTION_GATES = (9, 11)
+MOVES_AHEAD = 3
 TURNED = 4
 
 
@@ -71,58 +72,48 @@ def tile_list_replay_action_targets_kernel(
             rows = w1[a * PASS : (a + 1) * PASS, half * PASS : (half + 1) * PASS]
             nc.sync.dma_start(out=dst[:, a], in_=rows.rearrange("(p i) c -> p i c", i=PACK))
 
-        def place_rows(dst, first, src, a):
-            for quadrant in range(4):
-                nc.sync.dma_start(
-                    out=dst[QUADRANT * quadrant + first : QUADRANT * quadrant + first + 4, :],
-                    in_=src[16 * a + 4 * quadrant : 16 * a + 4 * quadrant + 4, :],
-                )
+        def move_rows(dst, to, src, start):
+            nc.sync.dma_start(out=dst[to : to + 4, :], in_=src[start : start + 4, :])
 
         def load_rows(dst, scales, engine):
+            nc.sync.dma_start(out=dst[0:SCALE_ROWS, :], in_=scales.bitcast(I32).rearrange("a q c -> (a q) c"))
             engine.memset(dst[SCALE_ROWS : 2 * QUADRANT, :], 0)
             engine.memset(dst[2 * QUADRANT : P, :], 0)
-            nc.sync.dma_start(out=dst[0:SCALE_ROWS, :], in_=scales.bitcast(I32).rearrange("a q c -> (a q) c"))
 
         idx = keep.tile([P, S // LIST_ROWS], U16, name="idx")
         idx2 = keep.tile([P, S2 // LIST_ROWS], U16, name="idx2")
         tab_s = held([P, T // 4], I32, "tab_s")
         tab2_s = held([P, T2 // 4], I32, "tab2_s")
         w4_raw_s = held([P, H // 4], I32, "w4_raw_s")
-        w4_raw = [held([P, PASSES, PASS // 2], I32, "w4_raw0", "w4_raw")]
+        w4_raw = held([P, PASSES, H // 2], I32, "w4_raw")
         tab_w = [held([P, T], I32, "tab_w0", "table")]
         planes = [held([P, (S + H) // 4], I32, f"planes{a}") for a in range(PASSES)]
-        identity = held([P, P], F32, "identity")
 
         nc.sync.dma_start(idx[:], offs)
+        load_rows(w4_raw_s, w4_scales, nc.vector)
         load_rows(tab_s, tab_scales, nc.vector)
-        load_rows(w4_raw_s, w4_scales, nc.gpsimd)
+        nc.gpsimd.memset(planes[1][:], 0)
         nc.sync.dma_start(idx2[:], offs2)
-        for a in range(PASSES):
-            nc.gpsimd.memset(planes[a][:], 0)
         load_rows(tab2_s, tab2_scales, nc.gpsimd)
-        w4_rows = w4_words.bitcast(I32).rearrange("a p (h c) -> h p a c", h=2)
-        nc.sync.dma_start(out=w4_raw[0][:], in_=w4_rows[0])
+        nc.sync.dma_start(out=w4_raw[:], in_=w4_words.bitcast(I32).rearrange("a p c -> p a c"))
         nc.sync.dma_start(out=tab_w[0][:], in_=tab_words[0].rearrange("p t i -> p (t i)").bitcast(I32))
-        make_identity(nc, identity[:])
 
         def regroup(dst, src):
             nc.vector.tensor_copy(
-                dst.rearrange("p a (t m) -> p a t m", t=PACK),
-                src.rearrange("p a (m t) -> p a t m", t=PACK),
+                dst.rearrange("p (r t m) -> p r t m", t=PACK, m=P),
+                src.rearrange("p (r m t) -> p r t m", t=PACK, m=P),
             )
 
         v_rows = placed([P, S], U8, "v_rows", TABLE_BYTES - S // 2)
-        rows = held([P, S + H], U8, "rows")
-        regroup(
-            rows[:, S:].rearrange("p (h c) -> p h c", h=2),
-            w4_raw_s[:].bitcast(U8).rearrange("p (h c) -> p h c", h=2),
-        )
+        regroup(planes[0][:].bitcast(U8)[:, S:], w4_raw_s[:].bitcast(U8))
         nc.vector.tensor_copy(v_rows[:], tab_s[:].bitcast(U8).indirect(idx[:]))
-        nc.vector.tensor_copy(rows[:, 0:S].bitcast(I32), v_rows[:].bitcast(I32))
-        place_rows(planes[0], 0, rows[:].bitcast(I32), 0)
+        nc.vector.tensor_copy(planes[0][:, 0 : S // 4], v_rows[:].bitcast(I32))
         tab_w.append(placed([P, T], I32, "tab_w1", 0))
-        nc.sync.dma_start(out=tab_w[1][:], in_=tab_words[1].rearrange("p t i -> p (t i)").bitcast(I32))
-        place_rows(planes[1], 0, rows[:].bitcast(I32), 1)
+        for group in range(1, 8):
+            a, quadrant = divmod(group, 4)
+            move_rows(planes[a], QUADRANT * quadrant, planes[0], 4 * group)
+            if group == MOVES_AHEAD:
+                nc.sync.dma_start(out=tab_w[1][:], in_=tab_words[1].rearrange("p t i -> p (t i)").bitcast(I32))
         w1_raw = [placed([P, PASSES, PACK, PASS], F32, "w1_raw0", TABLE_BYTES)]
         for a in range(PASSES):
             load_w1(w1_raw[0], 0, a)
@@ -136,10 +127,8 @@ def tile_list_replay_action_targets_kernel(
                 v_w[a][:, part * PASS : (part + 1) * PASS], tab_w[a][:].bitcast(U32).indirect(entries)
             )
 
-        w4_w = [held([P, PASSES, 2 * PASS], U8, f"w4_w{half}") for half in range(2)]
-        regroup(w4_w[0][:].bitcast(U16), w4_raw[0][:].bitcast(U16))
-        w4_raw.append(held([P, PASSES, PASS // 2], I32, "w4_raw1", "w4_raw"))
-        nc.sync.dma_start(out=w4_raw[1][:], in_=w4_rows[1])
+        w4_w = held([P, PASSES * 2 * H], U8, "w4_w")
+        regroup(w4_w[:].bitcast(U16), w4_raw[:].rearrange("p a c -> p (a c)").bitcast(U16))
         v2_rows = held([P, S2], U8, "v2_rows")
         nc.vector.tensor_copy(v2_rows[:], tab2_s[:].bitcast(U8).indirect(idx2[:]))
         gather_states(0, 0)
@@ -150,7 +139,10 @@ def tile_list_replay_action_targets_kernel(
 
         w1_w = [[held([P, PASS], U32, f"w1_w{half}{a}") for a in range(PASSES)] for half in range(2)]
         w1_s = [[held([P, PASS], U8, f"w1_s{half}{a}") for a in range(PASSES)] for half in range(2)]
-        grouped = [[held([P, PACK * PASS], BF16, f"grouped{half}{a}") for a in range(PASSES)] for half in range(2)]
+        grouped = [
+            [placed([P, PACK * PASS], BF16, f"grouped{half}{a}", (2 * PACK + 2 * half + a) * 2 * PACK * PASS) for a in range(PASSES)]
+            for half in range(2)
+        ]
         v2_w = [held([P, S2], U32, f"v2_w{half}") for half in range(2)]
         elu = {quad: held([P, PACK, PASS], F32, f"elu{quad[0]}{quad[1]}") for quad in QUADS}
         h = {quad: held([P, PACK * PASS], BF16, f"h{quad[0]}{quad[1]}") for quad in QUADS}
@@ -173,14 +165,15 @@ def tile_list_replay_action_targets_kernel(
         def gate(n, ring=GATE_RING):
             half, part = QUADS[n // PACK]
             t = n % PACK
+            first = half * PASS + P * t
             states = slice(part * PASS, (part + 1) * PASS)
             b = bank([P, PASS], "b", ring)
             mx_sum(
                 b[:],
                 [
                     (
-                        w4_w[half][:, a, 2 * P * t : 2 * P * (t + 1)].bitcast(FP4X4),
-                        w4_s[a][:, half * PASS + P * t : half * PASS + P * (t + 1)],
+                        w4_w[:, 2 * (a * H + first) : 2 * (a * H + first + P)].bitcast(FP4X4),
+                        w4_s[a][:, first : first + P],
                         v_w[a][:, states].bitcast(FP8X4),
                         v_s[a][:, states],
                     )
@@ -299,11 +292,6 @@ def tile_list_replay_action_targets_kernel(
             with nc.allow_non_contiguous_dma(reason="one value a partition for each chunk"):
                 nc.sync.dma_start(out=per_state[:, n, 0:TURNED], in_=values[0 : TURNED * P].rearrange("(c p) -> p c", p=P))
             nc.sync.dma_start(out=spread[:, n, :], in_=values[TURNED * P :].partition_broadcast(P))
-        v2_plane = placed([P, S2 // 4], I32, "v2_plane", TABLE_BYTES - S)
-        nc.gpsimd.memset(v2_plane[:], 0)
-        for a in range(PASSES):
-            place_rows(v2_plane, 4 * a, v2_rows[:].bitcast(I32), a)
-        v2_s = v2_plane[:].bitcast(U8)
 
         for a in range(PASSES):
             nc.vector.tensor_copy(*w1_views(0, a))
@@ -311,7 +299,14 @@ def tile_list_replay_action_targets_kernel(
             quantise_w1(0, a)
         gate(2, LINEAR_RING)
         gate(3, LINEAR_RING)
-        regroup(w4_w[1][:].bitcast(U16), w4_raw[1][:].bitcast(U16))
+        identity = placed([P, P], F32, "identity", 2 * TABLE_BYTES + 2 * PACK * PASS)
+        v2_plane = placed([P, S2 // 4], I32, "v2_plane", 2 * TABLE_BYTES + 3 * PACK * PASS)
+        nc.gpsimd.memset(v2_plane[:], 0)
+        make_identity(nc, identity[:])
+        for a in range(PASSES):
+            for quadrant in range(4):
+                move_rows(v2_plane, QUADRANT * quadrant + 4 * a, v2_rows[:].bitcast(I32), 16 * a + 4 * quadrant)
+        v2_s = v2_plane[:].bitcast(U8)
         for n in range(PACK, 3 * PACK):
             gate(n)
             hidden(n - PACK)

@@ -205,9 +205,9 @@ def tile_list_replay_action_targets_kernel(
                     ],
                 )
             nc.vector.tensor_tensor(
-                h[half, part][:, in_part * PASS : (in_part + 1) * PASS].rearrange("p (c e t) -> p c t e", e=2, t=PACK),
-                acc[:].rearrange("p t (c e) -> p c t e", e=2),
-                elu[half, part][:, :, in_part * P : (in_part + 1) * P].rearrange("p t (c e) -> p c t e", e=2),
+                h[half, part][:, in_part * PASS : (in_part + 1) * PASS].rearrange("p (c e t) -> p c t e", e=4, t=PACK),
+                acc[:].rearrange("p t (c e) -> p c t e", e=4),
+                elu[half, part][:, :, in_part * P : (in_part + 1) * P].rearrange("p t (c e) -> p c t e", e=4),
                 ALU.mult,
             )
 

@@ -22,19 +22,14 @@ PACK = 4
 PASS = P * PACK
 PASSES = K // PASS
 LIST_ROWS = 16
-
 QUADRANT = 32
 SCALE_ROWS = 32
-GATE_RING = ("gate", 3)
-LINEAR_RING = ("linear", 3)
-SPARE_RING = ("spare", 2)
-TABLE_BYTES = 4 * T
+CHUNKS = S // P
+KIB = 1024
 
 QUADS = [(half, part) for half in range(2) for part in range(2)]
-FIRST_LATE_CAST = 6
-ACTION_GATES = (9, 11)
 MOVES_AHEAD = 3
-TURNED = 4
+TURNED = 6
 
 
 def tile_list_replay_action_targets_kernel(
@@ -47,17 +42,17 @@ def tile_list_replay_action_targets_kernel(
         work = ctx.enter_context(tc.tile_pool(name="work", bufs=4))
         psum = ctx.enter_context(tc.psum_pool(name="psum", bufs=1))
 
-        def held(shape, dtype, name, tag=None):
-            return keep.tile(shape, dtype, name=name, tag=tag or name, align_bytes=64)
+        def held(shape, dtype, name):
+            return keep.tile(shape, dtype, name=name, align_bytes=64)
 
         def placed(shape, dtype, name, offset):
             return arena.tile(shape, dtype, name=name, offset=offset, align_bytes=64)
 
-        def bank(shape, name, ring):
-            return psum.tile(shape, F32, name=name, tag=ring[0], bufs=ring[1])
+        def bank(shape, name, number):
+            return psum.tile(shape, F32, name=name, tag=f"bank{number}")
 
-        def mx_sum(acc, operands):
-            for n, (lhs, lhs_scale, rhs, rhs_scale) in enumerate(operands):
+        def mx_sum(passes):
+            for n, (acc, lhs, lhs_scale, rhs, rhs_scale) in enumerate(passes):
                 nc.tensor.matmul_mx(
                     out=acc,
                     lhsT=lhs,
@@ -65,12 +60,15 @@ def tile_list_replay_action_targets_kernel(
                     rhs=rhs,
                     rhs_scale=rhs_scale,
                     start=(n == 0),
-                    stop=(n == len(operands) - 1),
+                    stop=(n == len(passes) - 1),
                 )
 
         def load_w1(dst, half, a):
             rows = w1[a * PASS : (a + 1) * PASS, half * PASS : (half + 1) * PASS]
             nc.sync.dma_start(out=dst[:, a], in_=rows.rearrange("(p i) c -> p i c", i=PACK))
+
+        def load_words(dst, words):
+            nc.sync.dma_start(out=dst, in_=words.rearrange("p t i -> p (t i)").bitcast(I32))
 
         def move_rows(dst, to, src, start):
             nc.sync.dma_start(out=dst[to : to + 4, :], in_=src[start : start + 4, :])
@@ -80,43 +78,43 @@ def tile_list_replay_action_targets_kernel(
             engine.memset(dst[SCALE_ROWS : 2 * QUADRANT, :], 0)
             engine.memset(dst[2 * QUADRANT : P, :], 0)
 
-        idx = keep.tile([P, S // LIST_ROWS], U16, name="idx")
-        idx2 = keep.tile([P, S2 // LIST_ROWS], U16, name="idx2")
-        tab_s = held([P, T // 4], I32, "tab_s")
-        tab2_s = held([P, T2 // 4], I32, "tab2_s")
-        w4_raw_s = held([P, H // 4], I32, "w4_raw_s")
-        w4_raw = held([P, PASSES, H // 2], I32, "w4_raw")
-        tab_w = [held([P, T], I32, "tab_w0", "table")]
-        planes = [held([P, (S + H) // 4], I32, f"planes{a}") for a in range(PASSES)]
-
-        nc.sync.dma_start(idx[:], offs)
-        load_rows(w4_raw_s, w4_scales, nc.vector)
-        load_rows(tab_s, tab_scales, nc.vector)
-        nc.gpsimd.memset(planes[1][:], 0)
-        nc.sync.dma_start(idx2[:], offs2)
-        load_rows(tab2_s, tab2_scales, nc.gpsimd)
-        nc.sync.dma_start(out=w4_raw[:], in_=w4_words.bitcast(I32).rearrange("a p c -> p a c"))
-        nc.sync.dma_start(out=tab_w[0][:], in_=tab_words[0].rearrange("p t i -> p (t i)").bitcast(I32))
-
         def regroup(dst, src):
             nc.vector.tensor_copy(
                 dst.rearrange("p (r t m) -> p r t m", t=PACK, m=P),
                 src.rearrange("p (r m t) -> p r t m", t=PACK, m=P),
             )
 
-        v_rows = placed([P, S], U8, "v_rows", TABLE_BYTES - S // 2)
+        TAB0, TAB1, PLANE1, W4, TAB2, RAW0, RAW1, ROUNDED = 0, 16 * KIB, 32 * KIB, 34 * KIB, 38 * KIB, 46 * KIB, 62 * KIB, 78 * KIB
+
+        idx = keep.tile([P, S // LIST_ROWS], U16, name="idx")
+        idx2 = keep.tile([P, S2 // LIST_ROWS], U16, name="idx2")
+        tab_s = held([P, T // 4], I32, "tab_s")
+        tab2_s = placed([P, T2 // 4], I32, "tab2_s", RAW1)
+        w4_raw_s = held([P, H // 4], I32, "w4_raw_s")
+        w4_raw = placed([P, PASSES, H // 2], I32, "w4_raw", RAW0 - 2 * KIB)
+        tab_w = [placed([P, T], I32, "tab_w0", TAB0)]
+        planes = [held([P, (S + H) // 4], I32, "planes0")]
+
+        nc.sync.dma_start(idx[:], offs)
+        load_rows(w4_raw_s, w4_scales, nc.vector)
+        load_rows(tab_s, tab_scales, nc.vector)
+        nc.sync.dma_start(idx2[:], offs2)
+        load_rows(tab2_s, tab2_scales, nc.gpsimd)
+        nc.sync.dma_start(out=w4_raw[:], in_=w4_words.bitcast(I32).rearrange("a p c -> p a c"))
+        load_words(tab_w[0][:], tab_words[0])
+
+        v_rows = placed([P, 3 * S], U8, "v_rows", PLANE1 - S // 2)
         regroup(planes[0][:].bitcast(U8)[:, S:], w4_raw_s[:].bitcast(U8))
-        nc.vector.tensor_copy(v_rows[:], tab_s[:].bitcast(U8).indirect(idx[:]))
-        nc.vector.tensor_copy(planes[0][:, 0 : S // 4], v_rows[:].bitcast(I32))
-        tab_w.append(placed([P, T], I32, "tab_w1", 0))
+        nc.vector.tensor_copy(v_rows[:, 0:S], tab_s[:].bitcast(U8).indirect(idx[:]))
+        nc.vector.tensor_copy(planes[0][:, 0 : S // 4], v_rows[:, 0:S].bitcast(I32))
+        planes.append(placed([P, (S + H) // 4], I32, "planes1", PLANE1))
+        nc.vector.memset(planes[1][:], 0)
+        tab_w.append(placed([P, T], I32, "tab_w1", TAB1))
         for group in range(1, 8):
             a, quadrant = divmod(group, 4)
             move_rows(planes[a], QUADRANT * quadrant, planes[0], 4 * group)
             if group == MOVES_AHEAD:
-                nc.sync.dma_start(out=tab_w[1][:], in_=tab_words[1].rearrange("p t i -> p (t i)").bitcast(I32))
-        w1_raw = [placed([P, PASSES, PACK, PASS], F32, "w1_raw0", TABLE_BYTES)]
-        for a in range(PASSES):
-            load_w1(w1_raw[0], 0, a)
+                load_words(tab_w[1][:], tab_words[1])
         v_s = [plane[:].bitcast(U8)[:, 0:S] for plane in planes]
         w4_s = [plane[:].bitcast(U8)[:, S:] for plane in planes]
         v_w = [held([P, S], U32, f"v_w{a}") for a in range(PASSES)]
@@ -127,83 +125,95 @@ def tile_list_replay_action_targets_kernel(
                 v_w[a][:, part * PASS : (part + 1) * PASS], tab_w[a][:].bitcast(U32).indirect(entries)
             )
 
-        w4_w = held([P, PASSES * 2 * H], U8, "w4_w")
+        w4_w = placed([P, PASSES * 2 * H], U8, "w4_w", W4)
         regroup(w4_w[:].bitcast(U16), w4_raw[:].rearrange("p a c -> p (a c)").bitcast(U16))
-        v2_rows = held([P, S2], U8, "v2_rows")
-        nc.vector.tensor_copy(v2_rows[:], tab2_s[:].bitcast(U8).indirect(idx2[:]))
+        tab2_w = placed([P, 2, T2], I32, "tab2_w", TAB2)
+        for half in range(2):
+            load_words(tab2_w[:, half, :], tab2_words[half])
+        w1_raw = [placed([P, PASSES, PACK, PASS], F32, "w1_raw0", RAW0)]
+        for a in range(PASSES):
+            load_w1(w1_raw[0], 0, a)
         gather_states(0, 0)
         gather_states(0, 1)
-        w1_raw.append(held([P, PASSES, PACK, PASS], F32, "w1_raw1", "table"))
+        v2_rows = placed([P, S2], U8, "v2_rows", TAB0)
+        nc.vector.tensor_copy(v2_rows[:], tab2_s[:].bitcast(U8).indirect(idx2[:]))
+        w1_raw.append(placed([P, PASSES, PACK, PASS], F32, "w1_raw1", RAW1))
         for a in range(PASSES):
             load_w1(w1_raw[1], 1, a)
+        identity = placed([P, P], F32, "identity", TAB0 + KIB)
+        make_identity(nc, identity[:])
 
-        w1_w = [[held([P, PASS], U32, f"w1_w{half}{a}") for a in range(PASSES)] for half in range(2)]
-        w1_s = [[held([P, PASS], U8, f"w1_s{half}{a}") for a in range(PASSES)] for half in range(2)]
-        grouped = [
-            [placed([P, PACK * PASS], BF16, f"grouped{half}{a}", (2 * PACK + 2 * half + a) * 2 * PACK * PASS) for a in range(PASSES)]
-            for half in range(2)
-        ]
-        v2_w = [held([P, S2], U32, f"v2_w{half}") for half in range(2)]
+        rounded = {(0, a): placed([P, PACK * PASS], BF16, f"rounded0{a}", ROUNDED + a * 4 * KIB) for a in range(PASSES)}
+        w1_w = [held([P, PASSES * PASS], U32, f"w1_w{half}") for half in range(2)]
+        w1_s = [held([P, PASSES * PASS], U8, f"w1_s{half}") for half in range(2)]
         elu = {quad: held([P, PACK, PASS], F32, f"elu{quad[0]}{quad[1]}") for quad in QUADS}
         h = {quad: held([P, PACK * PASS], BF16, f"h{quad[0]}{quad[1]}") for quad in QUADS}
-        h_w = {quad: held([P, PASS], U32, f"h_w{quad[0]}{quad[1]}") for quad in QUADS}
-        h_s = {quad: held([P, PASS], U8, f"h_s{quad[0]}{quad[1]}") for quad in QUADS}
-
-        products = {}
         scaled = {}
+        gates = {}
+        sums = {}
+        products = {}
 
-        def w1_views(half, a):
-            src = w1_raw[half][:, a].rearrange("p i (m u e) -> p u m i e", u=2, e=2)
-            dst = grouped[half][a][:].rearrange("p (u e m i) -> p u m i e", u=2, e=2, i=PACK)
-            return dst, src
+        def round_early(a):
+            src = w1_raw[0][:, a].rearrange("p i (m u e) -> p u m i e", u=2, e=2)
+            dst = rounded[0, a][:].rearrange("p (u e m i) -> p u m i e", u=2, e=2, i=PACK)
+            nc.vector.tensor_copy(dst, src)
 
-        def quantise_w1(half, a):
-            nc.vector.quantize_mx(
-                out=w1_w[half][a][:].bitcast(FP8X4), scales=w1_s[half][a][:], in_=grouped[half][a][:]
-            )
+        def quantise_early(a):
+            cols = slice(a * PASS, (a + 1) * PASS)
+            nc.vector.quantize_mx(out=w1_w[0][:, cols].bitcast(FP8X4), scales=w1_s[0][:, cols], in_=rounded[0, a][:])
 
-        def gate(n, ring=GATE_RING):
+        def gate(n, number):
             half, part = QUADS[n // PACK]
             t = n % PACK
             first = half * PASS + P * t
             states = slice(part * PASS, (part + 1) * PASS)
-            b = bank([P, PASS], "b", ring)
+            b = bank([P, PASS], "b", number)
             mx_sum(
-                b[:],
                 [
                     (
+                        b[:],
                         w4_w[:, 2 * (a * H + first) : 2 * (a * H + first + P)].bitcast(FP4X4),
                         w4_s[a][:, first : first + P],
                         v_w[a][:, states].bitcast(FP8X4),
                         v_s[a][:, states],
                     )
                     for a in range(PASSES)
-                ],
+                ]
             )
             clamped = work.tile([P, PASS], F32, name="clamped")
-            grown = work.tile([P, PASS], F32, name="grown", bufs=6)
+            grown = work.tile([P, PASS], F32, name="grown", bufs=8)
             nc.scalar.activation(clamped[:], b[:], ACT.Relu, scale=-1.0)
             nc.scalar.activation(grown[:], clamped[:], ACT.Exp, scale=-1.0)
-            nc.vector.scalar_tensor_tensor(elu[half, part][:, t, :], grown[:], -1.0, b[:], ALU.add, ALU.max)
+            gates[n] = (b, grown)
 
-        def hidden(n, ring=LINEAR_RING):
+        def merge(n):
+            b, grown = gates[n]
+            nc.vector.scalar_tensor_tensor(elu[QUADS[n // PACK]][:, n % PACK, :], grown[:], -1.0, b[:], ALU.add, ALU.max)
+
+        def linear(n, number):
             half, part = QUADS[n // PACK]
             in_part = n % PACK
             states = slice(part * PASS + in_part * P, part * PASS + (in_part + 1) * P)
-            acc = bank([P, PACK, P], "acc", ring)
+            acc = bank([P, PACK, P], "acc", number)
             for t in range(PACK):
                 mx_sum(
-                    acc[:, t, :],
                     [
                         (
-                            w1_w[half][a][:, P * t : P * (t + 1)].bitcast(FP8X4),
-                            w1_s[half][a][:, P * t : P * (t + 1)],
+                            acc[:, t, :],
+                            w1_w[half][:, a * PASS + P * t : a * PASS + P * (t + 1)].bitcast(FP8X4),
+                            w1_s[half][:, a * PASS + P * t : a * PASS + P * (t + 1)],
                             v_w[a][:, states].bitcast(FP8X4),
                             v_s[a][:, states],
                         )
                         for a in (1, 0)
-                    ],
+                    ]
                 )
+            sums[n] = acc
+
+        def product(n):
+            half, part = QUADS[n // PACK]
+            in_part = n % PACK
+            acc = sums[n]
             nc.vector.tensor_tensor(
                 h[half, part][:, in_part * PASS : (in_part + 1) * PASS].rearrange("p (c e t) -> p c t e", e=4, t=PACK),
                 acc[:].rearrange("p t (c e) -> p c t e", e=4),
@@ -218,136 +228,195 @@ def tile_list_replay_action_targets_kernel(
                 in_=h[quad][:, first * PASS : (first + count) * PASS],
             )
 
-        def targets_by_state(chunk, ring=SPARE_RING):
+        def targets_by_state(chunk, number):
             part, in_part = divmod(chunk, PACK)
             states = slice(in_part * P, (in_part + 1) * P)
-            q = bank([P, S2], "q", ring)
+            q = bank([P, S2], "q", number)
             mx_sum(
-                q[:],
                 [
                     (
+                        q[:],
                         h_w[half, part][:, states].bitcast(FP8X4),
                         h_s[half, part][:, states],
                         v2_w[half][:].bitcast(FP8X4),
                         v2_s[4 * half : P, :],
                     )
                     for half in (1, 0)
-                ],
+                ]
             )
             scaled[chunk] = work.tile([P, S2], F32, name="scaled", bufs=6)
             factor = per_state[:, 0, chunk : chunk + 1]
             offset = per_state[:, 1, chunk : chunk + 1]
             nc.scalar.activation(scaled[chunk][:], q[:], ACT.Identity, bias=offset, scale=factor)
 
-        def turn_and_store(first, ring=SPARE_RING):
+        def turn_pair(first, numbers, engines=(nc.scalar.copy, nc.scalar.copy)):
             for pair in range(2):
-                turned = bank([P, 2, 2, P], "turned", ring)
+                turned = bank([P, 2, 2, P], "turned", numbers[pair])
                 for i in range(2):
                     actions = slice((2 * pair + i) * P, (2 * pair + i + 1) * P)
                     for e in range(2):
                         nc.tensor.transpose(turned[:, i, e, :], scaled[first + e][:, actions], identity[:])
                 result = work.tile([P, 2, 2 * P], F32, name="result", bufs=8)
-                nc.scalar.copy(result[:], turned[:].rearrange("p i e j -> p i (e j)"))
+                engines[pair](result[:], turned[:].rearrange("p i e j -> p i (e j)"))
                 block = out[2 * pair * P : 2 * (pair + 1) * P, first * P : (first + 2) * P]
                 nc.sync.dma_start(out=block.rearrange("(i p) j -> p i j", p=P), in_=result[:])
 
-        by_action = [P, 2, 2 * P]
+        def turn_one(chunk, number, engine=nc.scalar.copy):
+            turned = bank([P, PACK, P], "turned", number)
+            for i in range(PACK):
+                nc.tensor.transpose(turned[:, i, :], scaled[chunk][:, i * P : (i + 1) * P], identity[:])
+            result = work.tile([P, PACK, P], F32, name="result", bufs=8)
+            engine(result[:], turned[:])
+            block = out[:, chunk * P : (chunk + 1) * P]
+            nc.sync.dma_start(out=block.rearrange("(i p) j -> p i j", p=P), in_=result[:])
 
-        def targets_by_action(first, pair, ring=GATE_RING):
-            states = slice((first - PACK) * P, (first - PACK + 2) * P)
-            spread_states = slice((first - TURNED) * P, (first - TURNED + 2) * P)
-            q = bank(by_action, "q", ring)
-            for i in range(2):
-                actions = slice((2 * pair + i) * P, (2 * pair + i + 1) * P)
+        def values_by_action(first, count, tile0, number):
+            shape = [P, PACK // count, count * P]
+            states = slice((first - PACK) * P, (first - PACK + count) * P)
+            q = bank(shape, "q", number)
+            for i in range(PACK // count):
+                actions = slice((tile0 + i) * P, (tile0 + i + 1) * P)
                 mx_sum(
-                    q[:, i, :],
                     [
                         (
+                            q[:, i, :],
                             v2_w[half][:, actions].bitcast(FP8X4),
                             v2_s[4 * half : P, actions],
                             h_w[half, 1][:, states].bitcast(FP8X4),
                             h_s[half, 1][:, states],
                         )
                         for half in (1, 0)
-                    ],
+                    ]
                 )
-            discounted = work.tile(by_action, F32, name="scaled", bufs=6)
-            nc.vector.tensor_tensor(discounted[:], q[:], spread[:, 0, spread_states].unsqueeze(1).to_broadcast(by_action), ALU.mult)
-            products[first, pair] = discounted
+            spread_states = slice((first - TURNED) * P, (first - TURNED + count) * P)
+            discounted = work.tile(shape, F32, name="scaled", bufs=6)
+            nc.vector.tensor_tensor(discounted[:], q[:], spread[:, 0, spread_states].unsqueeze(1).to_broadcast(shape), ALU.mult)
+            products[first, tile0] = discounted
 
-        def reward_and_store(first, pair):
-            result = work.tile(by_action, F32, name="result", bufs=8)
-            offset = spread[:, 1, (first - TURNED) * P : (first - TURNED + 2) * P].unsqueeze(1).to_broadcast(by_action)
-            nc.vector.tensor_tensor(result[:], products[first, pair][:], offset, ALU.add)
-            block = out[2 * pair * P : 2 * (pair + 1) * P, first * P : (first + 2) * P]
+        def reward_and_store(first, count, tile0, engine=nc.vector):
+            shape = [P, PACK // count, count * P]
+            result = work.tile(shape, F32, name="result", bufs=8)
+            offset = spread[:, 1, (first - TURNED) * P : (first - TURNED + count) * P].unsqueeze(1).to_broadcast(shape)
+            engine.tensor_tensor(result[:], products[first, tile0][:], offset, ALU.add)
+            block = out[tile0 * P : (tile0 + PACK // count) * P, first * P : (first + count) * P]
             nc.sync.dma_start(out=block.rearrange("(i p) j -> p i j", p=P), in_=result[:])
 
         gather_states(1, 0)
         gather_states(1, 1)
-        tab2_w = placed([P, 2, T2], I32, "tab2_w", 0)
-        nc.sync.dma_start(out=tab2_w[:], in_=tab2_words.rearrange("a p t i -> p a (t i)").bitcast(I32))
-        per_state = placed([P, 2, 2 * PACK], F32, "per_state", TABLE_BYTES // 2)
-        spread = placed([P, 2, S - TURNED * P], F32, "spread", TABLE_BYTES // 2 + 64)
-        for n, values in enumerate((discount, reward)):
+        per_state = placed([P, 2, 2 * PACK], F32, "per_state", TAB1 + 8 * KIB)
+        spread = placed([P, 2, S - TURNED * P], F32, "spread", TAB1 + 8 * KIB + 64)
+        for n, row in enumerate((discount, reward)):
             with nc.allow_non_contiguous_dma(reason="one value a partition for each chunk"):
-                nc.sync.dma_start(out=per_state[:, n, 0:TURNED], in_=values[0 : TURNED * P].rearrange("(c p) -> p c", p=P))
-            nc.sync.dma_start(out=spread[:, n, :], in_=values[TURNED * P :].partition_broadcast(P))
-
-        for a in range(PASSES):
-            nc.vector.tensor_copy(*w1_views(0, a))
-            gate(a, SPARE_RING)
-            quantise_w1(0, a)
-        gate(2, LINEAR_RING)
-        gate(3, LINEAR_RING)
-        identity = placed([P, P], F32, "identity", 2 * TABLE_BYTES + 2 * PACK * PASS)
-        v2_plane = placed([P, S2 // 4], I32, "v2_plane", 2 * TABLE_BYTES + 3 * PACK * PASS)
-        nc.gpsimd.memset(v2_plane[:], 0)
-        make_identity(nc, identity[:])
+                nc.sync.dma_start(out=per_state[:, n, 0:TURNED], in_=row[0 : TURNED * P].rearrange("(c p) -> p c", p=P))
+            nc.sync.dma_start(out=spread[:, n, :], in_=row[TURNED * P :].partition_broadcast(P))
+        v2_plane = placed([P, S2 // 4], I32, "v2_plane", TAB1 + 14 * KIB)
+        nc.vector.memset(v2_plane[:], 0)
         for a in range(PASSES):
             for quadrant in range(4):
                 move_rows(v2_plane, QUADRANT * quadrant + 4 * a, v2_rows[:].bitcast(I32), 16 * a + 4 * quadrant)
         v2_s = v2_plane[:].bitcast(U8)
-        for n in range(PACK, 3 * PACK):
-            gate(n)
-            hidden(n - PACK)
-            if n % PACK == PACK - 1:
-                quantise_h(QUADS[n // PACK - 1], 0, PACK)
-            if FIRST_LATE_CAST <= n < FIRST_LATE_CAST + 2 * PASSES:
-                a, u = divmod(n - FIRST_LATE_CAST, 2)
-                dst, src = w1_views(1, a)
-                nc.scalar.copy(dst[:, u], src[:, u])
-                if u == 1:
-                    quantise_w1(1, a)
-            if n in ACTION_GATES:
-                half = ACTION_GATES.index(n)
-                nc.vector.tensor_copy(v2_w[half][:], tab2_w[:, half, :].bitcast(U32).indirect(idx2[:]))
-        gate(12, SPARE_RING)
-        hidden(8, LINEAR_RING)
-        hidden(9, LINEAR_RING)
-        gate(13, SPARE_RING)
+
+        def round_late(a):
+            src = w1_raw[1][:, a].rearrange("p i (m t) -> p m t i", t=PACK)
+            dst = rounded_late[:, a * PACK * PASS : (a + 1) * PACK * PASS].rearrange("p (t m i) -> p m t i", t=PACK, i=PACK)
+            nc.gpsimd.tensor_scalar(dst, src, 1.0, 0.0, ALU.mult, ALU.add)
+
+        def gather_actions(half):
+            nc.vector.tensor_copy(v2_w[half][:], tab2_w[:, half, :].bitcast(U32).indirect(idx2[:]))
+
+        v2_w = [held([P, S2], U32, f"v2_w{half}") for half in range(2)]
+        gate(0, 0)
+        gate(1, 1)
+        gate(2, 2)
+        gate(3, 3)
+        gate(4, 4)
+        gate(5, 5)
+        gate(6, 6)
+        gate(7, 7)
+        gather_actions(0)
+        gather_actions(1)
+        merge(0)
+        merge(1)
+        round_early(0)
+        merge(2)
+        quantise_early(0)
+        round_early(1)
+        merge(3)
+        quantise_early(1)
+        rounded_late = placed([P, PASSES * PACK * PASS], BF16, "rounded_late", ROUNDED)
+        for a in range(PASSES):
+            round_late(a)
+        h_w = {quad: placed([P, PASS], U32, f"h_w{n}", RAW1 + n * 2 * KIB) for n, quad in enumerate(QUADS)}
+        h_s = {quad: held([P, PASS], U8, f"h_s{n}") for n, quad in enumerate(QUADS)}
+        gate(8, 3)
+        linear(0, 0)
+        linear(1, 1)
+        linear(2, 2)
+        merge(4)
+        gate(9, 4)
+        merge(5)
+        gate(10, 5)
+        product(0)
+        linear(3, 0)
+        merge(6)
+        gate(11, 6)
+        product(1)
+        linear(4, 1)
+        merge(7)
+        gate(12, 7)
+        product(2)
+        linear(5, 2)
+        merge(8)
+        gate(13, 3)
+        product(3)
+        linear(6, 0)
+        merge(9)
+        gate(14, 4)
+        product(4)
+        nc.vector.quantize_mx(out=w1_w[1][:].bitcast(FP8X4), scales=w1_s[1][:], in_=rounded_late[:])
+        linear(8, 1)
+        merge(10)
+        linear(9, 5)
+        merge(11)
+        linear(10, 6)
+        product(5)
+        linear(11, 2)
+        quantise_h(QUADS[0], 0, 4)
+        product(8)
+        gate(15, 1)
+        product(9)
+        merge(12)
         quantise_h(QUADS[2], 0, 2)
-        hidden(10, LINEAR_RING)
-        gate(14, GATE_RING)
-        hidden(11, LINEAR_RING)
-        gate(15, GATE_RING)
+        targets_by_state(0, 5)
+        targets_by_state(1, 7)
+        product(10)
+        linear(7, 6)
+        product(11)
+        linear(12, 2)
+        product(6)
         quantise_h(QUADS[2], 2, 2)
-        targets_by_state(0, GATE_RING)
-        targets_by_state(1, SPARE_RING)
-        hidden(12, LINEAR_RING)
-        hidden(13, LINEAR_RING)
-        targets_by_state(2, SPARE_RING)
-        targets_by_state(3, GATE_RING)
+        linear(13, 0)
+        merge(13)
+        targets_by_state(2, 3)
+        turn_pair(0, (5, 7))
+        merge(14)
+        targets_by_state(3, 4)
+        product(7)
+        linear(14, 6)
+        merge(15)
+        linear(15, 1)
+        quantise_h(QUADS[1], 0, 4)
+        product(12)
+        product(13)
+        turn_pair(2, (3, 4))
+        product(14)
         quantise_h(QUADS[3], 0, 2)
-        hidden(14, LINEAR_RING)
-        hidden(15, LINEAR_RING)
-        turn_and_store(0, GATE_RING)
-        targets_by_action(4, 0, LINEAR_RING)
-        targets_by_action(4, 1, LINEAR_RING)
+        targets_by_state(4, 2)
+        targets_by_state(5, 0)
+        product(15)
         quantise_h(QUADS[3], 2, 2)
-        turn_and_store(2, SPARE_RING)
-        reward_and_store(4, 0)
-        targets_by_action(6, 0, GATE_RING)
-        reward_and_store(4, 1)
-        targets_by_action(6, 1, LINEAR_RING)
-        reward_and_store(6, 0)
-        reward_and_store(6, 1)
+        values_by_action(6, 2, 0, 5)
+        values_by_action(6, 2, 2, 7)
+        turn_pair(4, (2, 0))
+        reward_and_store(6, 2, 0)
+        reward_and_store(6, 2, 2)

@@ -28,7 +28,6 @@ CHUNKS = S // P
 KIB = 1024
 
 QUADS = [(half, part) for half in range(2) for part in range(2)]
-MOVES_AHEAD = 3
 TURNED = 6
 
 
@@ -71,7 +70,7 @@ def tile_list_replay_action_targets_kernel(
             nc.sync.dma_start(out=dst, in_=words.rearrange("p t i -> p (t i)").bitcast(I32))
 
         def move_rows(dst, to, src, start):
-            nc.sync.dma_start(out=dst[to : to + 4, :], in_=src[start : start + 4, :])
+            nc.sync.dma_start(out=dst[to:P:QUADRANT, :], in_=src[start : start + 13 : 4, :])
 
         def load_rows(dst, scales, engine):
             nc.sync.dma_start(out=dst[0:SCALE_ROWS, :], in_=scales.bitcast(I32).rearrange("a q c -> (a q) c"))
@@ -84,37 +83,38 @@ def tile_list_replay_action_targets_kernel(
                 src.rearrange("p (r m t) -> p r t m", t=PACK, m=P),
             )
 
-        TAB0, TAB1, PLANE1, W4, TAB2, RAW0, RAW1, ROUNDED = 0, 16 * KIB, 32 * KIB, 34 * KIB, 38 * KIB, 46 * KIB, 62 * KIB, 78 * KIB
+        RAW1, TAB0, TAB1, PLANE1, SMALL, W4 = 0, KIB, 17 * KIB, 33 * KIB, 35 * KIB, 36 * KIB
+        TAB2, RAW0, ROUNDED = 40 * KIB, 48 * KIB, 64 * KIB
 
         idx = keep.tile([P, S // LIST_ROWS], U16, name="idx")
         idx2 = keep.tile([P, S2 // LIST_ROWS], U16, name="idx2")
         tab_s = held([P, T // 4], I32, "tab_s")
-        tab2_s = placed([P, T2 // 4], I32, "tab2_s", RAW1)
         w4_raw_s = held([P, H // 4], I32, "w4_raw_s")
         w4_raw = placed([P, PASSES, H // 2], I32, "w4_raw", RAW0 - 2 * KIB)
         tab_w = [placed([P, T], I32, "tab_w0", TAB0)]
+        tab2_s = held([P, T2 // 4], I32, "tab2_s")
         planes = [held([P, (S + H) // 4], I32, "planes0")]
 
         nc.sync.dma_start(idx[:], offs)
-        load_rows(w4_raw_s, w4_scales, nc.vector)
         load_rows(tab_s, tab_scales, nc.vector)
+        load_rows(w4_raw_s, w4_scales, nc.vector)
         nc.sync.dma_start(idx2[:], offs2)
         load_rows(tab2_s, tab2_scales, nc.gpsimd)
         nc.sync.dma_start(out=w4_raw[:], in_=w4_words.bitcast(I32).rearrange("a p c -> p a c"))
         load_words(tab_w[0][:], tab_words[0])
 
-        v_rows = placed([P, 3 * S], U8, "v_rows", PLANE1 - S // 2)
-        regroup(planes[0][:].bitcast(U8)[:, S:], w4_raw_s[:].bitcast(U8))
+        v_rows = placed([P, 4 * S], U8, "v_rows", PLANE1 - S // 2)
         nc.vector.tensor_copy(v_rows[:, 0:S], tab_s[:].bitcast(U8).indirect(idx[:]))
+        regroup(planes[0][:].bitcast(U8)[:, S:], w4_raw_s[:].bitcast(U8))
         nc.vector.tensor_copy(planes[0][:, 0 : S // 4], v_rows[:, 0:S].bitcast(I32))
         planes.append(placed([P, (S + H) // 4], I32, "planes1", PLANE1))
         nc.vector.memset(planes[1][:], 0)
         tab_w.append(placed([P, T], I32, "tab_w1", TAB1))
-        for group in range(1, 8):
-            a, quadrant = divmod(group, 4)
-            move_rows(planes[a], QUADRANT * quadrant, planes[0], 4 * group)
-            if group == MOVES_AHEAD:
-                load_words(tab_w[1][:], tab_words[1])
+        for quadrant in range(1, 4):
+            nc.sync.dma_start(out=planes[0][QUADRANT * quadrant : QUADRANT * quadrant + 4, :], in_=planes[0][4 * quadrant : 4 * quadrant + 4, :])
+        load_words(tab_w[1][:], tab_words[1])
+        for row in range(4):
+            move_rows(planes[1], row, planes[0], 16 + row)
         v_s = [plane[:].bitcast(U8)[:, 0:S] for plane in planes]
         w4_s = [plane[:].bitcast(U8)[:, S:] for plane in planes]
         v_w = [held([P, S], U32, f"v_w{a}") for a in range(PASSES)]
@@ -135,32 +135,38 @@ def tile_list_replay_action_targets_kernel(
             load_w1(w1_raw[0], 0, a)
         gather_states(0, 0)
         gather_states(0, 1)
-        v2_rows = placed([P, S2], U8, "v2_rows", TAB0)
+        v2_rows = held([P, S2], U8, "v2_rows")
         nc.vector.tensor_copy(v2_rows[:], tab2_s[:].bitcast(U8).indirect(idx2[:]))
         w1_raw.append(placed([P, PASSES, PACK, PASS], F32, "w1_raw1", RAW1))
         for a in range(PASSES):
             load_w1(w1_raw[1], 1, a)
-        identity = placed([P, P], F32, "identity", TAB0 + KIB)
+        v2_plane = placed([P, S2 // 4], I32, "v2_plane", TAB1 - KIB)
+        nc.vector.memset(v2_plane[:], 0)
+        for a in range(PASSES):
+            for row in range(4):
+                move_rows(v2_plane, 4 * a + row, v2_rows[:].bitcast(I32), 16 * a + row)
+        identity = placed([P, P], F32, "identity", SMALL + KIB // 2)
         make_identity(nc, identity[:])
 
         rounded = {(0, a): placed([P, PACK * PASS], BF16, f"rounded0{a}", ROUNDED + a * 4 * KIB) for a in range(PASSES)}
         w1_w = [held([P, PASSES * PASS], U32, f"w1_w{half}") for half in range(2)]
         w1_s = [held([P, PASSES * PASS], U8, f"w1_s{half}") for half in range(2)]
         elu = {quad: held([P, PACK, PASS], F32, f"elu{quad[0]}{quad[1]}") for quad in QUADS}
-        h = {quad: held([P, PACK * PASS], BF16, f"h{quad[0]}{quad[1]}") for quad in QUADS}
+        h = [held([P, 2 * PASS], BF16, f"h{chunk}") for chunk in range(CHUNKS)]
         scaled = {}
         gates = {}
+        sums_b = {}
         sums = {}
-        products = {}
+        values = {}
 
         def round_early(a):
             src = w1_raw[0][:, a].rearrange("p i (m u e) -> p u m i e", u=2, e=2)
             dst = rounded[0, a][:].rearrange("p (u e m i) -> p u m i e", u=2, e=2, i=PACK)
             nc.vector.tensor_copy(dst, src)
 
-        def quantise_early(a):
+        def quantise_w1(half, a):
             cols = slice(a * PASS, (a + 1) * PASS)
-            nc.vector.quantize_mx(out=w1_w[0][:, cols].bitcast(FP8X4), scales=w1_s[0][:, cols], in_=rounded[0, a][:])
+            nc.vector.quantize_mx(out=w1_w[half][:, cols].bitcast(FP8X4), scales=w1_s[half][:, cols], in_=rounded[half, a][:])
 
         def gate(n, number):
             half, part = QUADS[n // PACK]
@@ -180,6 +186,10 @@ def tile_list_replay_action_targets_kernel(
                     for a in range(PASSES)
                 ]
             )
+            sums_b[n] = b
+
+        def grow(n):
+            b = sums_b[n]
             clamped = work.tile([P, PASS], F32, name="clamped")
             grown = work.tile([P, PASS], F32, name="grown", bufs=8)
             nc.scalar.activation(clamped[:], b[:], ACT.Relu, scale=-1.0)
@@ -215,29 +225,23 @@ def tile_list_replay_action_targets_kernel(
             in_part = n % PACK
             acc = sums[n]
             nc.vector.tensor_tensor(
-                h[half, part][:, in_part * PASS : (in_part + 1) * PASS].rearrange("p (c e t) -> p c t e", e=4, t=PACK),
+                h[part * PACK + in_part][:, half * PASS : (half + 1) * PASS].rearrange("p (c e t) -> p c t e", e=4, t=PACK),
                 acc[:].rearrange("p t (c e) -> p c t e", e=4),
                 elu[half, part][:, :, in_part * P : (in_part + 1) * P].rearrange("p t (c e) -> p c t e", e=4),
                 ALU.mult,
             )
 
-        def quantise_h(quad, first, count):
-            nc.vector.quantize_mx(
-                out=h_w[quad][:, first * P : (first + count) * P].bitcast(FP8X4),
-                scales=h_s[quad][:, first * P : (first + count) * P],
-                in_=h[quad][:, first * PASS : (first + count) * PASS],
-            )
+        def quantise_h(chunk):
+            nc.vector.quantize_mx(out=h_w[chunk][:].bitcast(FP8X4), scales=h_s[chunk][:], in_=h[chunk][:])
 
         def targets_by_state(chunk, number):
-            part, in_part = divmod(chunk, PACK)
-            states = slice(in_part * P, (in_part + 1) * P)
             q = bank([P, S2], "q", number)
             mx_sum(
                 [
                     (
                         q[:],
-                        h_w[half, part][:, states].bitcast(FP8X4),
-                        h_s[half, part][:, states],
+                        h_w[chunk][:, half * P : (half + 1) * P].bitcast(FP8X4),
+                        h_s[chunk][:, half * P : (half + 1) * P],
                         v2_w[half][:].bitcast(FP8X4),
                         v2_s[4 * half : P, :],
                     )
@@ -254,7 +258,7 @@ def tile_list_replay_action_targets_kernel(
                 turned = bank([P, 2, 2, P], "turned", numbers[pair])
                 for i in range(2):
                     actions = slice((2 * pair + i) * P, (2 * pair + i + 1) * P)
-                    for e in range(2):
+                    for e in (1, 0):
                         nc.tensor.transpose(turned[:, i, e, :], scaled[first + e][:, actions], identity[:])
                 result = work.tile([P, 2, 2 * P], F32, name="result", bufs=8)
                 engines[pair](result[:], turned[:].rearrange("p i e j -> p i (e j)"))
@@ -270,35 +274,36 @@ def tile_list_replay_action_targets_kernel(
             block = out[:, chunk * P : (chunk + 1) * P]
             nc.sync.dma_start(out=block.rearrange("(i p) j -> p i j", p=P), in_=result[:])
 
-        def values_by_action(first, count, tile0, number):
-            shape = [P, PACK // count, count * P]
-            states = slice((first - PACK) * P, (first - PACK + count) * P)
-            q = bank(shape, "q", number)
-            for i in range(PACK // count):
-                actions = slice((tile0 + i) * P, (tile0 + i + 1) * P)
+        def values_by_action(chunk, number):
+            q = bank([P, PACK, P], "q", number)
+            for i in range(PACK):
+                actions = slice(i * P, (i + 1) * P)
                 mx_sum(
                     [
                         (
                             q[:, i, :],
                             v2_w[half][:, actions].bitcast(FP8X4),
                             v2_s[4 * half : P, actions],
-                            h_w[half, 1][:, states].bitcast(FP8X4),
-                            h_s[half, 1][:, states],
+                            h_w[chunk][:, half * P : (half + 1) * P].bitcast(FP8X4),
+                            h_s[chunk][:, half * P : (half + 1) * P],
                         )
-                        for half in (1, 0)
+                        for half in range(2)
                     ]
                 )
-            spread_states = slice((first - TURNED) * P, (first - TURNED + count) * P)
-            discounted = work.tile(shape, F32, name="scaled", bufs=6)
-            nc.vector.tensor_tensor(discounted[:], q[:], spread[:, 0, spread_states].unsqueeze(1).to_broadcast(shape), ALU.mult)
-            products[first, tile0] = discounted
+            values[chunk] = q
 
-        def reward_and_store(first, count, tile0, engine=nc.vector):
-            shape = [P, PACK // count, count * P]
-            result = work.tile(shape, F32, name="result", bufs=8)
-            offset = spread[:, 1, (first - TURNED) * P : (first - TURNED + count) * P].unsqueeze(1).to_broadcast(shape)
-            engine.tensor_tensor(result[:], products[first, tile0][:], offset, ALU.add)
-            block = out[tile0 * P : (tile0 + PACK // count) * P, first * P : (first + count) * P]
+        def along_states(n, chunk):
+            row = spread[:, n, (chunk - TURNED) * P : (chunk - TURNED + 1) * P]
+            return row.unsqueeze(1).to_broadcast([P, PACK, P])
+
+        def discount_values(chunk):
+            scaled[chunk] = work.tile([P, PACK, P], F32, name="scaled", bufs=6)
+            nc.vector.tensor_tensor(scaled[chunk][:], values[chunk][:], along_states(0, chunk), ALU.mult)
+
+        def reward_and_store(chunk, engine=nc.vector):
+            result = work.tile([P, PACK, P], F32, name="result", bufs=8)
+            engine.tensor_tensor(result[:], scaled[chunk][:], along_states(1, chunk), ALU.add)
+            block = out[:, chunk * P : (chunk + 1) * P]
             nc.sync.dma_start(out=block.rearrange("(i p) j -> p i j", p=P), in_=result[:])
 
         gather_states(1, 0)
@@ -309,16 +314,16 @@ def tile_list_replay_action_targets_kernel(
             with nc.allow_non_contiguous_dma(reason="one value a partition for each chunk"):
                 nc.sync.dma_start(out=per_state[:, n, 0:TURNED], in_=row[0 : TURNED * P].rearrange("(c p) -> p c", p=P))
             nc.sync.dma_start(out=spread[:, n, :], in_=row[TURNED * P :].partition_broadcast(P))
-        v2_plane = placed([P, S2 // 4], I32, "v2_plane", TAB1 + 14 * KIB)
-        nc.vector.memset(v2_plane[:], 0)
-        for a in range(PASSES):
-            for quadrant in range(4):
-                move_rows(v2_plane, QUADRANT * quadrant + 4 * a, v2_rows[:].bitcast(I32), 16 * a + 4 * quadrant)
         v2_s = v2_plane[:].bitcast(U8)
+
+        def round_on_scalar(a, u):
+            src = w1_raw[1][:, a].rearrange("p i (m u e) -> p u m i e", u=2, e=2)
+            dst = rounded[1, a][:].rearrange("p (u e m i) -> p u m i e", u=2, e=2, i=PACK)
+            nc.scalar.copy(dst[:, u], src[:, u])
 
         def round_late(a):
             src = w1_raw[1][:, a].rearrange("p i (m t) -> p m t i", t=PACK)
-            dst = rounded_late[:, a * PACK * PASS : (a + 1) * PACK * PASS].rearrange("p (t m i) -> p m t i", t=PACK, i=PACK)
+            dst = rounded[1, a][:].rearrange("p (t m i) -> p m t i", t=PACK, i=PACK)
             nc.gpsimd.tensor_scalar(dst, src, 1.0, 0.0, ALU.mult, ALU.add)
 
         def gather_actions(half):
@@ -326,97 +331,120 @@ def tile_list_replay_action_targets_kernel(
 
         v2_w = [held([P, S2], U32, f"v2_w{half}") for half in range(2)]
         gate(0, 0)
+        grow(0)
         gate(1, 1)
+        grow(1)
         gate(2, 2)
+        grow(2)
         gate(3, 3)
+        grow(3)
         gate(4, 4)
+        grow(4)
         gate(5, 5)
+        grow(5)
         gate(6, 6)
+        grow(6)
         gate(7, 7)
+        grow(7)
         gather_actions(0)
         gather_actions(1)
         merge(0)
+        gate(8, 0)
+        grow(8)
         merge(1)
+        gate(9, 1)
+        grow(9)
         round_early(0)
         merge(2)
-        quantise_early(0)
-        round_early(1)
+        gate(10, 2)
         merge(3)
-        quantise_early(1)
-        rounded_late = placed([P, PASSES * PACK * PASS], BF16, "rounded_late", ROUNDED)
-        for a in range(PASSES):
-            round_late(a)
-        h_w = {quad: placed([P, PASS], U32, f"h_w{n}", RAW1 + n * 2 * KIB) for n, quad in enumerate(QUADS)}
-        h_s = {quad: held([P, PASS], U8, f"h_s{n}") for n, quad in enumerate(QUADS)}
-        gate(8, 3)
-        linear(0, 0)
-        linear(1, 1)
-        linear(2, 2)
+        gate(11, 3)
+        quantise_w1(0, 0)
+        round_early(1)
         merge(4)
-        gate(9, 4)
+        gate(12, 4)
         merge(5)
-        gate(10, 5)
-        product(0)
-        linear(3, 0)
+        quantise_w1(0, 1)
+        rounded[1, 0] = placed([P, PACK * PASS], BF16, "rounded10", ROUNDED + 4 * KIB)
+        rounded[1, 1] = held([P, PACK * PASS], BF16, "rounded11")
+        h_w = [held([P, 2 * P], U32, f"h_w{chunk}") for chunk in range(CHUNKS)]
+        h_s = [held([P, 2 * P], U8, f"h_s{chunk}") for chunk in range(CHUNKS)]
+        round_late(0)
+        round_on_scalar(1, 0)
+        round_on_scalar(1, 1)
+        grow(10)
+        grow(11)
+        grow(12)
+        linear(0, 5)
         merge(6)
-        gate(11, 6)
-        product(1)
-        linear(4, 1)
+        linear(1, 6)
         merge(7)
-        gate(12, 7)
-        product(2)
-        linear(5, 2)
+        linear(2, 7)
+        product(0)
+        linear(3, 5)
         merge(8)
-        gate(13, 3)
-        product(3)
-        linear(6, 0)
+        gate(13, 0)
+        grow(13)
+        product(1)
+        linear(4, 6)
         merge(9)
-        gate(14, 4)
+        gate(14, 1)
+        product(2)
+        linear(5, 7)
+        product(3)
+        linear(6, 5)
+        quantise_w1(1, 0)
+        quantise_w1(1, 1)
         product(4)
-        nc.vector.quantize_mx(out=w1_w[1][:].bitcast(FP8X4), scales=w1_s[1][:], in_=rounded_late[:])
-        linear(8, 1)
-        merge(10)
-        linear(9, 5)
-        merge(11)
-        linear(10, 6)
+        linear(8, 6)
         product(5)
-        linear(11, 2)
-        quantise_h(QUADS[0], 0, 4)
+        linear(9, 7)
+        merge(10)
+        gate(15, 2)
+        merge(11)
+        linear(10, 3)
         product(8)
-        gate(15, 1)
-        product(9)
+        linear(11, 6)
         merge(12)
-        quantise_h(QUADS[2], 0, 2)
-        targets_by_state(0, 5)
-        targets_by_state(1, 7)
-        product(10)
-        linear(7, 6)
-        product(11)
-        linear(12, 2)
+        quantise_h(0)
+        targets_by_state(0, 4)
+        grow(14)
         product(6)
-        quantise_h(QUADS[2], 2, 2)
-        linear(13, 0)
+        linear(7, 5)
+        product(9)
+        linear(12, 7)
         merge(13)
-        targets_by_state(2, 3)
-        turn_pair(0, (5, 7))
+        quantise_h(1)
+        targets_by_state(1, 0)
+        grow(15)
+        product(10)
+        linear(13, 3)
         merge(14)
-        targets_by_state(3, 4)
+        quantise_h(2)
+        turn_pair(0, (4, 0))
+        targets_by_state(2, 1)
         product(7)
-        linear(14, 6)
+        linear(14, 5)
+        product(11)
+        linear(15, 6)
         merge(15)
-        linear(15, 1)
-        quantise_h(QUADS[1], 0, 4)
+        quantise_h(3)
+        targets_by_state(3, 2)
         product(12)
+        quantise_h(4)
+        targets_by_state(4, 4)
         product(13)
-        turn_pair(2, (3, 4))
-        product(14)
-        quantise_h(QUADS[3], 0, 2)
-        targets_by_state(4, 2)
+        turn_pair(2, (1, 2))
+        quantise_h(5)
         targets_by_state(5, 0)
+        product(14)
+        quantise_h(6)
+        values_by_action(6, 7)
         product(15)
-        quantise_h(QUADS[3], 2, 2)
-        values_by_action(6, 2, 0, 5)
-        values_by_action(6, 2, 2, 7)
-        turn_pair(4, (2, 0))
-        reward_and_store(6, 2, 0)
-        reward_and_store(6, 2, 2)
+        turn_pair(4, (4, 0))
+        quantise_h(7)
+        values_by_action(7, 3)
+        discount_values(6)
+        reward_and_store(6)
+        discount_values(7)
+        reward_and_store(7)

@@ -29,6 +29,8 @@ KIB = 1024
 
 QUADS = [(half, part) for half in range(2) for part in range(2)]
 TURNED = 6
+BATCHES = [(chunk, 1) for chunk in range(CHUNKS)]
+BATCH_OF = {first + n: (first, count) for first, count in BATCHES for n in range(count)}
 
 
 def tile_list_replay_action_targets_kernel(
@@ -84,7 +86,7 @@ def tile_list_replay_action_targets_kernel(
             )
 
         RAW1, TAB0, TAB1, PLANE1, SMALL, W4 = 0, KIB, 17 * KIB, 33 * KIB, 35 * KIB, 36 * KIB
-        TAB2, RAW0, ROUNDED = 40 * KIB, 48 * KIB, 64 * KIB
+        TAB2, RAW0, ROUNDED, FIRST_ELU = 40 * KIB, 48 * KIB, 64 * KIB, 72 * KIB
 
         idx = keep.tile([P, S // LIST_ROWS], U16, name="idx")
         idx2 = keep.tile([P, S2 // LIST_ROWS], U16, name="idx2")
@@ -145,14 +147,16 @@ def tile_list_replay_action_targets_kernel(
         for a in range(PASSES):
             for row in range(4):
                 move_rows(v2_plane, 4 * a + row, v2_rows[:].bitcast(I32), 16 * a + row)
+
         identity = placed([P, P], F32, "identity", SMALL + KIB // 2)
         make_identity(nc, identity[:])
 
         rounded = {(0, a): placed([P, PACK * PASS], BF16, f"rounded0{a}", ROUNDED + a * 4 * KIB) for a in range(PASSES)}
-        w1_w = [held([P, PASSES * PASS], U32, f"w1_w{half}") for half in range(2)]
+        w1_w = [held([P, PASSES * PASS], U32, "w1_w0")]
         w1_s = [held([P, PASSES * PASS], U8, f"w1_s{half}") for half in range(2)]
-        elu = {quad: held([P, PACK, PASS], F32, f"elu{quad[0]}{quad[1]}") for quad in QUADS}
-        h = [held([P, 2 * PASS], BF16, f"h{chunk}") for chunk in range(CHUNKS)]
+        elu = {quad: held([P, PACK, PASS], F32, f"elu{quad[0]}{quad[1]}") for quad in QUADS[1:]}
+        elu[QUADS[0]] = placed([P, PACK, PASS], F32, "elu00", FIRST_ELU)
+        h = {first: held([P, 2 * count * PASS], BF16, f"h{first}") for first, count in BATCHES}
         scaled = {}
         gates = {}
         sums_b = {}
@@ -224,8 +228,10 @@ def tile_list_replay_action_targets_kernel(
             half, part = QUADS[n // PACK]
             in_part = n % PACK
             acc = sums[n]
+            first, count = BATCH_OF[part * PACK + in_part]
+            place = half * count + part * PACK + in_part - first
             nc.vector.tensor_tensor(
-                h[part * PACK + in_part][:, half * PASS : (half + 1) * PASS].rearrange("p (c e t) -> p c t e", e=4, t=PACK),
+                h[first][:, place * PASS : (place + 1) * PASS].rearrange("p (c e t) -> p c t e", e=4, t=PACK),
                 acc[:].rearrange("p t (c e) -> p c t e", e=4),
                 elu[half, part][:, :, in_part * P : (in_part + 1) * P].rearrange("p t (c e) -> p c t e", e=4),
                 ALU.mult,
@@ -235,20 +241,21 @@ def tile_list_replay_action_targets_kernel(
             nc.vector.quantize_mx(out=h_w[chunk][:].bitcast(FP8X4), scales=h_s[chunk][:], in_=h[chunk][:])
 
         def targets_by_state(chunk, number):
+            first, count = BATCH_OF[chunk]
             q = bank([P, S2], "q", number)
             mx_sum(
                 [
                     (
                         q[:],
-                        h_w[chunk][:, half * P : (half + 1) * P].bitcast(FP8X4),
-                        h_s[chunk][:, half * P : (half + 1) * P],
+                        h_w[first][:, (half * count + chunk - first) * P : (half * count + chunk - first + 1) * P].bitcast(FP8X4),
+                        h_s[first][:, (half * count + chunk - first) * P : (half * count + chunk - first + 1) * P],
                         v2_w[half][:].bitcast(FP8X4),
                         v2_s[4 * half : P, :],
                     )
                     for half in (1, 0)
                 ]
             )
-            scaled[chunk] = work.tile([P, S2], F32, name="scaled", bufs=6)
+            scaled[chunk] = work.tile([P, S2], F32, name="scaled")
             factor = per_state[:, 0, chunk : chunk + 1]
             offset = per_state[:, 1, chunk : chunk + 1]
             nc.scalar.activation(scaled[chunk][:], q[:], ACT.Identity, bias=offset, scale=factor)
@@ -260,7 +267,7 @@ def tile_list_replay_action_targets_kernel(
                     actions = slice((2 * pair + i) * P, (2 * pair + i + 1) * P)
                     for e in (1, 0):
                         nc.tensor.transpose(turned[:, i, e, :], scaled[first + e][:, actions], identity[:])
-                result = work.tile([P, 2, 2 * P], F32, name="result", bufs=8)
+                result = work.tile([P, 2, 2 * P], F32, name="result", bufs=6)
                 engines[pair](result[:], turned[:].rearrange("p i e j -> p i (e j)"))
                 block = out[2 * pair * P : 2 * (pair + 1) * P, first * P : (first + 2) * P]
                 nc.sync.dma_start(out=block.rearrange("(i p) j -> p i j", p=P), in_=result[:])
@@ -269,41 +276,45 @@ def tile_list_replay_action_targets_kernel(
             turned = bank([P, PACK, P], "turned", number)
             for i in range(PACK):
                 nc.tensor.transpose(turned[:, i, :], scaled[chunk][:, i * P : (i + 1) * P], identity[:])
-            result = work.tile([P, PACK, P], F32, name="result", bufs=8)
+            result = work.tile([P, PACK, P], F32, name="result", bufs=6)
             engine(result[:], turned[:])
             block = out[:, chunk * P : (chunk + 1) * P]
             nc.sync.dma_start(out=block.rearrange("(i p) j -> p i j", p=P), in_=result[:])
 
-        def values_by_action(chunk, number):
-            q = bank([P, PACK, P], "q", number)
-            for i in range(PACK):
-                actions = slice(i * P, (i + 1) * P)
+        def values_by_action(first, tile0, number):
+            count = BATCH_OF[first][1]
+            q = bank([P, PACK // count, count * P], "q", number)
+            for i in range(PACK // count):
+                actions = slice((tile0 + i) * P, (tile0 + i + 1) * P)
                 mx_sum(
                     [
                         (
                             q[:, i, :],
                             v2_w[half][:, actions].bitcast(FP8X4),
                             v2_s[4 * half : P, actions],
-                            h_w[chunk][:, half * P : (half + 1) * P].bitcast(FP8X4),
-                            h_s[chunk][:, half * P : (half + 1) * P],
+                            h_w[first][:, half * count * P : (half + 1) * count * P].bitcast(FP8X4),
+                            h_s[first][:, half * count * P : (half + 1) * count * P],
                         )
                         for half in range(2)
                     ]
                 )
-            values[chunk] = q
+            values[first, tile0] = q
 
-        def along_states(n, chunk):
-            row = spread[:, n, (chunk - TURNED) * P : (chunk - TURNED + 1) * P]
-            return row.unsqueeze(1).to_broadcast([P, PACK, P])
+        def along_states(n, first):
+            count = BATCH_OF[first][1]
+            row = spread[:, n, (first - TURNED) * P : (first - TURNED + count) * P]
+            return row.unsqueeze(1).to_broadcast([P, PACK // count, count * P])
 
-        def discount_values(chunk):
-            scaled[chunk] = work.tile([P, PACK, P], F32, name="scaled", bufs=6)
-            nc.vector.tensor_tensor(scaled[chunk][:], values[chunk][:], along_states(0, chunk), ALU.mult)
+        def discount_values(first, tile0):
+            count = BATCH_OF[first][1]
+            scaled[first, tile0] = work.tile([P, PACK // count, count * P], F32, name="discounted")
+            nc.vector.tensor_tensor(scaled[first, tile0][:], values[first, tile0][:], along_states(0, first), ALU.mult)
 
-        def reward_and_store(chunk, engine=nc.vector):
-            result = work.tile([P, PACK, P], F32, name="result", bufs=8)
-            engine.tensor_tensor(result[:], scaled[chunk][:], along_states(1, chunk), ALU.add)
-            block = out[:, chunk * P : (chunk + 1) * P]
+        def reward_and_store(first, tile0):
+            count = BATCH_OF[first][1]
+            result = work.tile([P, PACK // count, count * P], F32, name="summed")
+            nc.vector.tensor_tensor(result[:], scaled[first, tile0][:], along_states(1, first), ALU.add)
+            block = out[tile0 * P : (tile0 + PACK // count) * P, first * P : (first + count) * P]
             nc.sync.dma_start(out=block.rearrange("(i p) j -> p i j", p=P), in_=result[:])
 
         gather_states(1, 0)
@@ -357,94 +368,95 @@ def tile_list_replay_action_targets_kernel(
         round_early(0)
         merge(2)
         gate(10, 2)
-        merge(3)
-        gate(11, 3)
         quantise_w1(0, 0)
         round_early(1)
-        merge(4)
-        gate(12, 4)
-        merge(5)
+        merge(3)
         quantise_w1(0, 1)
         rounded[1, 0] = placed([P, PACK * PASS], BF16, "rounded10", ROUNDED + 4 * KIB)
         rounded[1, 1] = held([P, PACK * PASS], BF16, "rounded11")
-        h_w = [held([P, 2 * P], U32, f"h_w{chunk}") for chunk in range(CHUNKS)]
-        h_s = [held([P, 2 * P], U8, f"h_s{chunk}") for chunk in range(CHUNKS)]
+        h_w = {first: held([P, 2 * count * P], U32, f"h_w{first}") for first, count in BATCHES}
+        h_s = {first: held([P, 2 * count * P], U8, f"h_s{first}") for first, count in BATCHES}
         round_late(0)
         round_on_scalar(1, 0)
         round_on_scalar(1, 1)
         grow(10)
-        grow(11)
-        grow(12)
-        linear(0, 5)
+        linear(0, 3)
+        merge(4)
+        linear(1, 4)
+        merge(5)
+        linear(2, 5)
         merge(6)
-        linear(1, 6)
-        merge(7)
-        linear(2, 7)
+        gate(11, 6)
+        grow(11)
         product(0)
-        linear(3, 5)
+        linear(3, 3)
+        merge(7)
+        gate(12, 7)
+        grow(12)
+        product(1)
+        linear(4, 4)
         merge(8)
         gate(13, 0)
         grow(13)
-        product(1)
-        linear(4, 6)
+        product(2)
+        linear(5, 5)
+        product(3)
+        linear(6, 3)
+        w1_w.append(placed([P, PASSES * PASS], U32, "w1_w1", FIRST_ELU))
         merge(9)
         gate(14, 1)
-        product(2)
-        linear(5, 7)
-        product(3)
-        linear(6, 5)
-        quantise_w1(1, 0)
-        quantise_w1(1, 1)
         product(4)
-        linear(8, 6)
+        linear(7, 4)
         product(5)
-        linear(9, 7)
+        quantise_w1(1, 1)
+        quantise_w1(1, 0)
+        linear(8, 5)
         merge(10)
         gate(15, 2)
         merge(11)
+        linear(9, 6)
+        product(6)
         linear(10, 3)
         product(8)
-        linear(11, 6)
+        linear(11, 5)
         merge(12)
         quantise_h(0)
-        targets_by_state(0, 4)
+        targets_by_state(0, 7)
         grow(14)
-        product(6)
-        linear(7, 5)
         product(9)
-        linear(12, 7)
+        linear(12, 6)
         merge(13)
         quantise_h(1)
         targets_by_state(1, 0)
         grow(15)
+        product(7)
+        linear(13, 4)
         product(10)
-        linear(13, 3)
+        linear(14, 3)
         merge(14)
         quantise_h(2)
-        turn_pair(0, (4, 0))
+        turn_pair(0, (7, 0))
         targets_by_state(2, 1)
-        product(7)
-        linear(14, 5)
         product(11)
-        linear(15, 6)
+        linear(15, 5)
         merge(15)
         quantise_h(3)
         targets_by_state(3, 2)
         product(12)
         quantise_h(4)
-        targets_by_state(4, 4)
+        targets_by_state(4, 7)
         product(13)
         turn_pair(2, (1, 2))
         quantise_h(5)
         targets_by_state(5, 0)
         product(14)
         quantise_h(6)
-        values_by_action(6, 7)
+        values_by_action(6, 0, 6)
         product(15)
-        turn_pair(4, (4, 0))
+        turn_pair(4, (7, 0))
         quantise_h(7)
-        values_by_action(7, 3)
-        discount_values(6)
-        reward_and_store(6)
-        discount_values(7)
-        reward_and_store(7)
+        values_by_action(7, 0, 4)
+        discount_values(6, 0)
+        reward_and_store(6, 0)
+        discount_values(7, 0)
+        reward_and_store(7, 0)

@@ -104,6 +104,10 @@ def tile_list_replay_action_targets_kernel(
         load_rows(tab2_s, tab2_scales, nc.gpsimd)
         nc.sync.dma_start(out=w4_raw[:], in_=w4_words.bitcast(I32).rearrange("a p c -> p a c"))
         load_words(tab_w[0][:], tab_words[0])
+        rows = held([P, P], F32, "rows")
+        nc.vector.memset(rows[:], 0.0)
+        for n, values_in in enumerate((discount, reward)):
+            nc.sync.dma_start(out=rows[CHUNKS * n : CHUNKS * n + TURNED, :], in_=values_in[0 : TURNED * P].rearrange("(c p) -> c p", p=P))
 
         v_rows = placed([P, 4 * S], U8, "v_rows", PLANE1 - S // 2)
         nc.vector.tensor_copy(v_rows[:, 0:S], tab_s[:].bitcast(U8).indirect(idx[:]))
@@ -150,6 +154,10 @@ def tile_list_replay_action_targets_kernel(
 
         identity = placed([P, P], F32, "identity", SMALL + KIB // 2)
         make_identity(nc, identity[:])
+        per_state = held([P, 2, CHUNKS], F32, "per_state")
+        columns = bank([P, P], "columns", 7)
+        nc.tensor.transpose(columns[:], rows[:], identity[:])
+        nc.vector.tensor_copy(per_state[:].rearrange("p n c -> p (n c)"), columns[:, 0 : 2 * CHUNKS])
 
         rounded = {(0, a): placed([P, PACK * PASS], BF16, f"rounded0{a}", ROUNDED + a * 4 * KIB) for a in range(PASSES)}
         w1_w = [held([P, PASSES * PASS], U32, "w1_w0")]
@@ -237,6 +245,25 @@ def tile_list_replay_action_targets_kernel(
                 ALU.mult,
             )
 
+        def quantise_half(chunk, half):
+            cols = slice(half * P, (half + 1) * P)
+            nc.vector.quantize_mx(out=h_w[chunk][:, cols].bitcast(FP8X4), scales=h_s[chunk][:, cols], in_=h[chunk][:, half * PASS : (half + 1) * PASS])
+
+        def values_pass(chunk, half, number):
+            if half == 0:
+                values[chunk, 0] = bank([P, PACK, P], "q", number)
+            for i in range(PACK):
+                actions = slice(i * P, (i + 1) * P)
+                nc.tensor.matmul_mx(
+                    out=values[chunk, 0][:, i, :],
+                    lhsT=v2_w[half][:, actions].bitcast(FP8X4),
+                    lhsT_scale=v2_s[4 * half : P, actions],
+                    rhs=h_w[chunk][:, half * P : (half + 1) * P].bitcast(FP8X4),
+                    rhs_scale=h_s[chunk][:, half * P : (half + 1) * P],
+                    start=(half == 0 and i == 0),
+                    stop=(half == 1 and i == PACK - 1),
+                )
+
         def quantise_h(chunk):
             nc.vector.quantize_mx(out=h_w[chunk][:].bitcast(FP8X4), scales=h_s[chunk][:], in_=h[chunk][:])
 
@@ -319,11 +346,8 @@ def tile_list_replay_action_targets_kernel(
 
         gather_states(1, 0)
         gather_states(1, 1)
-        per_state = placed([P, 2, 2 * PACK], F32, "per_state", TAB1 + 8 * KIB)
-        spread = placed([P, 2, S - TURNED * P], F32, "spread", TAB1 + 8 * KIB + 64)
+        spread = placed([P, 2, S - TURNED * P], F32, "spread", TAB1)
         for n, row in enumerate((discount, reward)):
-            with nc.allow_non_contiguous_dma(reason="one value a partition for each chunk"):
-                nc.sync.dma_start(out=per_state[:, n, 0:TURNED], in_=row[0 : TURNED * P].rearrange("(c p) -> p c", p=P))
             nc.sync.dma_start(out=spread[:, n, :], in_=row[TURNED * P :].partition_broadcast(P))
         v2_s = v2_plane[:].bitcast(U8)
 

@@ -28,8 +28,8 @@ CHUNKS = S // P
 KIB = 1024
 
 QUADS = [(half, part) for half in range(2) for part in range(2)]
-TURNED = 6
-BATCHES = [(chunk, 1) for chunk in range(CHUNKS)]
+TURNED = 4
+BATCHES = [(0, 1), (1, 1), (2, 1), (3, 1), (4, 2), (6, 2)]
 BATCH_OF = {first + n: (first, count) for first, count in BATCHES for n in range(count)}
 
 
@@ -308,40 +308,39 @@ def tile_list_replay_action_targets_kernel(
             block = out[:, chunk * P : (chunk + 1) * P]
             nc.sync.dma_start(out=block.rearrange("(i p) j -> p i j", p=P), in_=result[:])
 
-        def values_by_action(first, tile0, number):
-            count = BATCH_OF[first][1]
+        def values_by_action(chunk, count, tile0, number):
+            first, size = BATCH_OF[chunk]
             q = bank([P, PACK // count, count * P], "q", number)
             for i in range(PACK // count):
                 actions = slice((tile0 + i) * P, (tile0 + i + 1) * P)
-                mx_sum(
-                    [
+                passes = []
+                for half in range(2):
+                    place = half * size + chunk - first
+                    states = slice(place * P, (place + count) * P)
+                    passes.append(
                         (
                             q[:, i, :],
                             v2_w[half][:, actions].bitcast(FP8X4),
                             v2_s[4 * half : P, actions],
-                            h_w[first][:, half * count * P : (half + 1) * count * P].bitcast(FP8X4),
-                            h_s[first][:, half * count * P : (half + 1) * count * P],
+                            h_w[first][:, states].bitcast(FP8X4),
+                            h_s[first][:, states],
                         )
-                        for half in range(2)
-                    ]
-                )
-            values[first, tile0] = q
+                    )
+                mx_sum(passes)
+            values[chunk, tile0] = q
 
-        def along_states(n, first):
-            count = BATCH_OF[first][1]
-            row = spread[:, n, (first - TURNED) * P : (first - TURNED + count) * P]
+        def along_states(n, chunk, count):
+            row = spread[:, n, (chunk - TURNED) * P : (chunk - TURNED + count) * P]
             return row.unsqueeze(1).to_broadcast([P, PACK // count, count * P])
 
-        def discount_values(first, tile0):
-            count = BATCH_OF[first][1]
-            scaled[first, tile0] = work.tile([P, PACK // count, count * P], F32, name="discounted")
-            nc.vector.tensor_tensor(scaled[first, tile0][:], values[first, tile0][:], along_states(0, first), ALU.mult)
+        def discount_values(chunk, count, tile0):
+            scaled[chunk, tile0] = work.tile([P, PACK // count, count * P], F32, name="discounted")
+            nc.vector.tensor_tensor(scaled[chunk, tile0][:], values[chunk, tile0][:], along_states(0, chunk, count), ALU.mult)
 
-        def reward_and_store(first, tile0):
-            count = BATCH_OF[first][1]
+        def reward_and_store(chunk, count, tile0):
             result = work.tile([P, PACK // count, count * P], F32, name="summed")
-            nc.vector.tensor_tensor(result[:], scaled[first, tile0][:], along_states(1, first), ALU.add)
-            block = out[tile0 * P : (tile0 + PACK // count) * P, first * P : (first + count) * P]
+            nc.vector.tensor_tensor(result[:], scaled[chunk, tile0][:], along_states(1, chunk, count), ALU.add)
+            block = out[tile0 * P : (tile0 + PACK // count) * P, chunk * P : (chunk + count) * P]
             nc.sync.dma_start(out=block.rearrange("(i p) j -> p i j", p=P), in_=result[:])
 
         gather_states(1, 0)
@@ -392,9 +391,13 @@ def tile_list_replay_action_targets_kernel(
         round_early(0)
         merge(2)
         gate(10, 2)
+        merge(3)
+        gate(11, 3)
         quantise_w1(0, 0)
         round_early(1)
-        merge(3)
+        merge(4)
+        gate(12, 4)
+        merge(5)
         quantise_w1(0, 1)
         rounded[1, 0] = placed([P, PACK * PASS], BF16, "rounded10", ROUNDED + 4 * KIB)
         rounded[1, 1] = held([P, PACK * PASS], BF16, "rounded11")
@@ -404,83 +407,80 @@ def tile_list_replay_action_targets_kernel(
         round_on_scalar(1, 0)
         round_on_scalar(1, 1)
         grow(10)
-        linear(0, 3)
-        merge(4)
-        linear(1, 4)
-        merge(5)
-        linear(2, 5)
-        merge(6)
-        gate(11, 6)
         grow(11)
-        product(0)
-        linear(3, 3)
-        merge(7)
-        gate(12, 7)
         grow(12)
-        product(1)
-        linear(4, 4)
+        linear(0, 5)
+        merge(6)
+        linear(1, 6)
+        merge(7)
+        linear(2, 7)
+        product(0)
+        linear(3, 5)
         merge(8)
         gate(13, 0)
         grow(13)
-        product(2)
-        linear(5, 5)
-        product(3)
-        linear(6, 3)
-        w1_w.append(placed([P, PASSES * PASS], U32, "w1_w1", FIRST_ELU))
+        product(1)
+        linear(4, 6)
         merge(9)
         gate(14, 1)
-        product(4)
-        linear(7, 4)
-        product(5)
-        quantise_w1(1, 1)
+        product(2)
+        linear(5, 7)
+        product(3)
+        linear(6, 5)
+        w1_w.append(placed([P, PASSES * PASS], U32, "w1_w1", FIRST_ELU))
         quantise_w1(1, 0)
-        linear(8, 5)
+        quantise_w1(1, 1)
+        product(4)
+        linear(8, 6)
+        product(5)
+        linear(9, 7)
         merge(10)
         gate(15, 2)
         merge(11)
-        linear(9, 6)
-        product(6)
         linear(10, 3)
+        grow(14)
+        grow(15)
+        product(6)
+        linear(7, 5)
         product(8)
-        linear(11, 5)
+        linear(11, 6)
         merge(12)
+        linear(12, 4)
+        product(9)
         quantise_h(0)
         targets_by_state(0, 7)
-        grow(14)
-        product(9)
-        linear(12, 6)
-        merge(13)
-        quantise_h(1)
-        targets_by_state(1, 0)
-        grow(15)
-        product(7)
-        linear(13, 4)
         product(10)
-        linear(14, 3)
-        merge(14)
-        quantise_h(2)
-        turn_pair(0, (7, 0))
-        targets_by_state(2, 1)
+        quantise_h(1)
+        targets_by_state(1, 3)
         product(11)
-        linear(15, 5)
-        merge(15)
+        quantise_h(2)
+        targets_by_state(2, 6)
+        product(7)
         quantise_h(3)
-        targets_by_state(3, 2)
+        targets_by_state(3, 5)
+        merge(13)
+        linear(13, 0)
+        merge(14)
+        linear(14, 1)
+        merge(15)
+        linear(15, 2)
+        turn_pair(0, (7, 3))
+        turn_pair(2, (6, 5))
         product(12)
-        quantise_h(4)
-        targets_by_state(4, 7)
         product(13)
-        turn_pair(2, (1, 2))
-        quantise_h(5)
-        targets_by_state(5, 0)
         product(14)
-        quantise_h(6)
-        values_by_action(6, 0, 6)
+        quantise_h(4)
+        values_by_action(4, 2, 0, 4)
+        values_by_action(4, 2, 2, 0)
         product(15)
-        turn_pair(4, (7, 0))
-        quantise_h(7)
-        values_by_action(7, 0, 4)
-        discount_values(6, 0)
-        reward_and_store(6, 0)
-        discount_values(7, 0)
-        reward_and_store(7, 0)
+        discount_values(4, 2, 0)
+        quantise_h(6)
+        values_by_action(6, 2, 0, 1)
+        values_by_action(6, 2, 2, 2)
+        discount_values(4, 2, 2)
+        reward_and_store(4, 2, 0)
+        discount_values(6, 2, 0)
+        reward_and_store(4, 2, 2)
+        discount_values(6, 2, 2)
+        reward_and_store(6, 2, 0)
+        reward_and_store(6, 2, 2)

@@ -27,10 +27,19 @@ SCALE_ROWS = 32
 CHUNKS = S // P
 KIB = 1024
 
-QUADS = [(half, part) for half in range(2) for part in range(2)]
 TURNED = 4
-BATCHES = [(0, 1), (1, 1), (2, 1), (3, 1), (4, 2), (6, 2)]
-BATCH_OF = {first + n: (first, count) for first, count in BATCHES for n in range(count)}
+PAIR = 2 * P
+GATES = (
+    [(half, 0, PASS, t, 1) for half in range(2) for t in range(PACK)]
+    + [(half, PASS, PAIR, t, 2) for half in range(2) for t in (0, 2)]
+    + [(half, chunk * P, P, 0, PACK) for half in range(2) for chunk in (6, 7)]
+)
+PRODUCTS = (
+    [(half, chunk) for half in range(2) for chunk in range(4)]
+    + [(half, chunk) for half in range(2) for chunk in (4, 5)]
+    + [(half, chunk) for half in range(2) for chunk in (6, 7)]
+)
+SUMMED = 12
 
 
 def tile_list_replay_action_targets_kernel(
@@ -85,14 +94,14 @@ def tile_list_replay_action_targets_kernel(
                 src.rearrange("p (r m t) -> p r t m", t=PACK, m=P),
             )
 
-        RAW1, TAB0, TAB1, PLANE1, SMALL, W4 = 0, KIB, 17 * KIB, 33 * KIB, 35 * KIB, 36 * KIB
-        TAB2, RAW0, ROUNDED, FIRST_ELU = 40 * KIB, 48 * KIB, 64 * KIB, 72 * KIB
+        RAW1, TAB0, LATE_TAB2, ACTION_PLANE, TAB1, PLANE1, SMALL, W4 = 0, 8 * KIB, 16 * KIB, 20 * KIB, 24 * KIB, 40 * KIB, 42 * KIB, 43 * KIB
+        TAB2, RAW0, ROUNDED, FIRST_ELU, FIRST_H = 47 * KIB, 51 * KIB, 67 * KIB, 75 * KIB, 83 * KIB
 
         idx = keep.tile([P, S // LIST_ROWS], U16, name="idx")
         idx2 = keep.tile([P, S2 // LIST_ROWS], U16, name="idx2")
         tab_s = held([P, T // 4], I32, "tab_s")
         w4_raw_s = held([P, H // 4], I32, "w4_raw_s")
-        w4_raw = placed([P, PASSES, H // 2], I32, "w4_raw", RAW0 - 2 * KIB)
+        w4_raw = placed([P, PASSES, H // 2], I32, "w4_raw", RAW0 - KIB)
         tab_w = [placed([P, T], I32, "tab_w0", TAB0)]
         tab2_s = held([P, T2 // 4], I32, "tab2_s")
         planes = [held([P, (S + H) // 4], I32, "planes0")]
@@ -133,9 +142,8 @@ def tile_list_replay_action_targets_kernel(
 
         w4_w = placed([P, PASSES * 2 * H], U8, "w4_w", W4)
         regroup(w4_w[:].bitcast(U16), w4_raw[:].rearrange("p a c -> p (a c)").bitcast(U16))
-        tab2_w = placed([P, 2, T2], I32, "tab2_w", TAB2)
-        for half in range(2):
-            load_words(tab2_w[:, half, :], tab2_words[half])
+        tab2_w = [placed([P, T2], I32, "tab2_w0", TAB2)]
+        load_words(tab2_w[0][:], tab2_words[0])
         w1_raw = [placed([P, PASSES, PACK, PASS], F32, "w1_raw0", RAW0)]
         for a in range(PASSES):
             load_w1(w1_raw[0], 0, a)
@@ -146,7 +154,9 @@ def tile_list_replay_action_targets_kernel(
         w1_raw.append(placed([P, PASSES, PACK, PASS], F32, "w1_raw1", RAW1))
         for a in range(PASSES):
             load_w1(w1_raw[1], 1, a)
-        v2_plane = placed([P, S2 // 4], I32, "v2_plane", TAB1 - KIB)
+        tab2_w.append(placed([P, T2], I32, "tab2_w1", LATE_TAB2))
+        load_words(tab2_w[1][:], tab2_words[1])
+        v2_plane = placed([P, S2 // 4], I32, "v2_plane", ACTION_PLANE)
         nc.vector.memset(v2_plane[:], 0)
         for a in range(PASSES):
             for row in range(4):
@@ -162,9 +172,19 @@ def tile_list_replay_action_targets_kernel(
         rounded = {(0, a): placed([P, PACK * PASS], BF16, f"rounded0{a}", ROUNDED + a * 4 * KIB) for a in range(PASSES)}
         w1_w = [held([P, PASSES * PASS], U32, "w1_w0")]
         w1_s = [held([P, PASSES * PASS], U8, f"w1_s{half}") for half in range(2)]
-        elu = {quad: held([P, PACK, PASS], F32, f"elu{quad[0]}{quad[1]}") for quad in QUADS[1:]}
-        elu[QUADS[0]] = placed([P, PACK, PASS], F32, "elu00", FIRST_ELU)
-        h = {first: held([P, 2 * count * PASS], BF16, f"h{first}") for first, count in BATCHES}
+        elu = {
+            (0, 0): placed([P, PACK, PASS], F32, "elu00", FIRST_ELU),
+            (1, 0): held([P, PACK, PASS], F32, "elu10"),
+            (0, PASS): held([P, PACK, PAIR], F32, "elu04"),
+            (1, PASS): held([P, PACK, PAIR], F32, "elu14"),
+        }
+        h = {first: held([P, 2 * PACK * PAIR], BF16, f"h{first}") for first in (2, 4, 6)}
+        h[0] = placed([P, 2 * PACK * PAIR], BF16, "h0", FIRST_H)
+        h_w = {first: held([P, 2 * PAIR], U32, f"h_w{first}") for first in (0, 2, 4, 6)}
+        h_s = {first: held([P, 2 * PAIR], U8, f"h_s{first}") for first in (0, 2, 4, 6)}
+        clamps = {}
+        rises = {}
+        lifted = {}
         scaled = {}
         gates = {}
         sums_b = {}
@@ -181,41 +201,59 @@ def tile_list_replay_action_targets_kernel(
             nc.vector.quantize_mx(out=w1_w[half][:, cols].bitcast(FP8X4), scales=w1_s[half][:, cols], in_=rounded[half, a][:])
 
         def gate(n, number):
-            half, part = QUADS[n // PACK]
-            t = n % PACK
-            first = half * PASS + P * t
-            states = slice(part * PASS, (part + 1) * PASS)
-            b = bank([P, PASS], "b", number)
-            mx_sum(
-                [
-                    (
-                        b[:],
-                        w4_w[:, 2 * (a * H + first) : 2 * (a * H + first + P)].bitcast(FP4X4),
-                        w4_s[a][:, first : first + P],
-                        v_w[a][:, states].bitcast(FP8X4),
-                        v_s[a][:, states],
-                    )
-                    for a in range(PASSES)
-                ]
-            )
+            half, state0, count, t0, tiles = GATES[n]
+            states = slice(state0, state0 + count)
+            b = bank([P, tiles, count], "b", number)
+            for i in range(tiles):
+                first = half * PASS + P * (t0 + i)
+                mx_sum(
+                    [
+                        (
+                            b[:, i, :],
+                            w4_w[:, 2 * (a * H + first) : 2 * (a * H + first + P)].bitcast(FP4X4),
+                            w4_s[a][:, first : first + P],
+                            v_w[a][:, states].bitcast(FP8X4),
+                            v_s[a][:, states],
+                        )
+                        for a in range(PASSES)
+                    ]
+                )
             sums_b[n] = b
 
+        def gate_sums(n):
+            if n < SUMMED:
+                return sums_b[n][:].rearrange("p t s -> p (t s)")
+            return sums_b[n][:].rearrange("p t s -> p s t")
+
+        def shaped(n, tile):
+            if n < SUMMED:
+                return tile[:]
+            return tile[:].rearrange("p (s t) -> p s t", t=PACK)
+
+        def clamp(n):
+            clamps[n] = work.tile([P, PASS], F32, name="clamped")
+            nc.scalar.activation(shaped(n, clamps[n]), gate_sums(n), ACT.Relu, scale=-1.0)
+
         def grow(n):
-            b = sums_b[n]
-            clamped = work.tile([P, PASS], F32, name="clamped")
-            grown = work.tile([P, PASS], F32, name="grown", bufs=8)
-            nc.scalar.activation(clamped[:], b[:], ACT.Relu, scale=-1.0)
-            nc.scalar.activation(grown[:], clamped[:], ACT.Exp, scale=-1.0)
-            gates[n] = (b, grown)
+            gates[n] = work.tile([P, PASS], F32, name="grown", bufs=8)
+            nc.scalar.activation(gates[n][:], clamps[n][:], ACT.Exp, scale=-1.0)
+
+        def rise(n):
+            rises[n] = work.tile([P, PASS], F32, name="risen")
+            nc.scalar.activation(shaped(n, rises[n]), gate_sums(n), ACT.Relu)
 
         def merge(n):
-            b, grown = gates[n]
-            nc.vector.scalar_tensor_tensor(elu[QUADS[n // PACK]][:, n % PACK, :], grown[:], -1.0, b[:], ALU.add, ALU.max)
+            half, state0, count, t0, tiles = GATES[n]
+            dst = elu[half, state0][:, t0 : t0 + tiles, :].rearrange("p t s -> p (t s)")
+            nc.vector.scalar_tensor_tensor(dst, gates[n][:], -1.0, gate_sums(n), ALU.add, ALU.max)
+
+        def lift(n, offset):
+            lifted[n] = placed([P, PASS], F32, f"lifted{n}", offset)
+            nc.gpsimd.tensor_tensor(lifted[n][:], rises[n][:], gates[n][:], ALU.add)
 
         def linear(n, number):
-            half, part = QUADS[n // PACK]
-            in_part = n % PACK
-            states = slice(part * PASS + in_part * P, part * PASS + (in_part + 1) * P)
+            half, chunk = PRODUCTS[n]
+            states = slice(chunk * P, (chunk + 1) * P)
             acc = bank([P, PACK, P], "acc", number)
             for t in range(PACK):
                 mx_sum(
@@ -233,114 +271,103 @@ def tile_list_replay_action_targets_kernel(
             sums[n] = acc
 
         def product(n):
-            half, part = QUADS[n // PACK]
-            in_part = n % PACK
+            half, chunk = PRODUCTS[n]
             acc = sums[n]
-            first, count = BATCH_OF[part * PACK + in_part]
-            place = half * count + part * PACK + in_part - first
-            nc.vector.tensor_tensor(
-                h[first][:, place * PASS : (place + 1) * PASS].rearrange("p (c e t) -> p c t e", e=4, t=PACK),
-                acc[:].rearrange("p t (c e) -> p c t e", e=4),
-                elu[half, part][:, :, in_part * P : (in_part + 1) * P].rearrange("p t (c e) -> p c t e", e=4),
-                ALU.mult,
-            )
-
-        def quantise_half(chunk, half):
-            cols = slice(half * P, (half + 1) * P)
-            nc.vector.quantize_mx(out=h_w[chunk][:, cols].bitcast(FP8X4), scales=h_s[chunk][:, cols], in_=h[chunk][:, half * PASS : (half + 1) * PASS])
-
-        def values_pass(chunk, half, number):
-            if half == 0:
-                values[chunk, 0] = bank([P, PACK, P], "q", number)
-            for i in range(PACK):
-                actions = slice(i * P, (i + 1) * P)
-                nc.tensor.matmul_mx(
-                    out=values[chunk, 0][:, i, :],
-                    lhsT=v2_w[half][:, actions].bitcast(FP8X4),
-                    lhsT_scale=v2_s[4 * half : P, actions],
-                    rhs=h_w[chunk][:, half * P : (half + 1) * P].bitcast(FP8X4),
-                    rhs_scale=h_s[chunk][:, half * P : (half + 1) * P],
-                    start=(half == 0 and i == 0),
-                    stop=(half == 1 and i == PACK - 1),
+            place = 2 * half + chunk % 2
+            dst = h[chunk - chunk % 2][:, place * PASS : (place + 1) * PASS]
+            if n < SUMMED:
+                state0 = chunk // 4 * PASS
+                states = slice(chunk * P - state0, (chunk + 1) * P - state0)
+                nc.vector.tensor_tensor(
+                    dst.rearrange("p (c e t) -> p c t e", e=4, t=PACK),
+                    acc[:].rearrange("p t (c e) -> p c t e", e=4),
+                    elu[half, state0][:, :, states].rearrange("p t (c e) -> p c t e", e=4),
+                    ALU.mult,
+                )
+            else:
+                nc.vector.scalar_tensor_tensor(
+                    dst.rearrange("p (s t) -> p s t", t=PACK),
+                    shaped(n, lifted[n]),
+                    -1.0,
+                    acc[:].rearrange("p t s -> p s t"),
+                    ALU.add,
+                    ALU.mult,
                 )
 
-        def quantise_h(chunk):
-            nc.vector.quantize_mx(out=h_w[chunk][:].bitcast(FP8X4), scales=h_s[chunk][:], in_=h[chunk][:])
+        def quantise_h(first):
+            nc.vector.quantize_mx(out=h_w[first][:].bitcast(FP8X4), scales=h_s[first][:], in_=h[first][:])
 
-        def targets_by_state(chunk, number):
-            first, count = BATCH_OF[chunk]
+        def values_by_state(chunk, number):
+            first = chunk - chunk % 2
             q = bank([P, S2], "q", number)
-            mx_sum(
-                [
+            passes = []
+            for half in (1, 0):
+                place = 2 * half + chunk % 2
+                states = slice(place * P, (place + 1) * P)
+                passes.append(
                     (
                         q[:],
-                        h_w[first][:, (half * count + chunk - first) * P : (half * count + chunk - first + 1) * P].bitcast(FP8X4),
-                        h_s[first][:, (half * count + chunk - first) * P : (half * count + chunk - first + 1) * P],
+                        h_w[first][:, states].bitcast(FP8X4),
+                        h_s[first][:, states],
                         v2_w[half][:].bitcast(FP8X4),
                         v2_s[4 * half : P, :],
                     )
-                    for half in (1, 0)
-                ]
-            )
+                )
+            mx_sum(passes)
+            values[chunk] = q
+
+        def targets_by_state(chunk):
             scaled[chunk] = work.tile([P, S2], F32, name="scaled")
             factor = per_state[:, 0, chunk : chunk + 1]
             offset = per_state[:, 1, chunk : chunk + 1]
-            nc.scalar.activation(scaled[chunk][:], q[:], ACT.Identity, bias=offset, scale=factor)
+            nc.scalar.activation(scaled[chunk][:], values[chunk][:], ACT.Identity, bias=offset, scale=factor)
 
-        def turn_pair(first, numbers, engines=(nc.scalar.copy, nc.scalar.copy)):
+        def turn_pair(first, numbers):
             for pair in range(2):
                 turned = bank([P, 2, 2, P], "turned", numbers[pair])
                 for i in range(2):
                     actions = slice((2 * pair + i) * P, (2 * pair + i + 1) * P)
                     for e in (1, 0):
                         nc.tensor.transpose(turned[:, i, e, :], scaled[first + e][:, actions], identity[:])
-                result = work.tile([P, 2, 2 * P], F32, name="result", bufs=6)
-                engines[pair](result[:], turned[:].rearrange("p i e j -> p i (e j)"))
+                values[first, "turned", pair] = turned
+
+        def store_turned(first):
+            for pair in range(2):
+                result = work.tile([P, 2, PAIR], F32, name="result")
+                nc.scalar.copy(result[:], values[first, "turned", pair][:].rearrange("p i e j -> p i (e j)"))
                 block = out[2 * pair * P : 2 * (pair + 1) * P, first * P : (first + 2) * P]
                 nc.sync.dma_start(out=block.rearrange("(i p) j -> p i j", p=P), in_=result[:])
 
-        def turn_one(chunk, number, engine=nc.scalar.copy):
-            turned = bank([P, PACK, P], "turned", number)
-            for i in range(PACK):
-                nc.tensor.transpose(turned[:, i, :], scaled[chunk][:, i * P : (i + 1) * P], identity[:])
-            result = work.tile([P, PACK, P], F32, name="result", bufs=6)
-            engine(result[:], turned[:])
-            block = out[:, chunk * P : (chunk + 1) * P]
-            nc.sync.dma_start(out=block.rearrange("(i p) j -> p i j", p=P), in_=result[:])
-
-        def values_by_action(chunk, count, tile0, number):
-            first, size = BATCH_OF[chunk]
-            q = bank([P, PACK // count, count * P], "q", number)
-            for i in range(PACK // count):
+        def values_by_action(first, tile0, number):
+            q = bank([P, 2, PAIR], "q", number)
+            for i in range(2):
                 actions = slice((tile0 + i) * P, (tile0 + i + 1) * P)
-                passes = []
-                for half in range(2):
-                    place = half * size + chunk - first
-                    states = slice(place * P, (place + count) * P)
-                    passes.append(
+                mx_sum(
+                    [
                         (
                             q[:, i, :],
                             v2_w[half][:, actions].bitcast(FP8X4),
                             v2_s[4 * half : P, actions],
-                            h_w[first][:, states].bitcast(FP8X4),
-                            h_s[first][:, states],
+                            h_w[first][:, half * PAIR : (half + 1) * PAIR].bitcast(FP8X4),
+                            h_s[first][:, half * PAIR : (half + 1) * PAIR],
                         )
-                    )
-                mx_sum(passes)
-            values[chunk, tile0] = q
+                        for half in range(2)
+                    ]
+                )
+            values[first, tile0] = q
 
-        def along_states(n, chunk, count):
-            row = spread[:, n, (chunk - TURNED) * P : (chunk - TURNED + count) * P]
-            return row.unsqueeze(1).to_broadcast([P, PACK // count, count * P])
+        def along_states(n, first):
+            row = spread[:, n, (first - TURNED) * P : (first - TURNED + 2) * P]
+            return row.unsqueeze(1).to_broadcast([P, 2, PAIR])
 
-        def discount_values(chunk, count, tile0):
-            scaled[chunk, tile0] = work.tile([P, PACK // count, count * P], F32, name="discounted")
-            nc.vector.tensor_tensor(scaled[chunk, tile0][:], values[chunk, tile0][:], along_states(0, chunk, count), ALU.mult)
+        def discount_values(first, tile0):
+            scaled[first, tile0] = work.tile([P, 2, PAIR], F32, name="discounted")
+            nc.vector.tensor_tensor(scaled[first, tile0][:], values[first, tile0][:], along_states(0, first), ALU.mult)
 
-        def reward_and_store(chunk, count, tile0):
-            result = work.tile([P, PACK // count, count * P], F32, name="summed")
-            nc.vector.tensor_tensor(result[:], scaled[chunk, tile0][:], along_states(1, chunk, count), ALU.add)
-            block = out[tile0 * P : (tile0 + PACK // count) * P, chunk * P : (chunk + count) * P]
+        def reward_and_store(first, tile0):
+            result = work.tile([P, 2, PAIR], F32, name="summed")
+            nc.vector.tensor_tensor(result[:], scaled[first, tile0][:], along_states(1, first), ALU.add)
+            block = out[tile0 * P : (tile0 + 2) * P, first * P : (first + 2) * P]
             nc.sync.dma_start(out=block.rearrange("(i p) j -> p i j", p=P), in_=result[:])
 
         gather_states(1, 0)
@@ -350,137 +377,128 @@ def tile_list_replay_action_targets_kernel(
             nc.sync.dma_start(out=spread[:, n, :], in_=row[TURNED * P :].partition_broadcast(P))
         v2_s = v2_plane[:].bitcast(U8)
 
-        def round_on_scalar(a, u):
-            src = w1_raw[1][:, a].rearrange("p i (m u e) -> p u m i e", u=2, e=2)
-            dst = rounded[1, a][:].rearrange("p (u e m i) -> p u m i e", u=2, e=2, i=PACK)
-            nc.scalar.copy(dst[:, u], src[:, u])
-
         def round_late(a):
             src = w1_raw[1][:, a].rearrange("p i (m t) -> p m t i", t=PACK)
             dst = rounded[1, a][:].rearrange("p (t m i) -> p m t i", t=PACK, i=PACK)
             nc.gpsimd.tensor_scalar(dst, src, 1.0, 0.0, ALU.mult, ALU.add)
 
         def gather_actions(half):
-            nc.vector.tensor_copy(v2_w[half][:], tab2_w[:, half, :].bitcast(U32).indirect(idx2[:]))
+            nc.vector.tensor_copy(v2_w[half][:], tab2_w[half][:].bitcast(U32).indirect(idx2[:]))
 
         v2_w = [held([P, S2], U32, f"v2_w{half}") for half in range(2)]
+        def gate_and_clamp(n, number):
+            gate(n, number)
+            clamp(n)
+            grow(n - 1)
+            if n >= SUMMED:
+                rise(n)
+
         gate(0, 0)
+        clamp(0)
         grow(0)
         gate(1, 1)
-        grow(1)
-        gate(2, 2)
-        grow(2)
-        gate(3, 3)
-        grow(3)
-        gate(4, 4)
-        grow(4)
-        gate(5, 5)
-        grow(5)
-        gate(6, 6)
-        grow(6)
-        gate(7, 7)
-        grow(7)
+        clamp(1)
+        gate_and_clamp(2, 2)
+        gate_and_clamp(3, 3)
+        gate_and_clamp(4, 4)
+        gate_and_clamp(5, 5)
+        gate_and_clamp(6, 6)
+        gate_and_clamp(7, 7)
         gather_actions(0)
-        gather_actions(1)
         merge(0)
-        gate(8, 0)
-        grow(8)
-        merge(1)
-        gate(9, 1)
-        grow(9)
+        gate_and_clamp(8, 0)
         round_early(0)
-        merge(2)
-        gate(10, 2)
-        merge(3)
-        gate(11, 3)
+        merge(1)
+        gate_and_clamp(9, 1)
         quantise_w1(0, 0)
         round_early(1)
-        merge(4)
-        gate(12, 4)
-        merge(5)
+        merge(2)
         quantise_w1(0, 1)
         rounded[1, 0] = placed([P, PACK * PASS], BF16, "rounded10", ROUNDED + 4 * KIB)
-        rounded[1, 1] = held([P, PACK * PASS], BF16, "rounded11")
-        h_w = {first: held([P, 2 * count * P], U32, f"h_w{first}") for first, count in BATCHES}
-        h_s = {first: held([P, 2 * count * P], U8, f"h_s{first}") for first, count in BATCHES}
+        rounded[1, 1] = placed([P, PACK * PASS], BF16, "rounded11", ROUNDED)
         round_late(0)
-        round_on_scalar(1, 0)
-        round_on_scalar(1, 1)
-        grow(10)
-        grow(11)
-        grow(12)
-        linear(0, 5)
-        merge(6)
-        linear(1, 6)
-        merge(7)
-        linear(2, 7)
+        round_late(1)
+        linear(0, 2)
+        merge(3)
+        linear(1, 3)
+        merge(4)
+        linear(2, 4)
+        merge(5)
+        gate_and_clamp(10, 5)
         product(0)
-        linear(3, 5)
-        merge(8)
-        gate(13, 0)
-        grow(13)
+        linear(3, 2)
+        merge(6)
+        gate_and_clamp(11, 6)
         product(1)
-        linear(4, 6)
-        merge(9)
-        gate(14, 1)
+        linear(8, 3)
+        merge(7)
+        gate_and_clamp(12, 7)
         product(2)
-        linear(5, 7)
+        linear(9, 4)
+        merge(8)
+        gate_and_clamp(13, 0)
         product(3)
-        linear(6, 5)
+        gate_and_clamp(14, 2)
+        merge(9)
+        gate_and_clamp(15, 1)
+        grow(15)
         w1_w.append(placed([P, PASSES * PASS], U32, "w1_w1", FIRST_ELU))
         quantise_w1(1, 0)
-        quantise_w1(1, 1)
-        product(4)
-        linear(8, 6)
-        product(5)
-        linear(9, 7)
-        merge(10)
-        gate(15, 2)
-        merge(11)
-        linear(10, 3)
-        grow(14)
-        grow(15)
-        product(6)
-        linear(7, 5)
         product(8)
-        linear(11, 6)
-        merge(12)
-        linear(12, 4)
+        linear(12, 3)
+        merge(10)
+        quantise_w1(1, 1)
+        linear(4, 5)
         product(9)
-        quantise_h(0)
-        targets_by_state(0, 7)
-        product(10)
-        quantise_h(1)
-        targets_by_state(1, 3)
-        product(11)
-        quantise_h(2)
-        targets_by_state(2, 6)
+        linear(5, 7)
+        linear(6, 4)
+        gather_actions(1)
+        lift(12, LATE_TAB2)
+        lift(13, LATE_TAB2 + 2 * KIB)
+        product(4)
+        linear(7, 0)
+        linear(10, 5)
+        merge(11)
+        linear(11, 6)
+        product(5)
+        linear(13, 7)
+        product(6)
         product(7)
-        quantise_h(3)
-        targets_by_state(3, 5)
-        merge(13)
-        linear(13, 0)
-        merge(14)
-        linear(14, 1)
-        merge(15)
-        linear(15, 2)
-        turn_pair(0, (7, 3))
-        turn_pair(2, (6, 5))
+        quantise_h(0)
+        values_by_state(0, 4)
+        values_by_state(1, 2)
+        targets_by_state(0)
+        targets_by_state(1)
+        lift(14, FIRST_H)
+        lift(15, FIRST_H + 2 * KIB)
+        product(10)
+        linear(14, 0)
+        product(11)
+        linear(15, 1)
         product(12)
         product(13)
-        product(14)
+        turn_pair(0, (4, 2))
+        store_turned(0)
+        quantise_h(2)
+        values_by_state(2, 5)
+        values_by_state(3, 6)
+        targets_by_state(2)
+        targets_by_state(3)
         quantise_h(4)
-        values_by_action(4, 2, 0, 4)
-        values_by_action(4, 2, 2, 0)
+        values_by_action(4, 0, 3)
+        values_by_action(4, 2, 7)
+        product(14)
+        turn_pair(2, (5, 6))
+        store_turned(2)
         product(15)
-        discount_values(4, 2, 0)
+        discount_values(4, 0)
         quantise_h(6)
-        values_by_action(6, 2, 0, 1)
-        values_by_action(6, 2, 2, 2)
-        discount_values(4, 2, 2)
-        reward_and_store(4, 2, 0)
-        discount_values(6, 2, 0)
-        reward_and_store(4, 2, 2)
-        discount_values(6, 2, 2)
-        reward_and_store(6, 2, 0)
-        reward_and_store(6, 2, 2)
+        values_by_action(6, 0, 0)
+        values_by_action(6, 2, 1)
+        reward_and_store(4, 0)
+        discount_values(4, 2)
+        discount_values(6, 0)
+        reward_and_store(4, 2)
+        discount_values(6, 2)
+        reward_and_store(6, 0)
+        reward_and_store(6, 2)

@@ -280,8 +280,8 @@ def tile_list_replay_action_targets_kernel(
                 states = slice(chunk * P - state0, (chunk + 1) * P - state0)
                 nc.vector.tensor_tensor(
                     dst.rearrange("p (c e t) -> p c t e", e=4, t=PACK),
-                    acc[:].rearrange("p t (c e) -> p c t e", e=4),
                     elu[half, state0][:, :, states].rearrange("p t (c e) -> p c t e", e=4),
+                    acc[:].rearrange("p t (c e) -> p c t e", e=4),
                     ALU.mult,
                 )
             else:

@@ -221,18 +221,16 @@ def tile_list_replay_action_targets_kernel(
             sums_b[n] = b
 
         def gate_sums(n):
-            if n < SUMMED:
-                return sums_b[n][:].rearrange("p t s -> p (t s)")
-            return sums_b[n][:].rearrange("p t s -> p s t")
+            return sums_b[n][:].rearrange("p t s -> p (t s)")
 
-        def shaped(n, tile):
-            if n < SUMMED:
-                return tile[:]
-            return tile[:].rearrange("p (s t) -> p s t", t=PACK)
+        def in_pairs(n, tile):
+            dst = tile[:].rearrange("p (c e t) -> p c t e", e=2, t=PACK)
+            return dst, sums_b[n][:].rearrange("p t (c e) -> p c t e", e=2)
 
         def clamp(n):
             clamps[n] = work.tile([P, PASS], F32, name="clamped")
-            nc.scalar.activation(shaped(n, clamps[n]), gate_sums(n), ACT.Relu, scale=-1.0)
+            dst, src = (clamps[n][:], gate_sums(n)) if n < SUMMED else in_pairs(n, clamps[n])
+            nc.scalar.activation(dst, src, ACT.Relu, scale=-1.0)
 
         def grow(n):
             gates[n] = work.tile([P, PASS], F32, name="grown", bufs=8)
@@ -240,7 +238,7 @@ def tile_list_replay_action_targets_kernel(
 
         def rise(n):
             rises[n] = work.tile([P, PASS], F32, name="risen")
-            nc.scalar.activation(shaped(n, rises[n]), gate_sums(n), ACT.Relu)
+            nc.scalar.activation(*in_pairs(n, rises[n]), ACT.Relu)
 
         def merge(n):
             half, state0, count, t0, tiles = GATES[n]
@@ -287,7 +285,7 @@ def tile_list_replay_action_targets_kernel(
             else:
                 nc.vector.scalar_tensor_tensor(
                     dst.rearrange("p (s t) -> p s t", t=PACK),
-                    shaped(n, lifted[n]),
+                    lifted[n][:].rearrange("p (s t) -> p s t", t=PACK),
                     -1.0,
                     acc[:].rearrange("p t s -> p s t"),
                     ALU.add,

@@ -31,15 +31,16 @@ TURNED = 4
 PAIR = 2 * P
 GATES = (
     [(half, 0, PASS, t, 1) for half in range(2) for t in range(PACK)]
-    + [(half, PASS, PAIR, t, 2) for half in range(2) for t in (0, 2)]
-    + [(half, chunk * P, P, 0, PACK) for half in range(2) for chunk in (6, 7)]
+    + [(0, 2 * PAIR, PAIR, t, 2) for t in (0, 2)]
+    + [(1, chunk * P, P, 0, PACK) for chunk in (4, 5)]
+    + [(half, 3 * PAIR, PAIR, t, 2) for half in range(2) for t in (0, 2)]
 )
 PRODUCTS = (
     [(half, chunk) for half in range(2) for chunk in range(4)]
     + [(half, chunk) for half in range(2) for chunk in (4, 5)]
     + [(half, chunk) for half in range(2) for chunk in (6, 7)]
 )
-SUMMED = 12
+SUMMED = (10, 11)
 
 
 def tile_list_replay_action_targets_kernel(
@@ -95,7 +96,7 @@ def tile_list_replay_action_targets_kernel(
             )
 
         RAW1, TAB0, LATE_TAB2, ACTION_PLANE, TAB1, PLANE1, SMALL, W4 = 0, 8 * KIB, 16 * KIB, 20 * KIB, 24 * KIB, 40 * KIB, 42 * KIB, 43 * KIB
-        TAB2, RAW0, ROUNDED, FIRST_ELU, FIRST_H = 47 * KIB, 51 * KIB, 67 * KIB, 75 * KIB, 83 * KIB
+        TAB2, RAW0, ROUNDED, FIRST_ELU = 47 * KIB, 51 * KIB, 67 * KIB, 75 * KIB
 
         idx = keep.tile([P, S // LIST_ROWS], U16, name="idx")
         idx2 = keep.tile([P, S2 // LIST_ROWS], U16, name="idx2")
@@ -175,11 +176,11 @@ def tile_list_replay_action_targets_kernel(
         elu = {
             (0, 0): placed([P, PACK, PASS], F32, "elu00", FIRST_ELU),
             (1, 0): held([P, PACK, PASS], F32, "elu10"),
-            (0, PASS): held([P, PACK, PAIR], F32, "elu04"),
-            (1, PASS): held([P, PACK, PAIR], F32, "elu14"),
+            (0, 2 * PAIR): held([P, PACK, PAIR], F32, "elu04"),
+            (0, 3 * PAIR): held([P, PACK, PAIR], F32, "elu06"),
+            (1, 3 * PAIR): held([P, PACK, PAIR], F32, "elu16"),
         }
-        h = {first: held([P, 2 * PACK * PAIR], BF16, f"h{first}") for first in (2, 4, 6)}
-        h[0] = placed([P, 2 * PACK * PAIR], BF16, "h0", FIRST_H)
+        h = {first: held([P, 2 * PACK * PAIR], BF16, f"h{first}") for first in (0, 2, 4, 6)}
         h_w = {first: held([P, 2 * PAIR], U32, f"h_w{first}") for first in (0, 2, 4, 6)}
         h_s = {first: held([P, 2 * PAIR], U8, f"h_s{first}") for first in (0, 2, 4, 6)}
         clamps = {}
@@ -229,7 +230,7 @@ def tile_list_replay_action_targets_kernel(
 
         def clamp(n):
             clamps[n] = work.tile([P, PASS], F32, name="clamped")
-            dst, src = (clamps[n][:], gate_sums(n)) if n < SUMMED else in_pairs(n, clamps[n])
+            dst, src = (clamps[n][:], gate_sums(n)) if n not in SUMMED else in_pairs(n, clamps[n])
             nc.scalar.activation(dst, src, ACT.Relu, scale=-1.0)
 
         def grow(n):
@@ -273,8 +274,8 @@ def tile_list_replay_action_targets_kernel(
             acc = sums[n]
             place = 2 * half + chunk % 2
             dst = h[chunk - chunk % 2][:, place * PASS : (place + 1) * PASS]
-            if n < SUMMED:
-                state0 = chunk // 4 * PASS
+            if n not in SUMMED:
+                state0 = 0 if chunk < TURNED else chunk // 2 * PAIR
                 states = slice(chunk * P - state0, (chunk + 1) * P - state0)
                 nc.vector.tensor_tensor(
                     dst.rearrange("p (c e t) -> p c t e", e=4, t=PACK),
@@ -383,12 +384,12 @@ def tile_list_replay_action_targets_kernel(
         def gather_actions(half):
             nc.vector.tensor_copy(v2_w[half][:], tab2_w[half][:].bitcast(U32).indirect(idx2[:]))
 
-        v2_w = [held([P, S2], U32, f"v2_w{half}") for half in range(2)]
+        v2_w = [held([P, S2], U32, "v2_w0")]
         def gate_and_clamp(n, number):
             gate(n, number)
             clamp(n)
             grow(n - 1)
-            if n >= SUMMED:
+            if n in SUMMED:
                 rise(n)
 
         gate(0, 0)
@@ -441,58 +442,59 @@ def tile_list_replay_action_targets_kernel(
         gate_and_clamp(15, 1)
         grow(15)
         w1_w.append(placed([P, PASSES * PASS], U32, "w1_w1", FIRST_ELU))
+        v2_w.append(placed([P, S2], U32, "v2_w1", RAW1))
+        gather_actions(1)
         quantise_w1(1, 0)
-        product(8)
-        linear(12, 3)
-        merge(10)
         quantise_w1(1, 1)
         linear(4, 5)
+        linear(5, 6)
+        lift(10, ROUNDED)
+        lift(11, ROUNDED + 2 * KIB)
+        product(8)
+        linear(6, 3)
         product(9)
-        linear(5, 7)
-        linear(6, 4)
-        gather_actions(1)
-        lift(12, LATE_TAB2)
-        lift(13, LATE_TAB2 + 2 * KIB)
+        linear(7, 4)
         product(4)
-        linear(7, 0)
         linear(10, 5)
-        merge(11)
-        linear(11, 6)
         product(5)
-        linear(13, 7)
-        product(6)
-        product(7)
+        merge(12)
         quantise_h(0)
-        values_by_state(0, 4)
-        values_by_state(1, 2)
+        values_by_state(0, 6)
+        values_by_state(1, 7)
         targets_by_state(0)
         targets_by_state(1)
-        lift(14, FIRST_H)
-        lift(15, FIRST_H + 2 * KIB)
-        product(10)
-        linear(14, 0)
-        product(11)
-        linear(15, 1)
-        product(12)
-        product(13)
-        turn_pair(0, (4, 2))
-        store_turned(0)
+        product(6)
+        linear(11, 3)
+        product(7)
+        merge(13)
+        linear(12, 0)
         quantise_h(2)
-        values_by_state(2, 5)
-        values_by_state(3, 6)
+        turn_pair(0, (6, 7))
+        product(10)
+        values_by_state(2, 4)
+        values_by_state(3, 5)
+        store_turned(0)
         targets_by_state(2)
         targets_by_state(3)
+        product(11)
+        linear(13, 3)
+        merge(14)
+        linear(14, 2)
         quantise_h(4)
-        values_by_action(4, 0, 3)
+        merge(15)
+        linear(15, 1)
+        values_by_action(4, 0, 6)
+        turn_pair(2, (4, 5))
         values_by_action(4, 2, 7)
-        product(14)
-        turn_pair(2, (5, 6))
+        product(12)
         store_turned(2)
+        product(13)
+        product(14)
         product(15)
         discount_values(4, 0)
         quantise_h(6)
         values_by_action(6, 0, 0)
-        values_by_action(6, 2, 1)
+        values_by_action(6, 2, 3)
         reward_and_store(4, 0)
         discount_values(4, 2)
         discount_values(6, 0)

@@ -363,11 +363,13 @@ def tile_list_replay_action_targets_kernel(
             scaled[first, tile0] = work.tile([P, 2, PAIR], F32, name="discounted")
             nc.vector.tensor_tensor(scaled[first, tile0][:], values[first, tile0][:], along_states(0, first), ALU.mult)
 
-        def reward_and_store(first, tile0):
-            result = work.tile([P, 2, PAIR], F32, name="summed")
-            nc.vector.tensor_tensor(result[:], scaled[first, tile0][:], along_states(1, first), ALU.add)
-            block = out[tile0 * P : (tile0 + 2) * P, first * P : (first + 2) * P]
-            nc.sync.dma_start(out=block.rearrange("(i p) j -> p i j", p=P), in_=result[:])
+        def reward_and_store(first, tile0, tiles):
+            count = tiles.stop - tiles.start
+            result = work.tile([P, 2, PAIR], F32, name="summed", bufs=6)
+            reward_rows = along_states(1, first)[:, tiles, :]
+            nc.vector.tensor_tensor(result[:, tiles, :], scaled[first, tile0][:, tiles, :], reward_rows, ALU.add)
+            block = out[(tile0 + tiles.start) * P : (tile0 + tiles.stop) * P, first * P : (first + 2) * P]
+            nc.sync.dma_start(out=block.rearrange("(i p) j -> p i j", i=count), in_=result[:, tiles, :])
 
         gather_states(1, 0)
         gather_states(1, 1)
@@ -495,10 +497,11 @@ def tile_list_replay_action_targets_kernel(
         quantise_h(6)
         values_by_action(6, 0, 0)
         values_by_action(6, 2, 3)
-        reward_and_store(4, 0)
+        reward_and_store(4, 0, slice(0, 2))
         discount_values(4, 2)
         discount_values(6, 0)
-        reward_and_store(4, 2)
+        reward_and_store(4, 2, slice(0, 2))
         discount_values(6, 2)
-        reward_and_store(6, 0)
-        reward_and_store(6, 2)
+        for tile0 in (0, 2):
+            for i in range(2):
+                reward_and_store(6, tile0, slice(i, i + 1))

@@ -33,14 +33,15 @@ GATES = (
     [(half, 0, PASS, t, 1) for half in range(2) for t in range(PACK)]
     + [(0, 2 * PAIR, PAIR, t, 2) for t in (0, 2)]
     + [(1, chunk * P, P, 0, PACK) for chunk in (4, 5)]
-    + [(half, 3 * PAIR, PAIR, t, 2) for half in range(2) for t in (0, 2)]
+    + [(0, 3 * PAIR, PAIR, t, 2) for t in (0, 2)]
+    + [(1, chunk * P, P, 0, PACK) for chunk in (6, 7)]
 )
 PRODUCTS = (
     [(half, chunk) for half in range(2) for chunk in range(4)]
     + [(half, chunk) for half in range(2) for chunk in (4, 5)]
     + [(half, chunk) for half in range(2) for chunk in (6, 7)]
 )
-SUMMED = (10, 11)
+SUMMED = (10, 11, 14, 15)
 
 
 def tile_list_replay_action_targets_kernel(
@@ -96,7 +97,7 @@ def tile_list_replay_action_targets_kernel(
             )
 
         RAW1, TAB0, LATE_TAB2, ACTION_PLANE, TAB1, PLANE1, SMALL, W4 = 0, 8 * KIB, 16 * KIB, 20 * KIB, 24 * KIB, 40 * KIB, 42 * KIB, 43 * KIB
-        TAB2, RAW0, ROUNDED, FIRST_ELU = 47 * KIB, 51 * KIB, 67 * KIB, 75 * KIB
+        TAB2, RAW0, ROUNDED, FIRST_ELU, SECOND_H = 47 * KIB, 51 * KIB, 67 * KIB, 75 * KIB, 83 * KIB
 
         idx = keep.tile([P, S // LIST_ROWS], U16, name="idx")
         idx2 = keep.tile([P, S2 // LIST_ROWS], U16, name="idx2")
@@ -178,9 +179,9 @@ def tile_list_replay_action_targets_kernel(
             (1, 0): held([P, PACK, PASS], F32, "elu10"),
             (0, 2 * PAIR): held([P, PACK, PAIR], F32, "elu04"),
             (0, 3 * PAIR): held([P, PACK, PAIR], F32, "elu06"),
-            (1, 3 * PAIR): held([P, PACK, PAIR], F32, "elu16"),
         }
-        h = {first: held([P, 2 * PACK * PAIR], BF16, f"h{first}") for first in (0, 2, 4, 6)}
+        h = {first: held([P, 2 * PACK * PAIR], BF16, f"h{first}") for first in (0, 4, 6)}
+        h[2] = placed([P, 2 * PACK * PAIR], BF16, "h2", SECOND_H)
         h_w = {first: held([P, 2 * PAIR], U32, f"h_w{first}") for first in (0, 2, 4, 6)}
         h_s = {first: held([P, 2 * PAIR], U8, f"h_s{first}") for first in (0, 2, 4, 6)}
         clamps = {}
@@ -444,59 +445,59 @@ def tile_list_replay_action_targets_kernel(
         gate_and_clamp(15, 1)
         grow(15)
         w1_w.append(placed([P, PASSES * PASS], U32, "w1_w1", FIRST_ELU))
+        linear(12, 5)
         v2_w.append(placed([P, S2], U32, "v2_w1", RAW1))
         gather_actions(1)
         quantise_w1(1, 0)
         quantise_w1(1, 1)
-        linear(4, 5)
-        linear(5, 6)
         lift(10, ROUNDED)
         lift(11, ROUNDED + 2 * KIB)
+        linear(4, 6)
         product(8)
-        linear(6, 3)
+        linear(5, 3)
         product(9)
-        linear(7, 4)
+        linear(6, 4)
         product(4)
-        linear(10, 5)
-        product(5)
+        linear(7, 6)
         merge(12)
+        linear(10, 7)
+        product(5)
+        linear(11, 3)
+        product(6)
         quantise_h(0)
-        values_by_state(0, 6)
-        values_by_state(1, 7)
+        values_by_state(0, 4)
+        values_by_state(1, 2)
         targets_by_state(0)
         targets_by_state(1)
-        product(6)
-        linear(11, 3)
         product(7)
+        linear(13, 6)
         merge(13)
-        linear(12, 0)
+        linear(14, 1)
         quantise_h(2)
-        turn_pair(0, (6, 7))
+        lift(14, SECOND_H)
+        lift(15, SECOND_H + 2 * KIB)
+        values_by_state(2, 0)
+        turn_pair(0, (4, 2))
         product(10)
-        values_by_state(2, 4)
-        values_by_state(3, 5)
-        store_turned(0)
-        targets_by_state(2)
-        targets_by_state(3)
+        values_by_state(3, 7)
         product(11)
-        linear(13, 3)
-        merge(14)
-        linear(14, 2)
-        quantise_h(4)
-        merge(15)
-        linear(15, 1)
-        values_by_action(4, 0, 6)
-        turn_pair(2, (4, 5))
-        values_by_action(4, 2, 7)
+        linear(15, 3)
+        targets_by_state(2)
+        store_turned(0)
+        targets_by_state(3)
         product(12)
-        store_turned(2)
         product(13)
+        quantise_h(4)
+        values_by_action(4, 0, 5)
+        turn_pair(2, (0, 7))
+        values_by_action(4, 2, 6)
+        store_turned(2)
         product(14)
         product(15)
         discount_values(4, 0)
         quantise_h(6)
-        values_by_action(6, 0, 0)
-        values_by_action(6, 2, 3)
+        values_by_action(6, 0, 4)
+        values_by_action(6, 2, 2)
         reward_and_store(4, 0, slice(0, 2))
         discount_values(4, 2)
         discount_values(6, 0)

@@ -30,7 +30,8 @@ KIB = 1024
 TURNED = 4
 PAIR = 2 * P
 GATES = (
-    [(half, 0, PASS, t, 1) for half in range(2) for t in range(PACK)]
+    [(0, pair * PAIR, PAIR, t, 2) for pair in range(2) for t in (0, 2)]
+    + [(1, 0, PASS, t, 1) for t in range(PACK)]
     + [(0, 2 * PAIR, PAIR, t, 2) for t in (0, 2)]
     + [(1, chunk * P, P, 0, PACK) for chunk in (4, 5)]
     + [(0, 3 * PAIR, PAIR, t, 2) for t in (0, 2)]
@@ -136,11 +137,9 @@ def tile_list_replay_action_targets_kernel(
         w4_s = [plane[:].bitcast(U8)[:, S:] for plane in planes]
         v_w = [held([P, S], U32, f"v_w{a}") for a in range(PASSES)]
 
-        def gather_states(a, part):
-            entries = idx[:, part * PASS // LIST_ROWS : (part + 1) * PASS // LIST_ROWS]
-            nc.vector.tensor_copy(
-                v_w[a][:, part * PASS : (part + 1) * PASS], tab_w[a][:].bitcast(U32).indirect(entries)
-            )
+        def gather_states(a, first, count):
+            entries = idx[:, first // LIST_ROWS : (first + count) // LIST_ROWS]
+            nc.vector.tensor_copy(v_w[a][:, first : first + count], tab_w[a][:].bitcast(U32).indirect(entries))
 
         w4_w = placed([P, PASSES * 2 * H], U8, "w4_w", W4)
         regroup(w4_w[:].bitcast(U16), w4_raw[:].rearrange("p a c -> p (a c)").bitcast(U16))
@@ -149,8 +148,8 @@ def tile_list_replay_action_targets_kernel(
         w1_raw = [placed([P, PASSES, PACK, PASS], F32, "w1_raw0", RAW0)]
         for a in range(PASSES):
             load_w1(w1_raw[0], 0, a)
-        gather_states(0, 0)
-        gather_states(0, 1)
+        gather_states(0, 0, PASS)
+        gather_states(0, PASS, PASS)
         v2_rows = held([P, S2], U8, "v2_rows")
         nc.vector.tensor_copy(v2_rows[:], tab2_s[:].bitcast(U8).indirect(idx2[:]))
         w1_raw.append(placed([P, PASSES, PACK, PASS], F32, "w1_raw1", RAW1))
@@ -244,8 +243,10 @@ def tile_list_replay_action_targets_kernel(
 
         def merge(n):
             half, state0, count, t0, tiles = GATES[n]
-            dst = elu[half, state0][:, t0 : t0 + tiles, :].rearrange("p t s -> p (t s)")
-            nc.vector.scalar_tensor_tensor(dst, gates[n][:], -1.0, gate_sums(n), ALU.add, ALU.max)
+            base = 0 if state0 < PASS else state0
+            dst = elu[half, base][:, t0 : t0 + tiles, state0 - base : state0 - base + count]
+            grown = gates[n][:].rearrange("p (t s) -> p t s", t=tiles)
+            nc.vector.scalar_tensor_tensor(dst, grown, -1.0, sums_b[n][:], ALU.add, ALU.max)
 
         def lift(n, offset):
             lifted[n] = placed([P, PASS], F32, f"lifted{n}", offset)
@@ -372,8 +373,9 @@ def tile_list_replay_action_targets_kernel(
             block = out[(tile0 + tiles.start) * P : (tile0 + tiles.stop) * P, first * P : (first + 2) * P]
             nc.sync.dma_start(out=block.rearrange("(i p) j -> p i j", i=count), in_=result[:, tiles, :])
 
-        gather_states(1, 0)
-        gather_states(1, 1)
+        gather_states(1, 0, PAIR)
+        gather_states(1, PAIR, PAIR)
+        gather_states(1, PASS, PASS)
         spread = placed([P, 2, S - TURNED * P], F32, "spread", TAB1)
         for n, row in enumerate((discount, reward)):
             nc.sync.dma_start(out=spread[:, n, :], in_=row[TURNED * P :].partition_broadcast(P))
@@ -397,9 +399,7 @@ def tile_list_replay_action_targets_kernel(
 
         gate(0, 0)
         clamp(0)
-        grow(0)
-        gate(1, 1)
-        clamp(1)
+        gate_and_clamp(1, 1)
         gate_and_clamp(2, 2)
         gate_and_clamp(3, 3)
         gate_and_clamp(4, 4)

@@ -28,6 +28,7 @@ CHUNKS = S // P
 KIB = 1024
 
 TURNED = 4
+BY_STATE = 6
 PAIR = 2 * P
 GATES = (
     [(0, pair * PAIR, PAIR, t, 2) for pair in range(2) for t in (0, 2)]
@@ -119,7 +120,7 @@ def tile_list_replay_action_targets_kernel(
         rows = held([P, P], F32, "rows")
         nc.vector.memset(rows[:], 0.0)
         for n, values_in in enumerate((discount, reward)):
-            nc.sync.dma_start(out=rows[CHUNKS * n : CHUNKS * n + TURNED, :], in_=values_in[0 : TURNED * P].rearrange("(c p) -> c p", p=P))
+            nc.sync.dma_start(out=rows[CHUNKS * n : CHUNKS * n + BY_STATE, :], in_=values_in[0 : BY_STATE * P].rearrange("(c p) -> c p", p=P))
 
         v_rows = placed([P, 4 * S], U8, "v_rows", PLANE1 - S // 2)
         nc.vector.tensor_copy(v_rows[:, 0:S], tab_s[:].bitcast(U8).indirect(idx[:]))
@@ -339,6 +340,44 @@ def tile_list_replay_action_targets_kernel(
                 block = out[2 * pair * P : 2 * (pair + 1) * P, first * P : (first + 2) * P]
                 nc.sync.dma_start(out=block.rearrange("(i p) j -> p i j", p=P), in_=result[:])
 
+        def upper_values_by_state(first, number):
+            q = bank([P, 2, PAIR], "q", number)
+            for e in range(2):
+                passes = []
+                for half in (1, 0):
+                    states = slice((2 * half + e) * P, (2 * half + e + 1) * P)
+                    passes.append(
+                        (
+                            q[:, e, :],
+                            h_w[first][:, states].bitcast(FP8X4),
+                            h_s[first][:, states],
+                            v2_w[half][:, PAIR:].bitcast(FP8X4),
+                            v2_s[4 * half : P, PAIR:],
+                        )
+                    )
+                mx_sum(passes)
+            values[first, "upper"] = q
+
+        def upper_targets(first):
+            for e in range(2):
+                scaled[first + e] = work.tile([P, PAIR], F32, name="upper")
+                factor = per_state[:, 0, first + e : first + e + 1]
+                offset = per_state[:, 1, first + e : first + e + 1]
+                nc.scalar.activation(scaled[first + e][:], values[first, "upper"][:, e, :], ACT.Identity, bias=offset, scale=factor)
+
+        def turn_upper(first, number):
+            turned = bank([P, 2, 2, P], "turned", number)
+            for e in (1, 0):
+                for i in range(2):
+                    nc.tensor.transpose(turned[:, i, e, :], scaled[first + e][:, i * P : (i + 1) * P], identity[:])
+            values[first, "turned", 1] = turned
+
+        def store_upper(first):
+            for i in range(2):
+                result = work.tile([P, PAIR], F32, name="upper_result")
+                nc.scalar.copy(result[:], values[first, "turned", 1][:, i].rearrange("p e j -> p (e j)"))
+                nc.sync.dma_start(out=out[(2 + i) * P : (3 + i) * P, first * P : (first + 2) * P], in_=result[:])
+
         def values_by_action(first, tile0, number):
             q = bank([P, 2, PAIR], "q", number)
             for i in range(2):
@@ -488,20 +527,21 @@ def tile_list_replay_action_targets_kernel(
         product(12)
         product(13)
         quantise_h(4)
+        upper_values_by_state(4, 6)
         values_by_action(4, 0, 5)
+        upper_targets(4)
         turn_pair(2, (0, 7))
-        values_by_action(4, 2, 6)
-        store_turned(2)
+        turn_upper(4, 1)
         product(14)
+        store_turned(2)
+        store_upper(4)
         product(15)
         discount_values(4, 0)
         quantise_h(6)
         values_by_action(6, 0, 4)
         values_by_action(6, 2, 2)
         reward_and_store(4, 0, slice(0, 2))
-        discount_values(4, 2)
         discount_values(6, 0)
-        reward_and_store(4, 2, slice(0, 2))
         discount_values(6, 2)
         for tile0 in (0, 2):
             for i in range(2):

from contextlib import ExitStack

import concourse.mybir as mybir
from concourse.masks import make_identity

K, H, T, S, T2, S2 = 1024, 1024, 4096, 1024, 1024, 512
FLOPS = 2 * K * H * S * 2 + 2 * H * S2 * S

F32 = mybir.dt.float32
BF16 = mybir.dt.bfloat16
I32 = mybir.dt.int32
U32 = mybir.dt.uint32
U16 = mybir.dt.uint16
U8 = mybir.dt.uint8
FP8X4 = mybir.dt.float8_e4m3fn_x4
FP4X4 = mybir.dt.float4_e2m1fn_x4
ALU = mybir.AluOpType
ACT = mybir.ActivationFunctionType

P = 128
PACK = 4
PASS = P * PACK
PASSES = K // PASS
LIST_ROWS = 16
QUADRANT = 32
SCALE_ROWS = 32
CHUNKS = S // P
KIB = 1024

TURNED = 4
BY_STATE = 6
PAIR = 2 * P
GATES = (
    [(0, pair * PAIR, PAIR, t, 2) for pair in range(2) for t in (0, 2)]
    + [(1, 0, PASS, t, 1) for t in range(PACK)]
    + [(0, 2 * PAIR, PAIR, t, 2) for t in (0, 2)]
    + [(1, chunk * P, P, 0, PACK) for chunk in (4, 5)]
    + [(0, 3 * PAIR, PAIR, t, 2) for t in (0, 2)]
    + [(1, chunk * P, P, 0, PACK) for chunk in (6, 7)]
)
PRODUCTS = (
    [(half, chunk) for half in range(2) for chunk in range(4)]
    + [(half, chunk) for half in range(2) for chunk in (4, 5)]
    + [(half, chunk) for half in range(2) for chunk in (6, 7)]
)
SUMMED = (10, 11, 14, 15)


def tile_list_replay_action_targets_kernel(
    tc, tab_words, tab_scales, offs, tab2_words, tab2_scales, offs2, w1, w4_words, w4_scales, discount, reward, out
):
    nc = tc.nc
    with ExitStack() as ctx:
        keep = ctx.enter_context(tc.tile_pool(name="keep", bufs=1))
        arena = ctx.enter_context(tc.tile_pool(name="arena", bufs=1))
        work = ctx.enter_context(tc.tile_pool(name="work", bufs=4))
        psum = ctx.enter_context(tc.psum_pool(name="psum", bufs=1))

        def held(shape, dtype, name):
            return keep.tile(shape, dtype, name=name, align_bytes=64)

        def placed(shape, dtype, name, offset):
            return arena.tile(shape, dtype, name=name, offset=offset, align_bytes=64)

        def bank(shape, name, number):
            return psum.tile(shape, F32, name=name, tag=f"bank{number}")

        def mx_sum(passes):
            for n, (acc, lhs, lhs_scale, rhs, rhs_scale) in enumerate(passes):
                nc.tensor.matmul_mx(
                    out=acc,
                    lhsT=lhs,
                    lhsT_scale=lhs_scale,
                    rhs=rhs,
                    rhs_scale=rhs_scale,
                    start=(n == 0),
                    stop=(n == len(passes) - 1),
                )

        def load_w1(dst, half, a):
            rows = w1[a * PASS : (a + 1) * PASS, half * PASS : (half + 1) * PASS]
            nc.sync.dma_start(out=dst[:, a], in_=rows.rearrange("(p i) c -> p i c", i=PACK))

        def load_words(dst, words):
            nc.sync.dma_start(out=dst, in_=words.rearrange("p t i -> p (t i)").bitcast(I32))

        def move_rows(dst, to, src, start):
            nc.sync.dma_start(out=dst[to:P:QUADRANT, :], in_=src[start : start + 13 : 4, :])

        def load_rows(dst, scales, engine):
            nc.sync.dma_start(out=dst[0:SCALE_ROWS, :], in_=scales.bitcast(I32).rearrange("a q c -> (a q) c"))
            engine.memset(dst[SCALE_ROWS : 2 * QUADRANT, :], 0)
            engine.memset(dst[2 * QUADRANT : P, :], 0)

        def regroup(dst, src):
            nc.vector.tensor_copy(
                dst.rearrange("p (r t m) -> p r t m", t=PACK, m=P),
                src.rearrange("p (r m t) -> p r t m", t=PACK, m=P),
            )

        RAW1, TAB0, LATE_TAB2, ACTION_PLANE, TAB1, PLANE1, SMALL, W4 = 0, 8 * KIB, 16 * KIB, 20 * KIB, 24 * KIB, 40 * KIB, 42 * KIB, 43 * KIB
        TAB2, RAW0, ROUNDED, FIRST_ELU, SECOND_H = 47 * KIB, 51 * KIB, 67 * KIB, 75 * KIB, 83 * KIB

        idx = keep.tile([P, S // LIST_ROWS], U16, name="idx")
        idx2 = keep.tile([P, S2 // LIST_ROWS], U16, name="idx2")
        tab_s = held([P, T // 4], I32, "tab_s")
        w4_raw_s = held([P, H // 4], I32, "w4_raw_s")
        w4_raw = placed([P, PASSES, H // 2], I32, "w4_raw", RAW0 - KIB)
        tab_w = [placed([P, T], I32, "tab_w0", TAB0)]
        tab2_s = held([P, T2 // 4], I32, "tab2_s")
        planes = [held([P, (S + H) // 4], I32, "planes0")]

        nc.sync.dma_start(idx[:], offs)
        load_rows(tab_s, tab_scales, nc.vector)
        load_rows(w4_raw_s, w4_scales, nc.vector)
        nc.sync.dma_start(idx2[:], offs2)
        load_rows(tab2_s, tab2_scales, nc.gpsimd)
        nc.sync.dma_start(out=w4_raw[:], in_=w4_words.bitcast(I32).rearrange("a p c -> p a c"))
        load_words(tab_w[0][:], tab_words[0])
        rows = held([P, P], F32, "rows")
        nc.vector.memset(rows[:], 0.0)
        for n, values_in in enumerate((discount, reward)):
            nc.sync.dma_start(out=rows[CHUNKS * n : CHUNKS * n + BY_STATE, :], in_=values_in[0 : BY_STATE * P].rearrange("(c p) -> c p", p=P))

        v_rows = placed([P, 4 * S], U8, "v_rows", PLANE1 - S // 2)
        nc.vector.tensor_copy(v_rows[:, 0:S], tab_s[:].bitcast(U8).indirect(idx[:]))
        regroup(planes[0][:].bitcast(U8)[:, S:], w4_raw_s[:].bitcast(U8))
        nc.vector.tensor_copy(planes[0][:, 0 : S // 4], v_rows[:, 0:S].bitcast(I32))
        planes.append(placed([P, (S + H) // 4], I32, "planes1", PLANE1))
        nc.vector.memset(planes[1][:], 0)
        tab_w.append(placed([P, T], I32, "tab_w1", TAB1))
        for quadrant in range(1, 4):
            nc.sync.dma_start(out=planes[0][QUADRANT * quadrant : QUADRANT * quadrant + 4, :], in_=planes[0][4 * quadrant : 4 * quadrant + 4, :])
        load_words(tab_w[1][:], tab_words[1])
        for row in range(4):
            move_rows(planes[1], row, planes[0], 16 + row)
        v_s = [plane[:].bitcast(U8)[:, 0:S] for plane in planes]
        w4_s = [plane[:].bitcast(U8)[:, S:] for plane in planes]
        v_w = [held([P, S], U32, f"v_w{a}") for a in range(PASSES)]

        def gather_states(a, first, count):
            entries = idx[:, first // LIST_ROWS : (first + count) // LIST_ROWS]
            nc.vector.tensor_copy(v_w[a][:, first : first + count], tab_w[a][:].bitcast(U32).indirect(entries))

        w4_w = placed([P, PASSES * 2 * H], U8, "w4_w", W4)
        regroup(w4_w[:].bitcast(U16), w4_raw[:].rearrange("p a c -> p (a c)").bitcast(U16))
        tab2_w = [placed([P, T2], I32, "tab2_w0", TAB2)]
        load_words(tab2_w[0][:], tab2_words[0])
        w1_raw = [placed([P, PASSES, PACK, PASS], F32, "w1_raw0", RAW0)]
        for a in range(PASSES):
            load_w1(w1_raw[0], 0, a)
        gather_states(0, 0, PASS)
        gather_states(0, PASS, PASS)
        v2_rows = held([P, S2], U8, "v2_rows")
        nc.vector.tensor_copy(v2_rows[:], tab2_s[:].bitcast(U8).indirect(idx2[:]))
        w1_raw.append(placed([P, PASSES, PACK, PASS], F32, "w1_raw1", RAW1))
        for a in range(PASSES):
            load_w1(w1_raw[1], 1, a)
        tab2_w.append(placed([P, T2], I32, "tab2_w1", LATE_TAB2))
        load_words(tab2_w[1][:], tab2_words[1])
        v2_plane = placed([P, S2 // 4], I32, "v2_plane", ACTION_PLANE)
        nc.vector.memset(v2_plane[:], 0)
        for a in range(PASSES):
            for row in range(4):
                move_rows(v2_plane, 4 * a + row, v2_rows[:].bitcast(I32), 16 * a + row)

        identity = placed([P, P], F32, "identity", SMALL + KIB // 2)
        make_identity(nc, identity[:])
        per_state = held([P, 2, CHUNKS], F32, "per_state")
        columns = bank([P, P], "columns", 7)
        nc.tensor.transpose(columns[:], rows[:], identity[:])
        nc.vector.tensor_copy(per_state[:].rearrange("p n c -> p (n c)"), columns[:, 0 : 2 * CHUNKS])

        rounded = {(0, a): placed([P, PACK * PASS], BF16, f"rounded0{a}", ROUNDED + a * 4 * KIB) for a in range(PASSES)}
        w1_w = [held([P, PASSES * PASS], U32, "w1_w0")]
        w1_s = [held([P, PASSES * PASS], U8, f"w1_s{half}") for half in range(2)]
        elu = {
            (0, 0): placed([P, PACK, PASS], F32, "elu00", FIRST_ELU),
            (1, 0): held([P, PACK, PASS], F32, "elu10"),
            (0, 2 * PAIR): held([P, PACK, PAIR], F32, "elu04"),
            (0, 3 * PAIR): held([P, PACK, PAIR], F32, "elu06"),
        }
        h = {first: held([P, 2 * PACK * PAIR], BF16, f"h{first}") for first in (0, 4, 6)}
        h[2] = placed([P, 2 * PACK * PAIR], BF16, "h2", SECOND_H)
        h_w = {first: held([P, 2 * PAIR], U32, f"h_w{first}") for first in (0, 2, 4, 6)}
        h_s = {first: held([P, 2 * PAIR], U8, f"h_s{first}") for first in (0, 2, 4, 6)}
        clamps = {}
        rises = {}
        lifted = {}
        scaled = {}
        gates = {}
        sums_b = {}
        sums = {}
        values = {}

        def round_early(a):
            src = w1_raw[0][:, a].rearrange("p i (m u e) -> p u m i e", u=2, e=2)
            dst = rounded[0, a][:].rearrange("p (u e m i) -> p u m i e", u=2, e=2, i=PACK)
            nc.vector.tensor_copy(dst, src)

        def quantise_w1(half, a):
            cols = slice(a * PASS, (a + 1) * PASS)
            nc.vector.quantize_mx(out=w1_w[half][:, cols].bitcast(FP8X4), scales=w1_s[half][:, cols], in_=rounded[half, a][:])

        def gate(n, number):
            half, state0, count, t0, tiles = GATES[n]
            states = slice(state0, state0 + count)
            b = bank([P, tiles, count], "b", number)
            for i in range(tiles):
                first = half * PASS + P * (t0 + i)
                mx_sum(
                    [
                        (
                            b[:, i, :],
                            w4_w[:, 2 * (a * H + first) : 2 * (a * H + first + P)].bitcast(FP4X4),
                            w4_s[a][:, first : first + P],
                            v_w[a][:, states].bitcast(FP8X4),
                            v_s[a][:, states],
                        )
                        for a in range(PASSES)
                    ]
                )
            sums_b[n] = b

        def gate_sums(n):
            return sums_b[n][:].rearrange("p t s -> p (t s)")

        def in_pairs(n, tile):
            dst = tile[:].rearrange("p (c e t) -> p c t e", e=2, t=PACK)
            return dst, sums_b[n][:].rearrange("p t (c e) -> p c t e", e=2)

        def clamp(n):
            clamps[n] = work.tile([P, PASS], F32, name="clamped")
            dst, src = (clamps[n][:], gate_sums(n)) if n not in SUMMED else in_pairs(n, clamps[n])
            nc.scalar.activation(dst, src, ACT.Relu, scale=-1.0)

        def grow(n):
            gates[n] = work.tile([P, PASS], F32, name="grown", bufs=8)
            nc.scalar.activation(gates[n][:], clamps[n][:], ACT.Exp, scale=-1.0)

        def rise(n):
            rises[n] = work.tile([P, PASS], F32, name="risen")
            nc.scalar.activation(*in_pairs(n, rises[n]), ACT.Relu)

        def merge(n):
            half, state0, count, t0, tiles = GATES[n]
            base = 0 if state0 < PASS else state0
            dst = elu[half, base][:, t0 : t0 + tiles, state0 - base : state0 - base + count]
            grown = gates[n][:].rearrange("p (t s) -> p t s", t=tiles)
            nc.vector.scalar_tensor_tensor(dst, grown, -1.0, sums_b[n][:], ALU.add, ALU.max)

        def lift(n, offset):
            lifted[n] = placed([P, PASS], F32, f"lifted{n}", offset)
            nc.gpsimd.tensor_tensor(lifted[n][:], rises[n][:], gates[n][:], ALU.add)

        def linear(n, number):
            half, chunk = PRODUCTS[n]
            states = slice(chunk * P, (chunk + 1) * P)
            acc = bank([P, PACK, P], "acc", number)
            for t in range(PACK):
                mx_sum(
                    [
                        (
                            acc[:, t, :],
                            w1_w[half][:, a * PASS + P * t : a * PASS + P * (t + 1)].bitcast(FP8X4),
                            w1_s[half][:, a * PASS + P * t : a * PASS + P * (t + 1)],
                            v_w[a][:, states].bitcast(FP8X4),
                            v_s[a][:, states],
                        )
                        for a in (1, 0)
                    ]
                )
            sums[n] = acc

        def product(n):
            half, chunk = PRODUCTS[n]
            acc = sums[n]
            place = 2 * half + chunk % 2
            dst = h[chunk - chunk % 2][:, place * PASS : (place + 1) * PASS]
            if n not in SUMMED:
                state0 = 0 if chunk < TURNED else chunk // 2 * PAIR
                states = slice(chunk * P - state0, (chunk + 1) * P - state0)
                nc.vector.tensor_tensor(
                    dst.rearrange("p (c e t) -> p c t e", e=4, t=PACK),
                    elu[half, state0][:, :, states].rearrange("p t (c e) -> p c t e", e=4),
                    acc[:].rearrange("p t (c e) -> p c t e", e=4),
                    ALU.mult,
                )
            else:
                nc.vector.scalar_tensor_tensor(
                    dst.rearrange("p (s t) -> p s t", t=PACK),
                    lifted[n][:].rearrange("p (s t) -> p s t", t=PACK),
                    -1.0,
                    acc[:].rearrange("p t s -> p s t"),
                    ALU.add,
                    ALU.mult,
                )

        def quantise_h(first):
            nc.vector.quantize_mx(out=h_w[first][:].bitcast(FP8X4), scales=h_s[first][:], in_=h[first][:])

        def values_by_state(chunk, number):
            first = chunk - chunk % 2
            q = bank([P, S2], "q", number)
            passes = []
            for half in (1, 0):
                place = 2 * half + chunk % 2
                states = slice(place * P, (place + 1) * P)
                passes.append(
                    (
                        q[:],
                        h_w[first][:, states].bitcast(FP8X4),
                        h_s[first][:, states],
                        v2_w[half][:].bitcast(FP8X4),
                        v2_s[4 * half : P, :],
                    )
                )
            mx_sum(passes)
            values[chunk] = q

        def targets_by_state(chunk):
            scaled[chunk] = work.tile([P, S2], F32, name="scaled")
            factor = per_state[:, 0, chunk : chunk + 1]
            offset = per_state[:, 1, chunk : chunk + 1]
            nc.scalar.activation(scaled[chunk][:], values[chunk][:], ACT.Identity, bias=offset, scale=factor)

        def turn_pair(first, numbers):
            for pair in range(2):
                turned = bank([P, 2, 2, P], "turned", numbers[pair])
                for i in range(2):
                    actions = slice((2 * pair + i) * P, (2 * pair + i + 1) * P)
                    for e in (1, 0):
                        nc.tensor.transpose(turned[:, i, e, :], scaled[first + e][:, actions], identity[:])
                values[first, "turned", pair] = turned

        def store_turned(first):
            for pair in range(2):
                result = work.tile([P, 2, PAIR], F32, name="result")
                nc.scalar.copy(result[:], values[first, "turned", pair][:].rearrange("p i e j -> p i (e j)"))
                block = out[2 * pair * P : 2 * (pair + 1) * P, first * P : (first + 2) * P]
                nc.sync.dma_start(out=block.rearrange("(i p) j -> p i j", p=P), in_=result[:])

        def upper_values_by_state(first, number):
            q = bank([P, 2, PAIR], "q", number)
            for e in range(2):
                passes = []
                for half in (1, 0):
                    states = slice((2 * half + e) * P, (2 * half + e + 1) * P)
                    passes.append(
                        (
                            q[:, e, :],
                            h_w[first][:, states].bitcast(FP8X4),
                            h_s[first][:, states],
                            v2_w[half][:, PAIR:].bitcast(FP8X4),
                            v2_s[4 * half : P, PAIR:],
                        )
                    )
                mx_sum(passes)
            values[first, "upper"] = q

        def upper_targets(first):
            for e in range(2):
                scaled[first + e] = work.tile([P, PAIR], F32, name="upper")
                factor = per_state[:, 0, first + e : first + e + 1]
                offset = per_state[:, 1, first + e : first + e + 1]
                nc.scalar.activation(scaled[first + e][:], values[first, "upper"][:, e, :], ACT.Identity, bias=offset, scale=factor)

        def turn_upper(first, number):
            turned = bank([P, 2, 2, P], "turned", number)
            for e in (1, 0):
                for i in range(2):
                    nc.tensor.transpose(turned[:, i, e, :], scaled[first + e][:, i * P : (i + 1) * P], identity[:])
            values[first, "turned", 1] = turned

        def store_upper(first):
            for i in range(2):
                result = work.tile([P, PAIR], F32, name="upper_result")
                nc.scalar.copy(result[:], values[first, "turned", 1][:, i].rearrange("p e j -> p (e j)"))
                nc.sync.dma_start(out=out[(2 + i) * P : (3 + i) * P, first * P : (first + 2) * P], in_=result[:])

        def values_by_action(first, tile0, number):
            q = bank([P, 2, PAIR], "q", number)
            for i in range(2):
                actions = slice((tile0 + i) * P, (tile0 + i + 1) * P)
                mx_sum(
                    [
                        (
                            q[:, i, :],
                            v2_w[half][:, actions].bitcast(FP8X4),
                            v2_s[4 * half : P, actions],
                            h_w[first][:, half * PAIR : (half + 1) * PAIR].bitcast(FP8X4),
                            h_s[first][:, half * PAIR : (half + 1) * PAIR],
                        )
                        for half in range(2)
                    ]
                )
            values[first, tile0] = q

        def along_states(n, first):
            row = spread[:, n, (first - TURNED) * P : (first - TURNED + 2) * P]
            return row.unsqueeze(1).to_broadcast([P, 2, PAIR])

        def discount_values(first, tile0):
            scaled[first, tile0] = work.tile([P, 2, PAIR], F32, name="discounted")
            nc.vector.tensor_tensor(scaled[first, tile0][:], values[first, tile0][:], along_states(0, first), ALU.mult)

        def reward_and_store(first, tile0, tiles):
            count = tiles.stop - tiles.start
            result = work.tile([P, 2, PAIR], F32, name="summed", bufs=6)
            reward_rows = along_states(1, first)[:, tiles, :]
            nc.vector.tensor_tensor(result[:, tiles, :], scaled[first, tile0][:, tiles, :], reward_rows, ALU.add)
            block = out[(tile0 + tiles.start) * P : (tile0 + tiles.stop) * P, first * P : (first + 2) * P]
            nc.sync.dma_start(out=block.rearrange("(i p) j -> p i j", i=count), in_=result[:, tiles, :])

        gather_states(1, 0, PAIR)
        gather_states(1, PAIR, PAIR)
        gather_states(1, PASS, PASS)
        spread = placed([P, 2, S - TURNED * P], F32, "spread", TAB1)
        for n, row in enumerate((discount, reward)):
            nc.sync.dma_start(out=spread[:, n, :], in_=row[TURNED * P :].partition_broadcast(P))
        v2_s = v2_plane[:].bitcast(U8)

        def round_late(a):
            src = w1_raw[1][:, a].rearrange("p i (m t) -> p m t i", t=PACK)
            dst = rounded[1, a][:].rearrange("p (t m i) -> p m t i", t=PACK, i=PACK)
            nc.gpsimd.tensor_scalar(dst, src, 1.0, 0.0, ALU.mult, ALU.add)

        def gather_actions(half):
            nc.vector.tensor_copy(v2_w[half][:], tab2_w[half][:].bitcast(U32).indirect(idx2[:]))

        v2_w = [held([P, S2], U32, "v2_w0")]
        def gate_and_clamp(n, number):
            gate(n, number)
            clamp(n)
            grow(n - 1)
            if n in SUMMED:
                rise(n)

        gate(0, 0)
        clamp(0)
        gate_and_clamp(1, 1)
        gate_and_clamp(2, 2)
        gate_and_clamp(3, 3)
        gate_and_clamp(4, 4)
        gate_and_clamp(5, 5)
        gate_and_clamp(6, 6)
        gate_and_clamp(7, 7)
        gather_actions(0)
        merge(0)
        gate_and_clamp(8, 0)
        round_early(0)
        merge(1)
        gate_and_clamp(9, 1)
        quantise_w1(0, 0)
        round_early(1)
        merge(2)
        quantise_w1(0, 1)
        rounded[1, 0] = placed([P, PACK * PASS], BF16, "rounded10", ROUNDED + 4 * KIB)
        rounded[1, 1] = placed([P, PACK * PASS], BF16, "rounded11", ROUNDED)
        round_late(0)
        round_late(1)
        linear(0, 2)
        merge(3)
        linear(1, 3)
        merge(4)
        linear(2, 4)
        merge(5)
        gate_and_clamp(10, 5)
        product(0)
        linear(3, 2)
        merge(6)
        gate_and_clamp(11, 6)
        product(1)
        linear(8, 3)
        merge(7)
        gate_and_clamp(12, 7)
        product(2)
        linear(9, 4)
        merge(8)
        gate_and_clamp(13, 0)
        product(3)
        gate_and_clamp(14, 2)
        merge(9)
        gate_and_clamp(15, 1)
        grow(15)
        w1_w.append(placed([P, PASSES * PASS], U32, "w1_w1", FIRST_ELU))
        linear(12, 5)
        v2_w.append(placed([P, S2], U32, "v2_w1", RAW1))
        gather_actions(1)
        quantise_w1(1, 0)
        quantise_w1(1, 1)
        lift(10, ROUNDED)
        lift(11, ROUNDED + 2 * KIB)
        linear(4, 6)
        product(8)
        linear(5, 3)
        product(9)
        linear(6, 4)
        product(4)
        linear(7, 6)
        merge(12)
        linear(10, 7)
        product(5)
        linear(11, 3)
        product(6)
        quantise_h(0)
        values_by_state(0, 4)
        values_by_state(1, 2)
        targets_by_state(0)
        targets_by_state(1)
        product(7)
        linear(13, 6)
        merge(13)
        linear(14, 1)
        quantise_h(2)
        lift(14, SECOND_H)
        lift(15, SECOND_H + 2 * KIB)
        values_by_state(2, 0)
        turn_pair(0, (4, 2))
        product(10)
        values_by_state(3, 7)
        product(11)
        linear(15, 3)
        targets_by_state(2)
        store_turned(0)
        targets_by_state(3)
        product(12)
        product(13)
        quantise_h(4)
        upper_values_by_state(4, 6)
        values_by_action(4, 0, 5)
        upper_targets(4)
        turn_pair(2, (0, 7))
        turn_upper(4, 1)
        product(14)
        store_turned(2)
        store_upper(4)
        product(15)
        discount_values(4, 0)
        quantise_h(6)
        values_by_action(6, 0, 4)
        values_by_action(6, 2, 2)
        reward_and_store(4, 0, slice(0, 2))
        discount_values(6, 0)
        discount_values(6, 2)
        for tile0 in (0, 2):
            for i in range(2):
                reward_and_store(6, tile0, slice(i, i + 1))
